import numpy as np
import ml_dtypes


def mxq(x, axis, fmt="e4m3"):
    dtype, down = {"e4m3": (ml_dtypes.float8_e4m3fn, 7), "e5m2": (ml_dtypes.float8_e5m2, 14)}[fmt]
    v = np.moveaxis(np.asarray(x, np.float32).astype(ml_dtypes.bfloat16).astype(np.float64), axis, -1)
    blocks = v.reshape(v.shape[:-1] + (-1, 32))
    amax = np.abs(blocks).max(-1, keepdims=True)
    byte = np.maximum(np.where(amax > 0, np.frexp(amax)[1] - 1 + 127, 0) - down, 1)
    scale = np.exp2(byte - 127.0)
    codes = (blocks / scale).astype(np.float32).astype(dtype).astype(np.float64)
    return np.moveaxis((codes * scale).reshape(v.shape), -1, axis)


WIDE = False


def mx_kscale(k):
    if not WIDE:
        return np.ones(k)
    levels = np.array([10, -10, 5, -5, 0])
    if k % 512:
        return np.exp2(np.random.permutation(np.resize(levels, k // 32))).repeat(32)
    a = np.empty((k // 512, 16))
    for p in range(k // 512):
        a[p, :8] = np.random.permutation(np.resize(levels, 8))
        for g in range(8):
            far = levels[np.abs(levels - a[p, g]) >= 10]
            a[p, g + 8] = far[np.random.randint(len(far))]
    return np.exp2(a.ravel()).repeat(32)


def f64(x):
    return np.asarray(x).astype(np.float64)


def striped(idx):
    return np.tile(idx.reshape(-1, 16).T, (8, 1)).astype(np.uint16)


def unstriped(offs):
    return offs[:16].T.reshape(-1).astype(np.int64)


E2M1 = np.array([0.0, 0.5, 1.0, 1.5, 2.0, 3.0, 4.0, 6.0, -0.0, -0.5, -1.0, -1.5, -2.0, -3.0, -4.0, -6.0])


def pack_weight(w, fmt):
    k, n = w.shape
    w = f64(np.asarray(w, np.float32).astype(ml_dtypes.bfloat16)).reshape(k // 32, 32, n)
    amax = np.abs(w).max(1)
    if fmt == "e4m3":
        byte = np.frexp(amax)[1] - 1 + 127 - 7
    else:
        mant, ex = np.frexp(amax / 6.0)
        byte = np.where(mant > 0.5, ex, ex - 1) + 127
    byte = np.clip(np.where(amax > 0, byte, 1), 1, 254)
    scaled = (w * np.exp2(127.0 - byte)[:, None, :]).reshape(k, n).astype(np.float32)
    by_word = np.ascontiguousarray(scaled.reshape(k // 512, 128, 4, n).transpose(0, 1, 3, 2))
    if fmt == "e4m3":
        words = by_word.astype(ml_dtypes.float8_e4m3fn).view(np.uint8)
    else:
        c = by_word.astype(ml_dtypes.float4_e2m1fn).view(np.uint8) & 0xF
        words = (c[..., 0::2] | (c[..., 1::2] << 4)).reshape(k // 512, 128, 2 * n)
    return np.ascontiguousarray(words), np.ascontiguousarray(byte.astype(np.uint8).reshape(k // 512, 16, n))


def unpack_weight(words, scales, fmt):
    g, _, n = scales.shape
    words = np.ascontiguousarray(words).reshape(g, 128, n, -1)
    if fmt == "e4m3":
        vals = words.view(ml_dtypes.float8_e4m3fn).astype(np.float64)
    else:
        nib = np.empty((g, 128, n, 4), np.uint8)
        nib[..., 0::2] = words & 0xF
        nib[..., 1::2] = words >> 4
        vals = E2M1[nib]
    vals = vals * np.repeat(np.exp2(scales.astype(np.float64) - 127.0), 8, axis=1)[..., None]
    return vals.transpose(0, 1, 3, 2).reshape(g * 512, n)


def gelu(v):
    return 0.5 * v * (1.0 + np.tanh(np.sqrt(2.0 / np.pi) * (v + 0.044715 * v**3)))


def often(T, S):
    return np.random.permutation(T)[(T * np.random.uniform(0, 1, S) ** 4).astype(np.int64)]


K, K2, T, S, H = 1024, 512, 2048, 1024, 1024


def setup_inputs():
    n = np.random.standard_normal
    s = mx_kscale(K)[:, None]
    s2 = mx_kscale(K2)[:, None]
    u = mx_kscale(H)[:, None]
    tab_words, tab_scales = pack_weight(n((K, T)) * s, "e4m3")
    tab2_words, tab2_scales = pack_weight(n((K2, T)) * s2, "e2m1")
    w4_words, w4_scales = pack_weight(n((K, H)) / np.sqrt(K) / s * u.T, "e2m1")
    w8_words, w8_scales = pack_weight(n((H, H)) / np.sqrt(H) / u, "e4m3")
    return {
        "tab_words": tab_words, "tab_scales": tab_scales,
        "offs": striped(often(T, S)),
        "tab2_words": tab2_words, "tab2_scales": tab2_scales,
        "offs2": striped(often(T, S)),
        "w4_words": w4_words, "w4_scales": w4_scales,
        "w2": (n((K2, H)) / np.sqrt(K2) / s2).astype(np.float32),
        "rate": (-0.25 * np.exp(0.3 * n(H))).astype(np.float32),
        "w8_words": w8_words, "w8_scales": w8_scales,
        "step": (0.5 * np.exp(0.3 * n(H)) / u[:, 0]).astype(np.float32),
    }


def reference(tab_words, tab_scales, offs, tab2_words, tab2_scales, offs2,
              w4_words, w4_scales, w2, rate, w8_words, w8_scales, step):
    v = unpack_weight(tab_words, tab_scales, "e4m3")[:, unstriped(offs)]
    v2 = unpack_weight(tab2_words, tab2_scales, "e2m1")[:, unstriped(offs2)]
    w4 = unpack_weight(w4_words, w4_scales, "e2m1")
    w8 = unpack_weight(w8_words, w8_scales, "e4m3")
    a = w4.T @ v
    b = mxq(f64(w2), 0, "e4m3").T @ v2
    h = a * np.exp(f64(rate)[:, None] * (b * b))
    y = w8.T @ mxq(h, 0, "e4m3")
    return y + f64(step)[:, None] * a

@@ -1,0 +1,280 @@
+from contextlib import ExitStack
+
+import concourse.mybir as mybir
+
+K, K2, T, S, H = 1024, 512, 2048, 1024, 1024
+FLOPS = 2 * S * H * (K + K2 + H)
+
+F32 = mybir.dt.float32
+BF16 = mybir.dt.bfloat16
+I32 = mybir.dt.int32
+U32 = mybir.dt.uint32
+U16 = mybir.dt.uint16
+U8 = mybir.dt.uint8
+FP8X4 = mybir.dt.float8_e4m3fn_x4
+FP4X4 = mybir.dt.float4_e2m1fn_x4
+ALU = mybir.AluOpType
+ACT = mybir.ActivationFunctionType
+
+P = 128
+PACK = 4
+GROUPS = 2
+GATHER = 512
+BLOCK = 128
+CHUNK = 256
+
+
+def tile_list_mixed_layer_step_kernel(
+    tc, tab_words, tab_scales, offs, tab2_words, tab2_scales, offs2,
+    w4_words, w4_scales, w2, rate, w8_words, w8_scales, step, out,
+):
+    nc = tc.nc
+    with ExitStack() as ctx:
+        keep = ctx.enter_context(tc.tile_pool(name="keep", bufs=1))
+        ring = ctx.enter_context(tc.tile_pool(name="ring", bufs=3))
+        psum = ctx.enter_context(tc.psum_pool(name="psum", bufs=1))
+
+        def kept(shape, dtype, name):
+            return keep.tile(shape, dtype, name=name, align_bytes=64)
+
+        list1 = kept([P, S // 16], U16, "list1")
+        list2 = kept([P, S // 16], U16, "list2")
+        tab2_w = kept([P, T], U16, "tab2_w")
+        tab2_s = kept([P, T], U8, "tab2_s")
+        tab_w = [kept([P, T], U32, "tab_w%d" % a) for a in range(2)]
+        tab_s = kept([P, T], U8, "tab_s")
+        w2_raw = [[kept([P, PACK, 256], F32, "w2_raw%d%d" % (g, q)) for q in range(2)] for g in range(GROUPS)]
+        w4_raw = [kept([P, H], U16, "w4_raw%d" % a) for a in range(2)]
+        w4s_raw = kept([P, 2 * H], U8, "w4s_raw")
+        w8_raw = [kept([P, H], U32, "w8_raw%d" % a) for a in range(2)]
+        w8s_raw = kept([P, H], U8, "w8s_raw")
+        rate_sb = kept([P, GROUPS, PACK], F32, "rate_sb")
+        step_sb = kept([P, GROUPS, PACK], F32, "step_sb")
+        v_s1 = [kept([P, GATHER], U8, "v_s1_%d" % c) for c in range(2)]
+
+        for plane in (tab2_s, tab_s, w4s_raw, w8s_raw, v_s1[0], v_s1[1]):
+            nc.vector.memset(plane[:].bitcast(I32), 0)
+
+        def load_words(tile, src):
+            nc.sync.dma_start(out=tile[:].bitcast(I32), in_=src.bitcast(I32))
+
+        def load_w2(g, q):
+            c0 = 512 * g + 256 * q
+            nc.sync.dma_start(out=w2_raw[g][q][:], in_=w2.rearrange("(p j) c -> p j c", j=PACK)[:, :, c0 : c0 + 256])
+
+        nc.sync.dma_start(list2[:], offs2)
+        load_words(tab2_w, tab2_words[0])
+        for q in range(4):
+            nc.sync.dma_start(
+                out=tab2_s[32 * q : 32 * q + 4, :].bitcast(I32), in_=tab2_scales[0, 4 * q : 4 * q + 4, :].bitcast(I32)
+            )
+        nc.sync.dma_start(out=rate_sb[:], in_=rate.rearrange("(g p t) -> p g t", g=GROUPS, t=PACK))
+        load_w2(0, 0)
+        load_w2(0, 1)
+        nc.sync.dma_start(list1[:], offs)
+        for q in range(4):
+            nc.sync.dma_start(
+                out=tab_s[32 * q : 32 * q + 8, :].bitcast(I32), in_=tab_scales[:, 4 * q : 4 * q + 4, :].bitcast(I32)
+            )
+        for a in range(2):
+            load_words(tab_w[a], tab_words[a].rearrange("p t i -> p (t i)"))
+        for a in range(2):
+            load_words(w4_raw[a], w4_words[a])
+        for q in range(4):
+            nc.sync.dma_start(
+                out=w4s_raw[32 * q : 32 * q + 4, :].bitcast(I32).rearrange("r (a n) -> r a n", a=2),
+                in_=w4_scales[:, 4 * q : 4 * q + 4, :].bitcast(I32).rearrange("a r n -> r a n"),
+            )
+        load_w2(1, 0)
+        load_w2(1, 1)
+        for a in range(2):
+            load_words(w8_raw[a], w8_words[a].rearrange("p c i -> p (c i)"))
+        for q in range(4):
+            nc.sync.dma_start(
+                out=w8s_raw[32 * q : 32 * q + 8, :].bitcast(I32), in_=w8_scales[:, 4 * q : 4 * q + 4, :].bitcast(I32)
+            )
+        nc.sync.dma_start(out=step_sb[:], in_=step.rearrange("(g p t) -> p g t", g=GROUPS, t=PACK))
+
+        minus_rate = kept([P, GROUPS * PACK], F32, "minus_rate")
+        half = kept([P, GROUPS * PACK], F32, "half")
+        root = kept([P, GROUPS * PACK], F32, "root")
+        nc.gpsimd.memset(half[:], 0.5)
+        nc.gpsimd.tensor_scalar(
+            minus_rate[:], rate_sb[:].rearrange("p g t -> p (g t)"), -1.0, 0.0, ALU.mult, ALU.add
+        )
+        nc.gpsimd.tensor_tensor(root[:], minus_rate[:], half[:], ALU.pow)
+
+        v2_w = [kept([P, GATHER], U16, "v2_w%d" % c) for c in range(2)]
+        v2_s = [kept([P, GATHER], U8, "v2_s%d" % c) for c in range(2)]
+        v_w = [[kept([P, GATHER], U32, "v_w%d%d" % (a, c)) for c in range(2)] for a in range(2)]
+        v_s0 = [kept([P, GATHER], U8, "v_s0_%d" % c) for c in range(2)]
+        w2_bf = [kept([P, PACK, P, PACK], BF16, "w2_bf%d" % g) for g in range(GROUPS)]
+        w2_q = [kept([P, 512], U32, "w2_q%d" % g) for g in range(GROUPS)]
+        w2_s = [kept([P, 512], U8, "w2_s%d" % g) for g in range(GROUPS)]
+        w4_p = [kept([P, H], U16, "w4_p%d" % a) for a in range(2)]
+        w4_s = kept([P, 2 * H], U8, "w4_s")
+        w8_p = [kept([P, H], U32, "w8_p%d" % a) for a in range(2)]
+        w8_s = kept([P, H], U8, "w8_s")
+        decay = [[kept([P, 2, GATHER, 2], F32, "decay%d%d" % (g, c)) for c in range(2)] for g in range(GROUPS)]
+        n_chunks = S // CHUNK
+        a_sb = [[kept([P, PACK, CHUNK], F32, "a_sb%d%d" % (g, d)) for d in range(n_chunks)] for g in range(GROUPS)]
+        h_bf = [[kept([P, CHUNK, PACK], BF16, "h_bf%d%d" % (g, d)) for d in range(n_chunks)] for g in range(GROUPS)]
+        h_q = [[kept([P, CHUNK], U32, "h_q%d%d" % (g, d)) for d in range(n_chunks)] for g in range(GROUPS)]
+        h_s = [[kept([P, CHUNK], U8, "h_s%d%d" % (g, d)) for d in range(n_chunks)] for g in range(GROUPS)]
+
+        def gather(dst, window, lst, c):
+            cols = GATHER // 16
+            nc.vector.tensor_copy(dst[:], window[:].indirect(lst[:, c * cols : (c + 1) * cols]))
+
+        def gather_tab_scales(c):
+            gather(v_s0[c], tab_s, list1, c)
+            nc.sync.dma_start(out=v_s1[c][0:124, :].bitcast(I32), in_=v_s0[c][4:128, :].bitcast(I32))
+
+        def cast_w2(g, q):
+            nc.scalar.activation(
+                w2_bf[g][:, :, 64 * q : 64 * (q + 1), :].rearrange("p t m j -> p m j t"),
+                w2_raw[g][q][:].rearrange("p j (m t) -> p m j t", t=PACK),
+                ACT.Copy,
+            )
+
+        def quantize_w2(g):
+            nc.vector.quantize_mx(
+                out=w2_q[g][:].bitcast(FP8X4), scales=w2_s[g][:], in_=w2_bf[g][:].rearrange("p t m j -> p (t m j)")
+            )
+
+        def deal_columns(dst, src):
+            nc.vector.tensor_copy(
+                out=dst.rearrange("p (g t m) -> p g m t", t=PACK, m=P),
+                in_=src.rearrange("p (g m t) -> p g m t", t=PACK, m=P),
+            )
+
+        def make_decay(g, c):
+            for u in range(2):
+                square = ring.tile([P, 2, GATHER], F32, name="square")
+                for e in range(2):
+                    t = 2 * u + e
+                    b = psum.tile([P, GATHER], F32, name="b", bufs=2)
+                    nc.tensor.matmul_mx(
+                        out=b[:],
+                        lhsT=w2_q[g][:, P * t : P * (t + 1)].bitcast(FP8X4),
+                        lhsT_scale=w2_s[g][:, P * t : P * (t + 1)],
+                        rhs=v2_w[c][:].bitcast(FP4X4),
+                        rhs_scale=v2_s[c][:],
+                        start=True,
+                        stop=True,
+                    )
+                    nc.scalar.activation(
+                        square[:, e, :], b[:], ACT.Square, scale=root[:, PACK * g + t : PACK * g + t + 1]
+                    )
+                nc.scalar.activation(
+                    decay[g][c][:, u, :, :], square[:].rearrange("p e n -> p n e"), ACT.Exp, scale=-1.0
+                )
+
+        def make_h(g, j):
+            c, n0 = divmod(j * BLOCK, GATHER)
+            d, m0 = divmod(j * BLOCK, CHUNK)
+            acc = psum.tile([P, PACK, BLOCK], F32, name="acc", bufs=3)
+            for t in range(PACK):
+                col = 512 * g + P * t
+                for a in range(2):
+                    nc.tensor.matmul_mx(
+                        out=acc[:, t, :],
+                        lhsT=w4_p[a][:, col : col + P].bitcast(FP4X4),
+                        lhsT_scale=w4_s[:, H * a + col : H * a + col + P],
+                        rhs=v_w[a][c][:, n0 : n0 + BLOCK].bitcast(FP8X4),
+                        rhs_scale=(v_s0, v_s1)[a][c][:, n0 : n0 + BLOCK],
+                        start=(a == 0),
+                        stop=(a == 1),
+                    )
+            nc.vector.tensor_tensor(
+                h_bf[g][d][:, m0 : m0 + BLOCK, :].rearrange("p n (u e) -> p n u e", u=2),
+                acc[:].rearrange("p (u e) n -> p n u e", u=2),
+                decay[g][c][:, :, n0 : n0 + BLOCK, :].rearrange("p u n e -> p n u e"),
+                ALU.mult,
+            )
+            nc.scalar.activation(a_sb[g][d][:, :, m0 : m0 + BLOCK], acc[:], ACT.Copy)
+
+        def quantize_h(g, d):
+            nc.vector.quantize_mx(
+                out=h_q[g][d][:].bitcast(FP8X4), scales=h_s[g][d][:], in_=h_bf[g][d][:].rearrange("p n t -> p (n t)")
+            )
+
+        out_rows = out.rearrange("(g p t) j -> g p t j", g=GROUPS, t=PACK)
+
+        def mix(d):
+            for g in range(GROUPS):
+                result = ring.tile([P, PACK, CHUNK], F32, name="result")
+                for u in range(2):
+                    y = psum.tile([P, 2, CHUNK], F32, name="y", bufs=3)
+                    for e in range(2):
+                        col = 512 * g + P * (2 * u + e)
+                        for a in range(2):
+                            nc.tensor.matmul_mx(
+                                out=y[:, e, :],
+                                lhsT=w8_p[a][:, col : col + P].bitcast(FP8X4),
+                                lhsT_scale=w8_s[4 * a : P, col : col + P],
+                                rhs=h_q[a][d][:].bitcast(FP8X4),
+                                rhs_scale=h_s[a][d][:],
+                                start=(a == 0),
+                                stop=(a == 1),
+                            )
+                    for e in range(2):
+                        t = 2 * u + e
+                        nc.vector.scalar_tensor_tensor(
+                            result[:, t, :], a_sb[g][d][:, t, :], step_sb[:, g, t : t + 1], y[:, e, :],
+                            ALU.mult, ALU.add,
+                        )
+                nc.sync.dma_start(out=out_rows[g][:, :, d * CHUNK : (d + 1) * CHUNK], in_=result[:])
+
+        gather(v2_w[0], tab2_w, list2, 0)
+        gather(v2_s[0], tab2_s, list2, 0)
+        cast_w2(0, 0)
+        cast_w2(0, 1)
+        gather_tab_scales(0)
+        quantize_w2(0)
+        make_decay(0, 0)
+        gather(v_w[0][0], tab_w[0], list1, 0)
+        gather(v2_w[1], tab2_w, list2, 1)
+        gather(v_w[1][0], tab_w[1], list1, 0)
+        for a in range(2):
+            deal_columns(w4_p[a][:], w4_raw[a][:])
+        deal_columns(w4_s[:], w4s_raw[:])
+        cast_w2(1, 0)
+        cast_w2(1, 1)
+        make_h(0, 0)
+        make_h(0, 1)
+        gather(v2_s[1], tab2_s, list2, 1)
+        quantize_w2(1)
+        make_h(0, 2)
+        make_h(0, 3)
+        make_decay(1, 0)
+        gather_tab_scales(1)
+        quantize_h(0, 0)
+        quantize_h(0, 1)
+        for a in range(2):
+            deal_columns(w8_p[a][:].bitcast(I32), w8_raw[a][:].bitcast(I32))
+        deal_columns(w8_s[:], w8s_raw[:])
+        make_h(1, 0)
+        make_h(1, 1)
+        make_decay(0, 1)
+        gather(v_w[0][1], tab_w[0], list1, 1)
+        quantize_h(1, 0)
+        make_h(1, 2)
+        make_h(1, 3)
+        gather(v_w[1][1], tab_w[1], list1, 1)
+        quantize_h(1, 1)
+        make_decay(1, 1)
+        mix(0)
+        for g in range(GROUPS):
+            make_h(g, 4)
+            make_h(g, 5)
+        mix(1)
+        for g in range(GROUPS):
+            quantize_h(g, 2)
+        for g in range(GROUPS):
+            make_h(g, 6)
+            make_h(g, 7)
+        mix(2)
+        for g in range(GROUPS):
+            quantize_h(g, 3)
+        mix(3)

@@ -44,16 +44,18 @@ def tile_list_mixed_layer_step_kernel(
         tab_w = [kept([P, T], U32, "tab_w%d" % a) for a in range(2)]
         tab_s = kept([P, T], U8, "tab_s")
         w2_raw = [[kept([P, PACK, 256], F32, "w2_raw%d%d" % (g, q)) for q in range(2)] for g in range(GROUPS)]
-        w4_raw = [kept([P, H], U16, "w4_raw%d" % a) for a in range(2)]
+        w4_raw = kept([P, 2 * H], U16, "w4_raw")
         w4s_raw = kept([P, 2 * H], U8, "w4s_raw")
         w8_raw = [kept([P, H], U32, "w8_raw%d" % a) for a in range(2)]
         w8s_raw = kept([P, H], U8, "w8s_raw")
         rate_sb = kept([P, GROUPS, PACK], F32, "rate_sb")
         step_sb = kept([P, GROUPS, PACK], F32, "step_sb")
-        v_s1 = [kept([P, GATHER], U8, "v_s1_%d" % c) for c in range(2)]
+        v_s = [kept([P, S], U8, "v_s%d" % a) for a in range(2)]
 
-        for plane in (tab2_s, tab_s, w4s_raw, w8s_raw, v_s1[0], v_s1[1]):
+        for plane in (tab2_s, w4s_raw, v_s[1]):
             nc.vector.memset(plane[:].bitcast(I32), 0)
+        for plane in (tab_s, w8s_raw):
+            nc.gpsimd.memset(plane[:].bitcast(I32), 0)
 
         def load_words(tile, src):
             nc.sync.dma_start(out=tile[:].bitcast(I32), in_=src.bitcast(I32))
@@ -63,30 +65,36 @@ def tile_list_mixed_layer_step_kernel(
             nc.sync.dma_start(out=w2_raw[g][q][:], in_=w2.rearrange("(p j) c -> p j c", j=PACK)[:, :, c0 : c0 + 256])
 
         nc.sync.dma_start(list2[:], offs2)
-        load_words(tab2_w, tab2_words[0])
+        for q in range(2):
+            nc.sync.dma_start(
+                out=tab2_w[:, q * T // 2 : (q + 1) * T // 2].bitcast(I32),
+                in_=tab2_words[0, :, q * T : (q + 1) * T].bitcast(I32),
+            )
+        nc.sync.dma_start(list1[:], offs)
+        load_w2(0, 0)
         for q in range(4):
             nc.sync.dma_start(
                 out=tab2_s[32 * q : 32 * q + 4, :].bitcast(I32), in_=tab2_scales[0, 4 * q : 4 * q + 4, :].bitcast(I32)
             )
-        nc.sync.dma_start(out=rate_sb[:], in_=rate.rearrange("(g p t) -> p g t", g=GROUPS, t=PACK))
-        load_w2(0, 0)
         load_w2(0, 1)
-        nc.sync.dma_start(list1[:], offs)
+        nc.sync.dma_start(out=rate_sb[:], in_=rate.rearrange("(g p t) -> p g t", g=GROUPS, t=PACK))
+        load_w2(1, 0)
+        load_w2(1, 1)
         for q in range(4):
             nc.sync.dma_start(
                 out=tab_s[32 * q : 32 * q + 8, :].bitcast(I32), in_=tab_scales[:, 4 * q : 4 * q + 4, :].bitcast(I32)
             )
-        for a in range(2):
-            load_words(tab_w[a], tab_words[a].rearrange("p t i -> p (t i)"))
-        for a in range(2):
-            load_words(w4_raw[a], w4_words[a])
+        nc.sync.dma_start(
+            out=w4_raw[:].bitcast(I32).rearrange("p (a n) -> p a n", a=2),
+            in_=w4_words.bitcast(I32).rearrange("a p n -> p a n"),
+        )
         for q in range(4):
             nc.sync.dma_start(
                 out=w4s_raw[32 * q : 32 * q + 4, :].bitcast(I32).rearrange("r (a n) -> r a n", a=2),
                 in_=w4_scales[:, 4 * q : 4 * q + 4, :].bitcast(I32).rearrange("a r n -> r a n"),
             )
-        load_w2(1, 0)
-        load_w2(1, 1)
+        for a in range(2):
+            load_words(tab_w[a], tab_words[a].rearrange("p t i -> p (t i)"))
         for a in range(2):
             load_words(w8_raw[a], w8_words[a].rearrange("p c i -> p (c i)"))
         for q in range(4):
@@ -104,62 +112,69 @@ def tile_list_mixed_layer_step_kernel(
         )
         nc.gpsimd.tensor_tensor(root[:], minus_rate[:], half[:], ALU.pow)
 
+        n_chunks = S // CHUNK
         v2_w = [kept([P, GATHER], U16, "v2_w%d" % c) for c in range(2)]
         v2_s = [kept([P, GATHER], U8, "v2_s%d" % c) for c in range(2)]
-        v_w = [[kept([P, GATHER], U32, "v_w%d%d" % (a, c)) for c in range(2)] for a in range(2)]
-        v_s0 = [kept([P, GATHER], U8, "v_s0_%d" % c) for c in range(2)]
         w2_bf = [kept([P, PACK, P, PACK], BF16, "w2_bf%d" % g) for g in range(GROUPS)]
         w2_q = [kept([P, 512], U32, "w2_q%d" % g) for g in range(GROUPS)]
         w2_s = [kept([P, 512], U8, "w2_s%d" % g) for g in range(GROUPS)]
-        w4_p = [kept([P, H], U16, "w4_p%d" % a) for a in range(2)]
+        w4_p = kept([P, 2 * H], U16, "w4_p")
         w4_s = kept([P, 2 * H], U8, "w4_s")
         w8_p = [kept([P, H], U32, "w8_p%d" % a) for a in range(2)]
         w8_s = kept([P, H], U8, "w8_s")
         decay = [[kept([P, 2, GATHER, 2], F32, "decay%d%d" % (g, c)) for c in range(2)] for g in range(GROUPS)]
-        n_chunks = S // CHUNK
-        a_sb = [[kept([P, PACK, CHUNK], F32, "a_sb%d%d" % (g, d)) for d in range(n_chunks)] for g in range(GROUPS)]
+        a_sb = [[kept([P, 2, CHUNK, 2], F32, "a_sb%d%d" % (g, d)) for d in range(n_chunks)] for g in range(GROUPS)]
         h_bf = [[kept([P, CHUNK, PACK], BF16, "h_bf%d%d" % (g, d)) for d in range(n_chunks)] for g in range(GROUPS)]
         h_q = [[kept([P, CHUNK], U32, "h_q%d%d" % (g, d)) for d in range(n_chunks)] for g in range(GROUPS)]
         h_s = [[kept([P, CHUNK], U8, "h_s%d%d" % (g, d)) for d in range(n_chunks)] for g in range(GROUPS)]
+        v_w = {}
 
-        def gather(dst, window, lst, c):
-            cols = GATHER // 16
-            nc.vector.tensor_copy(dst[:], window[:].indirect(lst[:, c * cols : (c + 1) * cols]))
+        def gather(dst, window, lst, first, count):
+            nc.vector.tensor_copy(dst[:], window[:].indirect(lst[:, first // 16 : (first + count) // 16]))
 
-        def gather_tab_scales(c):
-            gather(v_s0[c], tab_s, list1, c)
-            nc.sync.dma_start(out=v_s1[c][0:124, :].bitcast(I32), in_=v_s0[c][4:128, :].bitcast(I32))
+        def gather_tab_words(d):
+            for a in range(2):
+                v_w[a, d] = ring.tile([P, CHUNK], U32, name="v_w%d" % a, bufs=2, align_bytes=64)
+                gather(v_w[a, d], tab_w[a], list1, d * CHUNK, CHUNK)
 
         def cast_w2(g, q):
-            nc.scalar.activation(
-                w2_bf[g][:, :, 64 * q : 64 * (q + 1), :].rearrange("p t m j -> p m j t"),
-                w2_raw[g][q][:].rearrange("p j (m t) -> p m j t", t=PACK),
-                ACT.Copy,
-            )
+            for u in range(2):
+                nc.scalar.activation(
+                    w2_bf[g][:, 2 * u : 2 * u + 2, 64 * q : 64 * (q + 1), :].rearrange("p e m j -> p m j e"),
+                    w2_raw[g][q][:].rearrange("p j (m t) -> p m j t", t=PACK)[:, :, :, 2 * u : 2 * u + 2],
+                    ACT.Copy,
+                )
 
         def quantize_w2(g):
             nc.vector.quantize_mx(
                 out=w2_q[g][:].bitcast(FP8X4), scales=w2_s[g][:], in_=w2_bf[g][:].rearrange("p t m j -> p (t m j)")
             )
 
-        def deal_columns(dst, src):
+        def deal_narrow(dst, src):
             nc.vector.tensor_copy(
-                out=dst.rearrange("p (g t m) -> p g m t", t=PACK, m=P),
-                in_=src.rearrange("p (g m t) -> p g m t", t=PACK, m=P),
+                out=dst.rearrange("p (g t m) -> p g t m", t=PACK, m=P),
+                in_=src.rearrange("p (g m t) -> p g t m", t=PACK, m=P),
             )
 
-        def make_decay(g, c):
+        def deal_words(dst, src):
+            nc.vector.tensor_copy(
+                out=dst.rearrange("p (g u e m) -> p g u m e", u=2, e=2, m=P),
+                in_=src.rearrange("p (g m u e) -> p g u m e", u=2, e=2, m=P),
+            )
+
+        def make_decay(g, first, count):
+            c, n0 = divmod(first, GATHER)
             for u in range(2):
-                square = ring.tile([P, 2, GATHER], F32, name="square")
+                square = ring.tile([P, 2, count], F32, name="square")
                 for e in range(2):
                     t = 2 * u + e
-                    b = psum.tile([P, GATHER], F32, name="b", bufs=2)
+                    b = psum.tile([P, count], F32, name="b", bufs=2)
                     nc.tensor.matmul_mx(
                         out=b[:],
                         lhsT=w2_q[g][:, P * t : P * (t + 1)].bitcast(FP8X4),
                         lhsT_scale=w2_s[g][:, P * t : P * (t + 1)],
-                        rhs=v2_w[c][:].bitcast(FP4X4),
-                        rhs_scale=v2_s[c][:],
+                        rhs=v2_w[c][:, n0 : n0 + count].bitcast(FP4X4),
+                        rhs_scale=v2_s[c][:, n0 : n0 + count],
                         start=True,
                         stop=True,
                     )
@@ -167,32 +182,37 @@ def tile_list_mixed_layer_step_kernel(
                         square[:, e, :], b[:], ACT.Square, scale=root[:, PACK * g + t : PACK * g + t + 1]
                     )
                 nc.scalar.activation(
-                    decay[g][c][:, u, :, :], square[:].rearrange("p e n -> p n e"), ACT.Exp, scale=-1.0
+                    decay[g][c][:, u, n0 : n0 + count, :], square[:].rearrange("p e n -> p n e"), ACT.Exp, scale=-1.0
                 )
 
-        def make_h(g, j):
-            c, n0 = divmod(j * BLOCK, GATHER)
-            d, m0 = divmod(j * BLOCK, CHUNK)
-            acc = psum.tile([P, PACK, BLOCK], F32, name="acc", bufs=3)
-            for t in range(PACK):
-                col = 512 * g + P * t
-                for a in range(2):
-                    nc.tensor.matmul_mx(
-                        out=acc[:, t, :],
-                        lhsT=w4_p[a][:, col : col + P].bitcast(FP4X4),
-                        lhsT_scale=w4_s[:, H * a + col : H * a + col + P],
-                        rhs=v_w[a][c][:, n0 : n0 + BLOCK].bitcast(FP8X4),
-                        rhs_scale=(v_s0, v_s1)[a][c][:, n0 : n0 + BLOCK],
-                        start=(a == 0),
-                        stop=(a == 1),
-                    )
+        def make_a(g, d):
+            for m0 in range(0, CHUNK, BLOCK):
+                n0 = d * CHUNK + m0
+                acc = psum.tile([P, PACK, BLOCK], F32, name="acc", bufs=3)
+                for t in range(PACK):
+                    for a in range(2):
+                        col = H * a + 512 * g + P * t
+                        nc.tensor.matmul_mx(
+                            out=acc[:, t, :],
+                            lhsT=w4_p[:, col : col + P].bitcast(FP4X4),
+                            lhsT_scale=w4_s[:, col : col + P],
+                            rhs=v_w[a, d][:, m0 : m0 + BLOCK].bitcast(FP8X4),
+                            rhs_scale=v_s[a][:, n0 : n0 + BLOCK],
+                            start=(a == 0),
+                            stop=(a == 1),
+                        )
+                nc.scalar.activation(
+                    a_sb[g][d][:, :, m0 : m0 + BLOCK, :], acc[:].rearrange("p (u e) n -> p u n e", u=2), ACT.Copy
+                )
+
+        def make_h(g, d):
+            c, n0 = divmod(d * CHUNK, GATHER)
             nc.vector.tensor_tensor(
-                h_bf[g][d][:, m0 : m0 + BLOCK, :].rearrange("p n (u e) -> p n u e", u=2),
-                acc[:].rearrange("p (u e) n -> p n u e", u=2),
-                decay[g][c][:, :, n0 : n0 + BLOCK, :].rearrange("p u n e -> p n u e"),
+                h_bf[g][d][:].rearrange("p n (u e) -> p n u e", u=2),
+                a_sb[g][d][:].rearrange("p u n e -> p n u e"),
+                decay[g][c][:, :, n0 : n0 + CHUNK, :].rearrange("p u n e -> p n u e"),
                 ALU.mult,
             )
-            nc.scalar.activation(a_sb[g][d][:, :, m0 : m0 + BLOCK], acc[:], ACT.Copy)
 
         def quantize_h(g, d):
             nc.vector.quantize_mx(
@@ -203,8 +223,8 @@ def tile_list_mixed_layer_step_kernel(
 
         def mix(d):
             for g in range(GROUPS):
-                result = ring.tile([P, PACK, CHUNK], F32, name="result")
                 for u in range(2):
+                    result = ring.tile([P, 2, CHUNK], F32, name="result", bufs=6)
                     y = psum.tile([P, 2, CHUNK], F32, name="y", bufs=3)
                     for e in range(2):
                         col = 512 * g + P * (2 * u + e)
@@ -221,60 +241,44 @@ def tile_list_mixed_layer_step_kernel(
                     for e in range(2):
                         t = 2 * u + e
                         nc.vector.scalar_tensor_tensor(
-                            result[:, t, :], a_sb[g][d][:, t, :], step_sb[:, g, t : t + 1], y[:, e, :],
+                            result[:, e, :], a_sb[g][d][:, u, :, e], step_sb[:, g, t : t + 1], y[:, e, :],
                             ALU.mult, ALU.add,
                         )
-                nc.sync.dma_start(out=out_rows[g][:, :, d * CHUNK : (d + 1) * CHUNK], in_=result[:])
+                    nc.sync.dma_start(
+                        out=out_rows[g][:, 2 * u : 2 * u + 2, d * CHUNK : (d + 1) * CHUNK], in_=result[:]
+                    )
 
-        gather(v2_w[0], tab2_w, list2, 0)
-        gather(v2_s[0], tab2_s, list2, 0)
-        cast_w2(0, 0)
-        cast_w2(0, 1)
-        gather_tab_scales(0)
-        quantize_w2(0)
-        make_decay(0, 0)
-        gather(v_w[0][0], tab_w[0], list1, 0)
-        gather(v2_w[1], tab2_w, list2, 1)
-        gather(v_w[1][0], tab_w[1], list1, 0)
+        for c in range(2):
+            gather(v2_w[c], tab2_w, list2, c * GATHER, GATHER)
+        for c in range(2):
+            gather(v2_s[c], tab2_s, list2, c * GATHER, GATHER)
+        for g in range(GROUPS):
+            cast_w2(g, 0)
+            cast_w2(g, 1)
+            quantize_w2(g)
+        gather(v_s[0], tab_s, list1, 0, S)
+        nc.gpsimd.dma_start(out=v_s[1][0:124, :].bitcast(I32), in_=v_s[0][4:128, :].bitcast(I32))
+        deal_narrow(w4_p[:], w4_raw[:])
+        deal_narrow(w4_s[:], w4s_raw[:])
+        gather_tab_words(0)
+        gather_tab_words(1)
+        make_decay(0, 0, GATHER)
+        make_a(0, 0)
+        make_decay(1, 0, GATHER)
+        make_a(1, 0)
         for a in range(2):
-            deal_columns(w4_p[a][:], w4_raw[a][:])
-        deal_columns(w4_s[:], w4s_raw[:])
-        cast_w2(1, 0)
-        cast_w2(1, 1)
-        make_h(0, 0)
-        make_h(0, 1)
-        gather(v2_s[1], tab2_s, list2, 1)
-        quantize_w2(1)
-        make_h(0, 2)
-        make_h(0, 3)
-        make_decay(1, 0)
-        gather_tab_scales(1)
-        quantize_h(0, 0)
-        quantize_h(0, 1)
-        for a in range(2):
-            deal_columns(w8_p[a][:].bitcast(I32), w8_raw[a][:].bitcast(I32))
-        deal_columns(w8_s[:], w8s_raw[:])
-        make_h(1, 0)
-        make_h(1, 1)
-        make_decay(0, 1)
-        gather(v_w[0][1], tab_w[0], list1, 1)
-        quantize_h(1, 0)
-        make_h(1, 2)
-        make_h(1, 3)
-        gather(v_w[1][1], tab_w[1], list1, 1)
-        quantize_h(1, 1)
-        make_decay(1, 1)
-        mix(0)
-        for g in range(GROUPS):
-            make_h(g, 4)
-            make_h(g, 5)
-        mix(1)
-        for g in range(GROUPS):
-            quantize_h(g, 2)
-        for g in range(GROUPS):
-            make_h(g, 6)
-            make_h(g, 7)
-        mix(2)
-        for g in range(GROUPS):
-            quantize_h(g, 3)
-        mix(3)
+            deal_words(w8_p[a][:].bitcast(I32), w8_raw[a][:].bitcast(I32))
+        deal_narrow(w8_s[:], w8s_raw[:])
+        for d in range(n_chunks):
+            for g in range(GROUPS):
+                make_h(g, d)
+            if d + 2 < n_chunks:
+                gather_tab_words(d + 2)
+            for g in range(GROUPS):
+                quantize_h(g, d)
+            if d + 1 < n_chunks:
+                for g in range(GROUPS):
+                    if (d + 1) * CHUNK >= GATHER:
+                        make_decay(g, (d + 1) * CHUNK, CHUNK)
+                    make_a(g, d + 1)
+            mix(d)

@@ -22,6 +22,7 @@ GROUPS = 2
 GATHER = 512
 BLOCK = 128
 CHUNK = 256
+SPANS = ((0, 256), (256, 256), (512, 256), (768, 128), (896, 128))
 
 
 def tile_list_mixed_layer_step_kernel(
@@ -45,17 +46,15 @@ def tile_list_mixed_layer_step_kernel(
         tab_s = kept([P, T], U8, "tab_s")
         w2_raw = [[kept([P, PACK, 256], F32, "w2_raw%d%d" % (g, q)) for q in range(2)] for g in range(GROUPS)]
         w4_raw = kept([P, 2 * H], U16, "w4_raw")
-        w4s_raw = kept([P, 2 * H], U8, "w4s_raw")
+        ws_raw = kept([P, 2 * H], U8, "ws_raw")
         w8_raw = [kept([P, H], U32, "w8_raw%d" % a) for a in range(2)]
-        w8s_raw = kept([P, H], U8, "w8s_raw")
         rate_sb = kept([P, GROUPS, PACK], F32, "rate_sb")
         step_sb = kept([P, GROUPS, PACK], F32, "step_sb")
         v_s = [kept([P, S], U8, "v_s%d" % a) for a in range(2)]
 
-        for plane in (tab2_s, w4s_raw, v_s[1]):
+        for plane in (tab2_s, ws_raw, v_s[1]):
             nc.vector.memset(plane[:].bitcast(I32), 0)
-        for plane in (tab_s, w8s_raw):
-            nc.gpsimd.memset(plane[:].bitcast(I32), 0)
+        nc.gpsimd.memset(tab_s[:].bitcast(I32), 0)
 
         def load_words(tile, src):
             nc.sync.dma_start(out=tile[:].bitcast(I32), in_=src.bitcast(I32))
@@ -79,28 +78,29 @@ def tile_list_mixed_layer_step_kernel(
         load_w2(0, 1)
         nc.sync.dma_start(out=rate_sb[:], in_=rate.rearrange("(g p t) -> p g t", g=GROUPS, t=PACK))
         load_w2(1, 0)
-        load_w2(1, 1)
         for q in range(4):
             nc.sync.dma_start(
                 out=tab_s[32 * q : 32 * q + 8, :].bitcast(I32), in_=tab_scales[:, 4 * q : 4 * q + 4, :].bitcast(I32)
             )
+        load_w2(1, 1)
         nc.sync.dma_start(
             out=w4_raw[:].bitcast(I32).rearrange("p (a n) -> p a n", a=2),
             in_=w4_words.bitcast(I32).rearrange("a p n -> p a n"),
         )
         for q in range(4):
             nc.sync.dma_start(
-                out=w4s_raw[32 * q : 32 * q + 4, :].bitcast(I32).rearrange("r (a n) -> r a n", a=2),
+                out=ws_raw[32 * q : 32 * q + 4, :].bitcast(I32).rearrange("r (a n) -> r a n", a=2),
                 in_=w4_scales[:, 4 * q : 4 * q + 4, :].bitcast(I32).rearrange("a r n -> r a n"),
+            )
+        for q in range(4):
+            nc.sync.dma_start(
+                out=ws_raw[32 * q + 4 : 32 * q + 12, 0:H].bitcast(I32),
+                in_=w8_scales[:, 4 * q : 4 * q + 4, :].bitcast(I32),
             )
         for a in range(2):
             load_words(tab_w[a], tab_words[a].rearrange("p t i -> p (t i)"))
         for a in range(2):
             load_words(w8_raw[a], w8_words[a].rearrange("p c i -> p (c i)"))
-        for q in range(4):
-            nc.sync.dma_start(
-                out=w8s_raw[32 * q : 32 * q + 8, :].bitcast(I32), in_=w8_scales[:, 4 * q : 4 * q + 4, :].bitcast(I32)
-            )
         nc.sync.dma_start(out=step_sb[:], in_=step.rearrange("(g p t) -> p g t", g=GROUPS, t=PACK))
 
         minus_rate = kept([P, GROUPS * PACK], F32, "minus_rate")
@@ -112,29 +112,33 @@ def tile_list_mixed_layer_step_kernel(
         )
         nc.gpsimd.tensor_tensor(root[:], minus_rate[:], half[:], ALU.pow)
 
-        n_chunks = S // CHUNK
         v2_w = [kept([P, GATHER], U16, "v2_w%d" % c) for c in range(2)]
         v2_s = [kept([P, GATHER], U8, "v2_s%d" % c) for c in range(2)]
         w2_bf = [kept([P, PACK, P, PACK], BF16, "w2_bf%d" % g) for g in range(GROUPS)]
         w2_q = [kept([P, 512], U32, "w2_q%d" % g) for g in range(GROUPS)]
         w2_s = [kept([P, 512], U8, "w2_s%d" % g) for g in range(GROUPS)]
         w4_p = kept([P, 2 * H], U16, "w4_p")
-        w4_s = kept([P, 2 * H], U8, "w4_s")
+        w_s = kept([P, 2 * H], U8, "w_s")
         w8_p = [kept([P, H], U32, "w8_p%d" % a) for a in range(2)]
-        w8_s = kept([P, H], U8, "w8_s")
         decay = [[kept([P, 2, GATHER, 2], F32, "decay%d%d" % (g, c)) for c in range(2)] for g in range(GROUPS)]
-        a_sb = [[kept([P, 2, CHUNK, 2], F32, "a_sb%d%d" % (g, d)) for d in range(n_chunks)] for g in range(GROUPS)]
-        h_bf = [[kept([P, CHUNK, PACK], BF16, "h_bf%d%d" % (g, d)) for d in range(n_chunks)] for g in range(GROUPS)]
-        h_q = [[kept([P, CHUNK], U32, "h_q%d%d" % (g, d)) for d in range(n_chunks)] for g in range(GROUPS)]
-        h_s = [[kept([P, CHUNK], U8, "h_s%d%d" % (g, d)) for d in range(n_chunks)] for g in range(GROUPS)]
+        a_sb = [[kept([P, 2, n, 2], F32, "a_sb%d%d" % (g, d)) for d, (f, n) in enumerate(SPANS)] for g in range(GROUPS)]
+        h_q = [[kept([P, n], U32, "h_q%d%d" % (g, d)) for d, (f, n) in enumerate(SPANS)] for g in range(GROUPS)]
+        h_s = [[kept([P, n], U8, "h_s%d%d" % (g, d)) for d, (f, n) in enumerate(SPANS)] for g in range(GROUPS)]
+        h_bf = {}
         v_w = {}
+        banks = [psum.tile([P, 512], F32, name="bank%d" % i) for i in range(6)]
+        taken = []
+
+        def take_bank():
+            taken.append(banks[len(taken) % len(banks)])
+            return taken[-1]
 
         def gather(dst, window, lst, first, count):
             nc.vector.tensor_copy(dst[:], window[:].indirect(lst[:, first // 16 : (first + count) // 16]))
 
         def gather_tab_words(d):
             for a in range(2):
-                v_w[a, d] = ring.tile([P, CHUNK], U32, name="v_w%d" % a, bufs=2, align_bytes=64)
+                v_w[a, d] = kept([P, CHUNK], U32, "v_w%d%d" % (a, d))
                 gather(v_w[a, d], tab_w[a], list1, d * CHUNK, CHUNK)
 
         def cast_w2(g, q):
@@ -144,6 +148,12 @@ def tile_list_mixed_layer_step_kernel(
                     w2_raw[g][q][:].rearrange("p j (m t) -> p m j t", t=PACK)[:, :, :, 2 * u : 2 * u + 2],
                     ACT.Copy,
                 )
+
+        def cast_w2_on_vector(g, q):
+            nc.vector.tensor_copy(
+                out=w2_bf[g][:, :, 64 * q : 64 * (q + 1), :].rearrange("p (u e) m j -> p u m j e", u=2),
+                in_=w2_raw[g][q][:].rearrange("p j (m u e) -> p u m j e", u=2, e=2),
+            )
 
         def quantize_w2(g):
             nc.vector.quantize_mx(
@@ -168,9 +178,9 @@ def tile_list_mixed_layer_step_kernel(
                 square = ring.tile([P, 2, count], F32, name="square")
                 for e in range(2):
                     t = 2 * u + e
-                    b = psum.tile([P, count], F32, name="b", bufs=2)
+                    b = take_bank()[:, 0:count]
                     nc.tensor.matmul_mx(
-                        out=b[:],
+                        out=b,
                         lhsT=w2_q[g][:, P * t : P * (t + 1)].bitcast(FP8X4),
                         lhsT_scale=w2_s[g][:, P * t : P * (t + 1)],
                         rhs=v2_w[c][:, n0 : n0 + count].bitcast(FP4X4),
@@ -179,106 +189,113 @@ def tile_list_mixed_layer_step_kernel(
                         stop=True,
                     )
                     nc.scalar.activation(
-                        square[:, e, :], b[:], ACT.Square, scale=root[:, PACK * g + t : PACK * g + t + 1]
+                        square[:, e, :], b, ACT.Square, scale=root[:, PACK * g + t : PACK * g + t + 1]
                     )
                 nc.scalar.activation(
                     decay[g][c][:, u, n0 : n0 + count, :], square[:].rearrange("p e n -> p n e"), ACT.Exp, scale=-1.0
                 )
 
-        def make_a(g, d):
-            for m0 in range(0, CHUNK, BLOCK):
-                n0 = d * CHUNK + m0
-                acc = psum.tile([P, PACK, BLOCK], F32, name="acc", bufs=3)
+        def make_h(g, d, from_psum):
+            first, count = SPANS[d]
+            c, n0 = divmod(first, GATHER)
+            h_bf[g, d] = ring.tile([P, count, PACK], BF16, name="h_bf%d" % g, bufs=2, align_bytes=64)
+            for m0 in range(0, count, BLOCK):
+                k, w0 = divmod(first + m0, CHUNK)
+                acc = take_bank()[:].rearrange("p (t n) -> p t n", t=PACK)
                 for t in range(PACK):
                     for a in range(2):
                         col = H * a + 512 * g + P * t
                         nc.tensor.matmul_mx(
                             out=acc[:, t, :],
                             lhsT=w4_p[:, col : col + P].bitcast(FP4X4),
-                            lhsT_scale=w4_s[:, col : col + P],
-                            rhs=v_w[a, d][:, m0 : m0 + BLOCK].bitcast(FP8X4),
-                            rhs_scale=v_s[a][:, n0 : n0 + BLOCK],
+                            lhsT_scale=w_s[:, col : col + P],
+                            rhs=v_w[a, k][:, w0 : w0 + BLOCK].bitcast(FP8X4),
+                            rhs_scale=v_s[a][:, first + m0 : first + m0 + BLOCK],
                             start=(a == 0),
                             stop=(a == 1),
                         )
+                if from_psum:
+                    nc.vector.tensor_tensor(
+                        h_bf[g, d][:, m0 : m0 + BLOCK, :].rearrange("p n (u e) -> p n u e", u=2),
+                        acc.rearrange("p (u e) n -> p n u e", u=2),
+                        decay[g][c][:, :, n0 + m0 : n0 + m0 + BLOCK, :].rearrange("p u n e -> p n u e"),
+                        ALU.mult,
+                    )
                 nc.scalar.activation(
-                    a_sb[g][d][:, :, m0 : m0 + BLOCK, :], acc[:].rearrange("p (u e) n -> p u n e", u=2), ACT.Copy
+                    a_sb[g][d][:, :, m0 : m0 + BLOCK, :], acc.rearrange("p (u e) n -> p u n e", u=2), ACT.Copy
                 )
-
-        def make_h(g, d):
-            c, n0 = divmod(d * CHUNK, GATHER)
-            nc.vector.tensor_tensor(
-                h_bf[g][d][:].rearrange("p n (u e) -> p n u e", u=2),
-                a_sb[g][d][:].rearrange("p u n e -> p n u e"),
-                decay[g][c][:, :, n0 : n0 + CHUNK, :].rearrange("p u n e -> p n u e"),
-                ALU.mult,
-            )
+            if not from_psum:
+                nc.vector.tensor_tensor(
+                    h_bf[g, d][:].rearrange("p n (u e) -> p n u e", u=2),
+                    a_sb[g][d][:].rearrange("p u n e -> p n u e"),
+                    decay[g][c][:, :, n0 : n0 + count, :].rearrange("p u n e -> p n u e"),
+                    ALU.mult,
+                )
 
         def quantize_h(g, d):
             nc.vector.quantize_mx(
-                out=h_q[g][d][:].bitcast(FP8X4), scales=h_s[g][d][:], in_=h_bf[g][d][:].rearrange("p n t -> p (n t)")
+                out=h_q[g][d][:].bitcast(FP8X4), scales=h_s[g][d][:], in_=h_bf[g, d][:].rearrange("p n t -> p (n t)")
             )
 
         out_rows = out.rearrange("(g p t) j -> g p t j", g=GROUPS, t=PACK)
 
         def mix(d):
+            first, count = SPANS[d]
+            per_bank = 512 // count
             for g in range(GROUPS):
-                for u in range(2):
-                    result = ring.tile([P, 2, CHUNK], F32, name="result", bufs=6)
-                    y = psum.tile([P, 2, CHUNK], F32, name="y", bufs=3)
-                    for e in range(2):
-                        col = 512 * g + P * (2 * u + e)
+                for t0 in range(0, PACK, per_bank):
+                    result = ring.tile([P, per_bank, count], F32, name="result", bufs=6)
+                    y = psum.tile([P, per_bank, count], F32, name="y", bufs=2)
+                    for i in range(per_bank):
+                        col = 512 * g + P * (t0 + i)
                         for a in range(2):
                             nc.tensor.matmul_mx(
-                                out=y[:, e, :],
+                                out=y[:, i, :],
                                 lhsT=w8_p[a][:, col : col + P].bitcast(FP8X4),
-                                lhsT_scale=w8_s[4 * a : P, col : col + P],
+                                lhsT_scale=w_s[4 + 4 * a : P, col : col + P],
                                 rhs=h_q[a][d][:].bitcast(FP8X4),
                                 rhs_scale=h_s[a][d][:],
                                 start=(a == 0),
                                 stop=(a == 1),
                             )
-                    for e in range(2):
-                        t = 2 * u + e
+                    for i in range(per_bank):
+                        t = t0 + i
                         nc.vector.scalar_tensor_tensor(
-                            result[:, e, :], a_sb[g][d][:, u, :, e], step_sb[:, g, t : t + 1], y[:, e, :],
+                            result[:, i, :], a_sb[g][d][:, t // 2, :, t % 2], step_sb[:, g, t : t + 1], y[:, i, :],
                             ALU.mult, ALU.add,
                         )
-                    nc.sync.dma_start(
-                        out=out_rows[g][:, 2 * u : 2 * u + 2, d * CHUNK : (d + 1) * CHUNK], in_=result[:]
-                    )
+                    nc.sync.dma_start(out=out_rows[g][:, t0 : t0 + per_bank, first : first + count], in_=result[:])
 
         for c in range(2):
             gather(v2_w[c], tab2_w, list2, c * GATHER, GATHER)
         for c in range(2):
             gather(v2_s[c], tab2_s, list2, c * GATHER, GATHER)
-        for g in range(GROUPS):
-            cast_w2(g, 0)
-            cast_w2(g, 1)
-            quantize_w2(g)
+        cast_w2(0, 0)
+        cast_w2(0, 1)
+        quantize_w2(0)
+        cast_w2(1, 0)
         gather(v_s[0], tab_s, list1, 0, S)
         nc.gpsimd.dma_start(out=v_s[1][0:124, :].bitcast(I32), in_=v_s[0][4:128, :].bitcast(I32))
-        deal_narrow(w4_p[:], w4_raw[:])
-        deal_narrow(w4_s[:], w4s_raw[:])
-        gather_tab_words(0)
-        gather_tab_words(1)
+        cast_w2_on_vector(1, 1)
         make_decay(0, 0, GATHER)
-        make_a(0, 0)
+        quantize_w2(1)
+        deal_narrow(w4_p[:], w4_raw[:])
+        deal_narrow(w_s[:], ws_raw[:])
+        for k in range(S // CHUNK):
+            gather_tab_words(k)
         make_decay(1, 0, GATHER)
-        make_a(1, 0)
         for a in range(2):
             deal_words(w8_p[a][:].bitcast(I32), w8_raw[a][:].bitcast(I32))
-        deal_narrow(w8_s[:], w8s_raw[:])
-        for d in range(n_chunks):
-            for g in range(GROUPS):
-                make_h(g, d)
-            if d + 2 < n_chunks:
-                gather_tab_words(d + 2)
-            for g in range(GROUPS):
-                quantize_h(g, d)
-            if d + 1 < n_chunks:
-                for g in range(GROUPS):
-                    if (d + 1) * CHUNK >= GATHER:
-                        make_decay(g, (d + 1) * CHUNK, CHUNK)
-                    make_a(g, d + 1)
+        last = len(SPANS) - 1
+        make_h(1, 0, False)
+        make_h(0, 0, False)
+        for d in range(len(SPANS)):
+            quantize_h(0, d)
+            quantize_h(1, d)
+            if d < last:
+                first = SPANS[d + 1][0]
+                for g in (1, 0):
+                    if first >= GATHER and first % CHUNK == 0:
+                        make_decay(g, first, CHUNK)
+                    make_h(g, d + 1, d + 1 == last)
             mix(d)

@@ -69,24 +69,15 @@ def tile_list_mixed_layer_step_kernel(
                 out=tab2_w[:, q * T // 2 : (q + 1) * T // 2].bitcast(I32),
                 in_=tab2_words[0, :, q * T : (q + 1) * T].bitcast(I32),
             )
-        nc.sync.dma_start(list1[:], offs)
+        nc.sync.dma_start(out=rate_sb[:], in_=rate.rearrange("(g p t) -> p g t", g=GROUPS, t=PACK))
         load_w2(0, 0)
         for q in range(4):
             nc.sync.dma_start(
                 out=tab2_s[32 * q : 32 * q + 4, :].bitcast(I32), in_=tab2_scales[0, 4 * q : 4 * q + 4, :].bitcast(I32)
             )
         load_w2(0, 1)
-        nc.sync.dma_start(out=rate_sb[:], in_=rate.rearrange("(g p t) -> p g t", g=GROUPS, t=PACK))
+        nc.sync.dma_start(list1[:], offs)
         load_w2(1, 0)
-        for q in range(4):
-            nc.sync.dma_start(
-                out=tab_s[32 * q : 32 * q + 8, :].bitcast(I32), in_=tab_scales[:, 4 * q : 4 * q + 4, :].bitcast(I32)
-            )
-        load_w2(1, 1)
-        nc.sync.dma_start(
-            out=w4_raw[:].bitcast(I32).rearrange("p (a n) -> p a n", a=2),
-            in_=w4_words.bitcast(I32).rearrange("a p n -> p a n"),
-        )
         for q in range(4):
             nc.sync.dma_start(
                 out=ws_raw[32 * q : 32 * q + 4, :].bitcast(I32).rearrange("r (a n) -> r a n", a=2),
@@ -97,20 +88,25 @@ def tile_list_mixed_layer_step_kernel(
                 out=ws_raw[32 * q + 4 : 32 * q + 12, 0:H].bitcast(I32),
                 in_=w8_scales[:, 4 * q : 4 * q + 4, :].bitcast(I32),
             )
+        for q in range(4):
+            nc.sync.dma_start(
+                out=tab_s[32 * q : 32 * q + 8, :].bitcast(I32), in_=tab_scales[:, 4 * q : 4 * q + 4, :].bitcast(I32)
+            )
+        load_w2(1, 1)
+        nc.sync.dma_start(
+            out=w4_raw[:].bitcast(I32).rearrange("p (a n) -> p a n", a=2),
+            in_=w4_words.bitcast(I32).rearrange("a p n -> p a n"),
+        )
         for a in range(2):
             load_words(tab_w[a], tab_words[a].rearrange("p t i -> p (t i)"))
         for a in range(2):
             load_words(w8_raw[a], w8_words[a].rearrange("p c i -> p (c i)"))
         nc.sync.dma_start(out=step_sb[:], in_=step.rearrange("(g p t) -> p g t", g=GROUPS, t=PACK))
 
-        minus_rate = kept([P, GROUPS * PACK], F32, "minus_rate")
-        half = kept([P, GROUPS * PACK], F32, "half")
+        log_rate = kept([P, GROUPS * PACK], F32, "log_rate")
         root = kept([P, GROUPS * PACK], F32, "root")
-        nc.gpsimd.memset(half[:], 0.5)
-        nc.gpsimd.tensor_scalar(
-            minus_rate[:], rate_sb[:].rearrange("p g t -> p (g t)"), -1.0, 0.0, ALU.mult, ALU.add
-        )
-        nc.gpsimd.tensor_tensor(root[:], minus_rate[:], half[:], ALU.pow)
+        nc.scalar.activation(log_rate[:], rate_sb[:].rearrange("p g t -> p (g t)"), ACT.Ln, scale=-1.0)
+        nc.scalar.activation(root[:], log_rate[:], ACT.Exp, scale=0.5)
 
         v2_w = [kept([P, GATHER], U16, "v2_w%d" % c) for c in range(2)]
         v2_s = [kept([P, GATHER], U8, "v2_s%d" % c) for c in range(2)]
@@ -274,13 +270,16 @@ def tile_list_mixed_layer_step_kernel(
         cast_w2(0, 1)
         quantize_w2(0)
         cast_w2(1, 0)
+        deal_narrow(w_s[:], ws_raw[:])
         gather(v_s[0], tab_s, list1, 0, S)
-        nc.gpsimd.dma_start(out=v_s[1][0:124, :].bitcast(I32), in_=v_s[0][4:128, :].bitcast(I32))
+        for q in range(4):
+            nc.scalar.dma_start(
+                out=v_s[1][32 * q : 32 * q + 4, :].bitcast(I32), in_=v_s[0][32 * q + 4 : 32 * q + 8, :].bitcast(I32)
+            )
         cast_w2_on_vector(1, 1)
         make_decay(0, 0, GATHER)
         quantize_w2(1)
         deal_narrow(w4_p[:], w4_raw[:])
-        deal_narrow(w_s[:], ws_raw[:])
         for k in range(S // CHUNK):
             gather_tab_words(k)
         make_decay(1, 0, GATHER)

@@ -18,11 +18,17 @@ ACT = mybir.ActivationFunctionType
 
 P = 128
 PACK = 4
-GROUPS = 2
-GATHER = 512
-BLOCK = 128
+K_PASS = P * PACK
+PASSES = K // K_PASS
+GROUPS = H // K_PASS
+QUADS = 4
+BANK = 512
+HALF = S // 2
 CHUNK = 256
+BLOCK = BANK // PACK
+W2_COLS = 256
 SPANS = ((0, 256), (256, 256), (512, 256), (768, 128), (896, 128))
+RING_BANKS = 6
 
 
 def tile_list_mixed_layer_step_kernel(
@@ -42,15 +48,15 @@ def tile_list_mixed_layer_step_kernel(
         list2 = kept([P, S // 16], U16, "list2")
         tab2_w = kept([P, T], U16, "tab2_w")
         tab2_s = kept([P, T], U8, "tab2_s")
-        tab_w = [kept([P, T], U32, "tab_w%d" % a) for a in range(2)]
+        tab_w = [kept([P, T], U32, "tab_w%d" % s) for s in range(PASSES)]
         tab_s = kept([P, T], U8, "tab_s")
-        w2_raw = [[kept([P, PACK, 256], F32, "w2_raw%d%d" % (g, q)) for q in range(2)] for g in range(GROUPS)]
-        w4_raw = kept([P, 2 * H], U16, "w4_raw")
-        ws_raw = kept([P, 2 * H], U8, "ws_raw")
-        w8_raw = [kept([P, H], U32, "w8_raw%d" % a) for a in range(2)]
+        w2_raw = [[kept([P, PACK, W2_COLS], F32, "w2_raw%d%d" % (g, q)) for q in range(2)] for g in range(GROUPS)]
+        w4_raw = kept([P, PASSES * H], U16, "w4_raw")
+        ws_raw = kept([P, PASSES * H], U8, "ws_raw")
+        w8_raw = [kept([P, H], U32, "w8_raw%d" % s) for s in range(PASSES)]
         rate_sb = kept([P, GROUPS, PACK], F32, "rate_sb")
         step_sb = kept([P, GROUPS, PACK], F32, "step_sb")
-        v_s = [kept([P, S], U8, "v_s%d" % a) for a in range(2)]
+        v_s = [kept([P, S], U8, "v_s%d" % s) for s in range(PASSES)]
 
         for plane in (tab2_s, ws_raw, v_s[1]):
             nc.vector.memset(plane[:].bitcast(I32), 0)
@@ -60,8 +66,10 @@ def tile_list_mixed_layer_step_kernel(
             nc.sync.dma_start(out=tile[:].bitcast(I32), in_=src.bitcast(I32))
 
         def load_w2(g, q):
-            c0 = 512 * g + 256 * q
-            nc.sync.dma_start(out=w2_raw[g][q][:], in_=w2.rearrange("(p j) c -> p j c", j=PACK)[:, :, c0 : c0 + 256])
+            c0 = K_PASS * g + W2_COLS * q
+            nc.sync.dma_start(
+                out=w2_raw[g][q][:], in_=w2.rearrange("(p i) c -> p i c", i=PACK)[:, :, c0 : c0 + W2_COLS]
+            )
 
         nc.sync.dma_start(list2[:], offs2)
         for q in range(2):
@@ -71,36 +79,36 @@ def tile_list_mixed_layer_step_kernel(
             )
         nc.sync.dma_start(out=rate_sb[:], in_=rate.rearrange("(g p t) -> p g t", g=GROUPS, t=PACK))
         load_w2(0, 0)
-        for q in range(4):
+        for z in range(QUADS):
             nc.sync.dma_start(
-                out=tab2_s[32 * q : 32 * q + 4, :].bitcast(I32), in_=tab2_scales[0, 4 * q : 4 * q + 4, :].bitcast(I32)
+                out=tab2_s[32 * z : 32 * z + 4, :].bitcast(I32), in_=tab2_scales[0, 4 * z : 4 * z + 4, :].bitcast(I32)
             )
         load_w2(0, 1)
         nc.sync.dma_start(list1[:], offs)
         load_w2(1, 0)
-        for q in range(4):
-            nc.sync.dma_start(
-                out=ws_raw[32 * q : 32 * q + 4, :].bitcast(I32).rearrange("r (a n) -> r a n", a=2),
-                in_=w4_scales[:, 4 * q : 4 * q + 4, :].bitcast(I32).rearrange("a r n -> r a n"),
-            )
-        for q in range(4):
-            nc.sync.dma_start(
-                out=ws_raw[32 * q + 4 : 32 * q + 12, 0:H].bitcast(I32),
-                in_=w8_scales[:, 4 * q : 4 * q + 4, :].bitcast(I32),
-            )
-        for q in range(4):
-            nc.sync.dma_start(
-                out=tab_s[32 * q : 32 * q + 8, :].bitcast(I32), in_=tab_scales[:, 4 * q : 4 * q + 4, :].bitcast(I32)
-            )
         load_w2(1, 1)
+        for z in range(QUADS):
+            nc.sync.dma_start(
+                out=ws_raw[32 * z + 4 : 32 * z + 12, 0:H].bitcast(I32),
+                in_=w8_scales[:, 4 * z : 4 * z + 4, :].bitcast(I32),
+            )
+        for z in range(QUADS):
+            nc.sync.dma_start(
+                out=tab_s[32 * z : 32 * z + 8, :].bitcast(I32), in_=tab_scales[:, 4 * z : 4 * z + 4, :].bitcast(I32)
+            )
+        for z in range(QUADS):
+            nc.sync.dma_start(
+                out=ws_raw[32 * z : 32 * z + 4, :].bitcast(I32).rearrange("r (s c) -> r s c", s=PASSES),
+                in_=w4_scales[:, 4 * z : 4 * z + 4, :].bitcast(I32).rearrange("s r c -> r s c"),
+            )
         nc.sync.dma_start(
-            out=w4_raw[:].bitcast(I32).rearrange("p (a n) -> p a n", a=2),
-            in_=w4_words.bitcast(I32).rearrange("a p n -> p a n"),
+            out=w4_raw[:].bitcast(I32).rearrange("p (s c) -> p s c", s=PASSES),
+            in_=w4_words.bitcast(I32).rearrange("s p c -> p s c"),
         )
-        for a in range(2):
-            load_words(tab_w[a], tab_words[a].rearrange("p t i -> p (t i)"))
-        for a in range(2):
-            load_words(w8_raw[a], w8_words[a].rearrange("p c i -> p (c i)"))
+        for s in range(PASSES):
+            load_words(tab_w[s], tab_words[s].rearrange("p c i -> p (c i)"))
+        for s in range(PASSES):
+            load_words(w8_raw[s], w8_words[s].rearrange("p c i -> p (c i)"))
         nc.sync.dma_start(out=step_sb[:], in_=step.rearrange("(g p t) -> p g t", g=GROUPS, t=PACK))
 
         log_rate = kept([P, GROUPS * PACK], F32, "log_rate")
@@ -108,52 +116,54 @@ def tile_list_mixed_layer_step_kernel(
         nc.scalar.activation(log_rate[:], rate_sb[:].rearrange("p g t -> p (g t)"), ACT.Ln, scale=-1.0)
         nc.scalar.activation(root[:], log_rate[:], ACT.Exp, scale=0.5)
 
-        v2_w = [kept([P, GATHER], U16, "v2_w%d" % c) for c in range(2)]
-        v2_s = [kept([P, GATHER], U8, "v2_s%d" % c) for c in range(2)]
+        v2_w = [kept([P, HALF], U16, "v2_w%d" % c) for c in range(2)]
+        v2_s = [kept([P, HALF], U8, "v2_s%d" % c) for c in range(2)]
         w2_bf = [kept([P, PACK, P, PACK], BF16, "w2_bf%d" % g) for g in range(GROUPS)]
-        w2_q = [kept([P, 512], U32, "w2_q%d" % g) for g in range(GROUPS)]
-        w2_s = [kept([P, 512], U8, "w2_s%d" % g) for g in range(GROUPS)]
-        w4_p = kept([P, 2 * H], U16, "w4_p")
-        w_s = kept([P, 2 * H], U8, "w_s")
-        w8_p = [kept([P, H], U32, "w8_p%d" % a) for a in range(2)]
-        decay = [[kept([P, 2, GATHER, 2], F32, "decay%d%d" % (g, c)) for c in range(2)] for g in range(GROUPS)]
-        a_sb = [[kept([P, 2, n, 2], F32, "a_sb%d%d" % (g, d)) for d, (f, n) in enumerate(SPANS)] for g in range(GROUPS)]
+        w2_q = [kept([P, K_PASS], U32, "w2_q%d" % g) for g in range(GROUPS)]
+        w2_s = [kept([P, K_PASS], U8, "w2_s%d" % g) for g in range(GROUPS)]
+        w4_p = kept([P, PASSES * H], U16, "w4_p")
+        w_s = kept([P, PASSES * H], U8, "w_s")
+        w8_p = [kept([P, H], U32, "w8_p%d" % s) for s in range(PASSES)]
+        decay = [[kept([P, 2, HALF, 2], F32, "decay%d%d" % (g, c)) for c in range(2)] for g in range(GROUPS)]
+        a_sb = [[kept([P, PACK, n], F32, "a_sb%d%d" % (g, d)) for d, (f, n) in enumerate(SPANS)] for g in range(GROUPS)]
         h_q = [[kept([P, n], U32, "h_q%d%d" % (g, d)) for d, (f, n) in enumerate(SPANS)] for g in range(GROUPS)]
         h_s = [[kept([P, n], U8, "h_s%d%d" % (g, d)) for d, (f, n) in enumerate(SPANS)] for g in range(GROUPS)]
         h_bf = {}
         v_w = {}
-        banks = [psum.tile([P, 512], F32, name="bank%d" % i) for i in range(6)]
+        banks = [psum.tile([P, BANK], F32, name="bank%d" % i) for i in range(RING_BANKS)]
         taken = []
 
         def take_bank():
-            taken.append(banks[len(taken) % len(banks)])
+            taken.append(banks[len(taken) % RING_BANKS])
             return taken[-1]
 
-        def gather(dst, window, lst, first, count):
-            nc.vector.tensor_copy(dst[:], window[:].indirect(lst[:, first // 16 : (first + count) // 16]))
+        def gather(dst, window, offsets, first, count):
+            nc.vector.tensor_copy(dst[:], window[:].indirect(offsets[:, first // 16 : (first + count) // 16]))
 
-        def gather_tab_words(d):
-            for a in range(2):
-                v_w[a, d] = kept([P, CHUNK], U32, "v_w%d%d" % (a, d))
-                gather(v_w[a, d], tab_w[a], list1, d * CHUNK, CHUNK)
+        def gather_tab_words(k):
+            for s in range(PASSES):
+                v_w[s, k] = kept([P, CHUNK], U32, "v_w%d%d" % (s, k))
+                gather(v_w[s, k], tab_w[s], list1, k * CHUNK, CHUNK)
 
-        def cast_w2(g, q):
+        m_cols = W2_COLS // PACK
+
+        def round_w2_on_scalar(g, q):
             for u in range(2):
                 nc.scalar.activation(
-                    w2_bf[g][:, 2 * u : 2 * u + 2, 64 * q : 64 * (q + 1), :].rearrange("p e m j -> p m j e"),
-                    w2_raw[g][q][:].rearrange("p j (m t) -> p m j t", t=PACK)[:, :, :, 2 * u : 2 * u + 2],
+                    w2_bf[g][:, 2 * u : 2 * u + 2, m_cols * q : m_cols * (q + 1), :].rearrange("p e m i -> p m i e"),
+                    w2_raw[g][q][:].rearrange("p i (m t) -> p m i t", t=PACK)[:, :, :, 2 * u : 2 * u + 2],
                     ACT.Copy,
                 )
 
-        def cast_w2_on_vector(g, q):
+        def round_w2_on_vector(g, q):
             nc.vector.tensor_copy(
-                out=w2_bf[g][:, :, 64 * q : 64 * (q + 1), :].rearrange("p (u e) m j -> p u m j e", u=2),
-                in_=w2_raw[g][q][:].rearrange("p j (m u e) -> p u m j e", u=2, e=2),
+                out=w2_bf[g][:, :, m_cols * q : m_cols * (q + 1), :].rearrange("p (u e) m i -> p u m i e", u=2),
+                in_=w2_raw[g][q][:].rearrange("p i (m u e) -> p u m i e", u=2, e=2),
             )
 
         def quantize_w2(g):
             nc.vector.quantize_mx(
-                out=w2_q[g][:].bitcast(FP8X4), scales=w2_s[g][:], in_=w2_bf[g][:].rearrange("p t m j -> p (t m j)")
+                out=w2_q[g][:].bitcast(FP8X4), scales=w2_s[g][:], in_=w2_bf[g][:].rearrange("p t m i -> p (t m i)")
             )
 
         def deal_narrow(dst, src):
@@ -169,7 +179,7 @@ def tile_list_mixed_layer_step_kernel(
             )
 
         def make_decay(g, first, count):
-            c, n0 = divmod(first, GATHER)
+            c, n0 = divmod(first, HALF)
             for u in range(2):
                 square = ring.tile([P, 2, count], F32, name="square")
                 for e in range(2):
@@ -191,42 +201,35 @@ def tile_list_mixed_layer_step_kernel(
                     decay[g][c][:, u, n0 : n0 + count, :], square[:].rearrange("p e n -> p n e"), ACT.Exp, scale=-1.0
                 )
 
-        def make_h(g, d, from_psum):
+        def make_h(g, d, product_first):
             first, count = SPANS[d]
-            c, n0 = divmod(first, GATHER)
+            c, n0 = divmod(first, HALF)
             h_bf[g, d] = ring.tile([P, count, PACK], BF16, name="h_bf%d" % g, bufs=2, align_bytes=64)
             for m0 in range(0, count, BLOCK):
                 k, w0 = divmod(first + m0, CHUNK)
                 acc = take_bank()[:].rearrange("p (t n) -> p t n", t=PACK)
                 for t in range(PACK):
-                    for a in range(2):
-                        col = H * a + 512 * g + P * t
+                    for s in range(PASSES):
+                        col = H * s + K_PASS * g + P * t
                         nc.tensor.matmul_mx(
                             out=acc[:, t, :],
                             lhsT=w4_p[:, col : col + P].bitcast(FP4X4),
                             lhsT_scale=w_s[:, col : col + P],
-                            rhs=v_w[a, k][:, w0 : w0 + BLOCK].bitcast(FP8X4),
-                            rhs_scale=v_s[a][:, first + m0 : first + m0 + BLOCK],
-                            start=(a == 0),
-                            stop=(a == 1),
+                            rhs=v_w[s, k][:, w0 : w0 + BLOCK].bitcast(FP8X4),
+                            rhs_scale=v_s[s][:, first + m0 : first + m0 + BLOCK],
+                            start=(s == 0),
+                            stop=(s == PASSES - 1),
                         )
-                if from_psum:
-                    nc.vector.tensor_tensor(
-                        h_bf[g, d][:, m0 : m0 + BLOCK, :].rearrange("p n (u e) -> p n u e", u=2),
-                        acc.rearrange("p (u e) n -> p n u e", u=2),
-                        decay[g][c][:, :, n0 + m0 : n0 + m0 + BLOCK, :].rearrange("p u n e -> p n u e"),
-                        ALU.mult,
-                    )
-                nc.scalar.activation(
-                    a_sb[g][d][:, :, m0 : m0 + BLOCK, :], acc.rearrange("p (u e) n -> p u n e", u=2), ACT.Copy
-                )
-            if not from_psum:
+                if not product_first:
+                    nc.scalar.activation(a_sb[g][d][:, :, m0 : m0 + BLOCK], acc, ACT.Copy)
                 nc.vector.tensor_tensor(
-                    h_bf[g, d][:].rearrange("p n (u e) -> p n u e", u=2),
-                    a_sb[g][d][:].rearrange("p u n e -> p n u e"),
-                    decay[g][c][:, :, n0 : n0 + count, :].rearrange("p u n e -> p n u e"),
+                    h_bf[g, d][:, m0 : m0 + BLOCK, :].rearrange("p n (u e) -> p n u e", u=2),
+                    acc.rearrange("p (u e) n -> p n u e", u=2),
+                    decay[g][c][:, :, n0 + m0 : n0 + m0 + BLOCK, :].rearrange("p u n e -> p n u e"),
                     ALU.mult,
                 )
+                if product_first:
+                    nc.scalar.activation(a_sb[g][d][:, :, m0 : m0 + BLOCK], acc, ACT.Copy)
 
         def quantize_h(g, d):
             nc.vector.quantize_mx(
@@ -235,56 +238,58 @@ def tile_list_mixed_layer_step_kernel(
 
         out_rows = out.rearrange("(g p t) j -> g p t j", g=GROUPS, t=PACK)
 
-        def mix(d):
+        def finish(d):
             first, count = SPANS[d]
-            per_bank = 512 // count
+            per_bank = BANK // count
             for g in range(GROUPS):
                 for t0 in range(0, PACK, per_bank):
                     result = ring.tile([P, per_bank, count], F32, name="result", bufs=6)
                     y = psum.tile([P, per_bank, count], F32, name="y", bufs=2)
                     for i in range(per_bank):
-                        col = 512 * g + P * (t0 + i)
-                        for a in range(2):
+                        col = K_PASS * g + P * (t0 + i)
+                        for s in range(PASSES):
                             nc.tensor.matmul_mx(
                                 out=y[:, i, :],
-                                lhsT=w8_p[a][:, col : col + P].bitcast(FP8X4),
-                                lhsT_scale=w_s[4 + 4 * a : P, col : col + P],
-                                rhs=h_q[a][d][:].bitcast(FP8X4),
-                                rhs_scale=h_s[a][d][:],
-                                start=(a == 0),
-                                stop=(a == 1),
+                                lhsT=w8_p[s][:, col : col + P].bitcast(FP8X4),
+                                lhsT_scale=w_s[4 + 4 * s : P, col : col + P],
+                                rhs=h_q[s][d][:].bitcast(FP8X4),
+                                rhs_scale=h_s[s][d][:],
+                                start=(s == 0),
+                                stop=(s == PASSES - 1),
                             )
                     for i in range(per_bank):
                         t = t0 + i
                         nc.vector.scalar_tensor_tensor(
-                            result[:, i, :], a_sb[g][d][:, t // 2, :, t % 2], step_sb[:, g, t : t + 1], y[:, i, :],
+                            result[:, i, :], a_sb[g][d][:, t, :], step_sb[:, g, t : t + 1], y[:, i, :],
                             ALU.mult, ALU.add,
                         )
                     nc.sync.dma_start(out=out_rows[g][:, t0 : t0 + per_bank, first : first + count], in_=result[:])
 
         for c in range(2):
-            gather(v2_w[c], tab2_w, list2, c * GATHER, GATHER)
+            gather(v2_w[c], tab2_w, list2, c * HALF, HALF)
         for c in range(2):
-            gather(v2_s[c], tab2_s, list2, c * GATHER, GATHER)
-        cast_w2(0, 0)
-        cast_w2(0, 1)
+            gather(v2_s[c], tab2_s, list2, c * HALF, HALF)
+        round_w2_on_scalar(0, 0)
+        round_w2_on_scalar(0, 1)
         quantize_w2(0)
-        cast_w2(1, 0)
-        deal_narrow(w_s[:], ws_raw[:])
-        gather(v_s[0], tab_s, list1, 0, S)
-        for q in range(4):
-            nc.scalar.dma_start(
-                out=v_s[1][32 * q : 32 * q + 4, :].bitcast(I32), in_=v_s[0][32 * q + 4 : 32 * q + 8, :].bitcast(I32)
-            )
-        cast_w2_on_vector(1, 1)
-        make_decay(0, 0, GATHER)
+        round_w2_on_scalar(1, 0)
+        round_w2_on_vector(1, 1)
+        make_decay(0, 0, HALF)
         quantize_w2(1)
+
+        gather(v_s[0], tab_s, list1, 0, S)
+        for z in range(QUADS):
+            nc.scalar.dma_start(
+                out=v_s[1][32 * z : 32 * z + 4, :].bitcast(I32), in_=v_s[0][32 * z + 4 : 32 * z + 8, :].bitcast(I32)
+            )
+        deal_narrow(w_s[:], ws_raw[:])
         deal_narrow(w4_p[:], w4_raw[:])
         for k in range(S // CHUNK):
             gather_tab_words(k)
-        make_decay(1, 0, GATHER)
-        for a in range(2):
-            deal_words(w8_p[a][:].bitcast(I32), w8_raw[a][:].bitcast(I32))
+        make_decay(1, 0, HALF)
+        for s in range(PASSES):
+            deal_words(w8_p[s][:].bitcast(I32), w8_raw[s][:].bitcast(I32))
+
         last = len(SPANS) - 1
         make_h(1, 0, False)
         make_h(0, 0, False)
@@ -294,7 +299,7 @@ def tile_list_mixed_layer_step_kernel(
             if d < last:
                 first = SPANS[d + 1][0]
                 for g in (1, 0):
-                    if first >= GATHER and first % CHUNK == 0:
+                    if first >= HALF and first % CHUNK == 0:
                         make_decay(g, first, CHUNK)
                     make_h(g, d + 1, d + 1 == last)
-            mix(d)
+            finish(d)

@@ -23,12 +23,13 @@ PASSES = K // K_PASS
 GROUPS = H // K_PASS
 QUADS = 4
 BANK = 512
+BANKS = 8
 HALF = S // 2
 CHUNK = 256
 BLOCK = BANK // PACK
 W2_COLS = 256
+W2_BYTES = 2 * PACK * K_PASS
 SPANS = ((0, 256), (256, 256), (512, 256), (768, 128), (896, 128))
-RING_BANKS = 6
 
 
 def tile_list_mixed_layer_step_kernel(
@@ -38,29 +39,35 @@ def tile_list_mixed_layer_step_kernel(
     nc = tc.nc
     with ExitStack() as ctx:
         keep = ctx.enter_context(tc.tile_pool(name="keep", bufs=1))
+        reuse = ctx.enter_context(tc.tile_pool(name="reuse", bufs=1))
         ring = ctx.enter_context(tc.tile_pool(name="ring", bufs=3))
         psum = ctx.enter_context(tc.psum_pool(name="psum", bufs=1))
 
         def kept(shape, dtype, name):
             return keep.tile(shape, dtype, name=name, align_bytes=64)
 
+        def placed(shape, dtype, name, offset):
+            return reuse.tile(shape, dtype, name=name, align_bytes=64, offset=offset)
+
         list1 = kept([P, S // 16], U16, "list1")
         list2 = kept([P, S // 16], U16, "list2")
         tab2_w = kept([P, T], U16, "tab2_w")
         tab2_s = kept([P, T], U8, "tab2_s")
         tab_w = [kept([P, T], U32, "tab_w%d" % s) for s in range(PASSES)]
-        tab_s = kept([P, T], U8, "tab_s")
+        tab_s = placed([P, T], U8, "tab_s", 3 * W2_BYTES)
         w2_raw = [[kept([P, PACK, W2_COLS], F32, "w2_raw%d%d" % (g, q)) for q in range(2)] for g in range(GROUPS)]
-        w4_raw = kept([P, PASSES * H], U16, "w4_raw")
-        ws_raw = kept([P, PASSES * H], U8, "ws_raw")
+        w4_raw = [
+            placed([P, PASSES * K_PASS], U16, "w4_raw0", 2 * W2_BYTES), kept([P, PASSES * K_PASS], U16, "w4_raw1")
+        ]
+        w4s_raw = kept([P, PASSES * H], U8, "w4s_raw")
+        w8s_raw = kept([P, H], U8, "w8s_raw")
         w8_raw = [kept([P, H], U32, "w8_raw%d" % s) for s in range(PASSES)]
         rate_sb = kept([P, GROUPS, PACK], F32, "rate_sb")
         step_sb = kept([P, GROUPS, PACK], F32, "step_sb")
-        v_s = [kept([P, S], U8, "v_s%d" % s) for s in range(PASSES)]
+        v_s1 = kept([P, S], U8, "v_s1")
 
-        for plane in (tab2_s, ws_raw, v_s[1]):
+        for plane in (tab2_s, tab_s, w4s_raw, w8s_raw, v_s1):
             nc.vector.memset(plane[:].bitcast(I32), 0)
-        nc.gpsimd.memset(tab_s[:].bitcast(I32), 0)
 
         def load_words(tile, src):
             nc.sync.dma_start(out=tile[:].bitcast(I32), in_=src.bitcast(I32))
@@ -71,79 +78,78 @@ def tile_list_mixed_layer_step_kernel(
                 out=w2_raw[g][q][:], in_=w2.rearrange("(p i) c -> p i c", i=PACK)[:, :, c0 : c0 + W2_COLS]
             )
 
-        nc.sync.dma_start(list2[:], offs2)
-        for q in range(2):
+        def load_w4(g):
+            half = K_PASS // 2
             nc.sync.dma_start(
-                out=tab2_w[:, q * T // 2 : (q + 1) * T // 2].bitcast(I32),
-                in_=tab2_words[0, :, q * T : (q + 1) * T].bitcast(I32),
+                out=w4_raw[g][:].bitcast(I32).rearrange("p (s c) -> p s c", s=PASSES),
+                in_=w4_words.bitcast(I32).rearrange("s p c -> p s c")[:, :, half * g : half * (g + 1)],
             )
+
+        def load_two_planes(queue, tile, src):
+            for z in range(QUADS):
+                queue.dma_start(
+                    out=tile[32 * z : 32 * z + 8, :].bitcast(I32), in_=src[:, 4 * z : 4 * z + 4, :].bitcast(I32)
+                )
+
         nc.sync.dma_start(out=rate_sb[:], in_=rate.rearrange("(g p t) -> p g t", g=GROUPS, t=PACK))
+        nc.sync.dma_start(list2[:], offs2)
+        for r in range(4):
+            nc.sync.dma_start(out=tab2_s[r:P:32, :].bitcast(I32), in_=tab2_scales[0, r:16:4, :].bitcast(I32))
         load_w2(0, 0)
-        for z in range(QUADS):
-            nc.sync.dma_start(
-                out=tab2_s[32 * z : 32 * z + 4, :].bitcast(I32), in_=tab2_scales[0, 4 * z : 4 * z + 4, :].bitcast(I32)
-            )
         load_w2(0, 1)
+        load_words(tab2_w, tab2_words[0])
         nc.sync.dma_start(list1[:], offs)
+        load_two_planes(nc.gpsimd, tab_s, tab_scales)
+        for r in range(4):
+            nc.gpsimd.dma_start(
+                out=w4s_raw[r:P:32, :].bitcast(I32).rearrange("z (s c) -> z s c", s=PASSES),
+                in_=w4_scales[:, r:16:4, :].bitcast(I32).rearrange("s z c -> z s c"),
+            )
+        load_two_planes(nc.gpsimd, w8s_raw, w8_scales)
         load_w2(1, 0)
         load_w2(1, 1)
-        for z in range(QUADS):
-            nc.sync.dma_start(
-                out=ws_raw[32 * z + 4 : 32 * z + 12, 0:H].bitcast(I32),
-                in_=w8_scales[:, 4 * z : 4 * z + 4, :].bitcast(I32),
-            )
-        for z in range(QUADS):
-            nc.sync.dma_start(
-                out=tab_s[32 * z : 32 * z + 8, :].bitcast(I32), in_=tab_scales[:, 4 * z : 4 * z + 4, :].bitcast(I32)
-            )
-        for z in range(QUADS):
-            nc.sync.dma_start(
-                out=ws_raw[32 * z : 32 * z + 4, :].bitcast(I32).rearrange("r (s c) -> r s c", s=PASSES),
-                in_=w4_scales[:, 4 * z : 4 * z + 4, :].bitcast(I32).rearrange("s r c -> r s c"),
-            )
-        nc.sync.dma_start(
-            out=w4_raw[:].bitcast(I32).rearrange("p (s c) -> p s c", s=PASSES),
-            in_=w4_words.bitcast(I32).rearrange("s p c -> p s c"),
-        )
-        for s in range(PASSES):
-            load_words(tab_w[s], tab_words[s].rearrange("p c i -> p (c i)"))
-        for s in range(PASSES):
-            load_words(w8_raw[s], w8_words[s].rearrange("p c i -> p (c i)"))
-        nc.sync.dma_start(out=step_sb[:], in_=step.rearrange("(g p t) -> p g t", g=GROUPS, t=PACK))
+        load_words(tab_w[0], tab_words[0].rearrange("p c i -> p (c i)"))
+        load_w4(0)
 
         log_rate = kept([P, GROUPS * PACK], F32, "log_rate")
         root = kept([P, GROUPS * PACK], F32, "root")
         nc.scalar.activation(log_rate[:], rate_sb[:].rearrange("p g t -> p (g t)"), ACT.Ln, scale=-1.0)
         nc.scalar.activation(root[:], log_rate[:], ACT.Exp, scale=0.5)
 
-        v2_w = [kept([P, HALF], U16, "v2_w%d" % c) for c in range(2)]
-        v2_s = [kept([P, HALF], U8, "v2_s%d" % c) for c in range(2)]
-        w2_bf = [kept([P, PACK, P, PACK], BF16, "w2_bf%d" % g) for g in range(GROUPS)]
+        w2_bf = [placed([P, PACK, P, PACK], BF16, "w2_bf%d" % g, W2_BYTES * g) for g in range(GROUPS)]
         w2_q = [kept([P, K_PASS], U32, "w2_q%d" % g) for g in range(GROUPS)]
         w2_s = [kept([P, K_PASS], U8, "w2_s%d" % g) for g in range(GROUPS)]
-        w4_p = kept([P, PASSES * H], U16, "w4_p")
-        w_s = kept([P, PASSES * H], U8, "w_s")
-        w8_p = [kept([P, H], U32, "w8_p%d" % s) for s in range(PASSES)]
+        w4_s = [
+            [placed([P, K_PASS], U8, "w4_s%d%d" % (g, s), S + K_PASS * (PASSES * g + s)) for s in range(PASSES)]
+            for g in range(GROUPS)
+        ]
+        w4_p = [
+            [placed([P, K_PASS], U16, "w4_p0%d" % s, W2_BYTES + 2 * K_PASS * s) for s in range(PASSES)],
+            [kept([P, K_PASS], U16, "w4_p1%d" % s) for s in range(PASSES)],
+        ]
+        w8_s = [placed([P, K_PASS], U8, "w8_s%d" % g, 2 * W2_BYTES + 2 * K_PASS + K_PASS * g) for g in range(GROUPS)]
+        w8_p = [[kept([P, K_PASS], U32, "w8_p%d%d" % (s, g)) for g in range(GROUPS)] for s in range(PASSES)]
         decay = [[kept([P, 2, HALF, 2], F32, "decay%d%d" % (g, c)) for c in range(2)] for g in range(GROUPS)]
         a_sb = [[kept([P, PACK, n], F32, "a_sb%d%d" % (g, d)) for d, (f, n) in enumerate(SPANS)] for g in range(GROUPS)]
         h_q = [[kept([P, n], U32, "h_q%d%d" % (g, d)) for d, (f, n) in enumerate(SPANS)] for g in range(GROUPS)]
         h_s = [[kept([P, n], U8, "h_s%d%d" % (g, d)) for d, (f, n) in enumerate(SPANS)] for g in range(GROUPS)]
         h_bf = {}
         v_w = {}
-        banks = [psum.tile([P, BANK], F32, name="bank%d" % i) for i in range(RING_BANKS)]
+        v2_w = {}
+        v2_s = {}
+        banks = [psum.tile([P, BANK], F32, name="bank%d" % i) for i in range(BANKS)]
         taken = []
 
         def take_bank():
-            taken.append(banks[len(taken) % RING_BANKS])
+            taken.append(banks[len(taken) % BANKS])
             return taken[-1]
 
         def gather(dst, window, offsets, first, count):
             nc.vector.tensor_copy(dst[:], window[:].indirect(offsets[:, first // 16 : (first + count) // 16]))
 
-        def gather_tab_words(k):
-            for s in range(PASSES):
-                v_w[s, k] = kept([P, CHUNK], U32, "v_w%d%d" % (s, k))
-                gather(v_w[s, k], tab_w[s], list1, k * CHUNK, CHUNK)
+        def gather_tab_words(s, k):
+            v_w[s, k] = kept([P, CHUNK], U32, "v_w%d%d" % (s, k))
+            gather(v_w[s, k], tab_w[s], list1, k * CHUNK, CHUNK)
 
         m_cols = W2_COLS // PACK
 
@@ -166,36 +172,41 @@ def tile_list_mixed_layer_step_kernel(
                 out=w2_q[g][:].bitcast(FP8X4), scales=w2_s[g][:], in_=w2_bf[g][:].rearrange("p t m i -> p (t m i)")
             )
 
-        def deal_narrow(dst, src):
-            nc.vector.tensor_copy(
-                out=dst.rearrange("p (g t m) -> p g t m", t=PACK, m=P),
-                in_=src.rearrange("p (g m t) -> p g t m", t=PACK, m=P),
+        def deal(dst, src):
+            nc.gpsimd.tensor_copy(
+                out=dst.rearrange("p (t m) -> p t m", t=PACK), in_=src.rearrange("p (m t) -> p t m", t=PACK)
             )
 
-        def deal_words(dst, src):
-            nc.vector.tensor_copy(
-                out=dst.rearrange("p (g u e m) -> p g u m e", u=2, e=2, m=P),
-                in_=src.rearrange("p (g m u e) -> p g u m e", u=2, e=2, m=P),
-            )
+        def deal_w8(g):
+            for s in range(PASSES):
+                nc.vector.tensor_copy(
+                    out=w8_p[s][g][:].bitcast(I32).rearrange("p (u e m) -> p u m e", u=2, e=2),
+                    in_=w8_raw[s][:, K_PASS * g : K_PASS * (g + 1)].bitcast(I32).rearrange("p (m u e) -> p u m e", u=2, e=2),
+                )
 
         def make_decay(g, first, count):
             c, n0 = divmod(first, HALF)
+            per_bank = BANK // count
             for u in range(2):
                 square = ring.tile([P, 2, count], F32, name="square")
+                b = []
                 for e in range(2):
-                    t = 2 * u + e
-                    b = take_bank()[:, 0:count]
+                    if e % per_bank == 0:
+                        bank = take_bank()
+                    b.append(bank[:, count * (e % per_bank) : count * (e % per_bank + 1)])
                     nc.tensor.matmul_mx(
-                        out=b,
-                        lhsT=w2_q[g][:, P * t : P * (t + 1)].bitcast(FP8X4),
-                        lhsT_scale=w2_s[g][:, P * t : P * (t + 1)],
+                        out=b[e],
+                        lhsT=w2_q[g][:, P * (2 * u + e) : P * (2 * u + e + 1)].bitcast(FP8X4),
+                        lhsT_scale=w2_s[g][:, P * (2 * u + e) : P * (2 * u + e + 1)],
                         rhs=v2_w[c][:, n0 : n0 + count].bitcast(FP4X4),
                         rhs_scale=v2_s[c][:, n0 : n0 + count],
                         start=True,
                         stop=True,
                     )
+                for e in range(2):
+                    t = 2 * u + e
                     nc.scalar.activation(
-                        square[:, e, :], b, ACT.Square, scale=root[:, PACK * g + t : PACK * g + t + 1]
+                        square[:, e, :], b[e], ACT.Square, scale=root[:, PACK * g + t : PACK * g + t + 1]
                     )
                 nc.scalar.activation(
                     decay[g][c][:, u, n0 : n0 + count, :], square[:].rearrange("p e n -> p n e"), ACT.Exp, scale=-1.0
@@ -208,17 +219,17 @@ def tile_list_mixed_layer_step_kernel(
             for m0 in range(0, count, BLOCK):
                 k, w0 = divmod(first + m0, CHUNK)
                 acc = take_bank()[:].rearrange("p (t n) -> p t n", t=PACK)
-                for t in range(PACK):
-                    for s in range(PASSES):
-                        col = H * s + K_PASS * g + P * t
+                for s in range(PASSES):
+                    for t in range(PACK):
+                        col = P * t
                         nc.tensor.matmul_mx(
                             out=acc[:, t, :],
-                            lhsT=w4_p[:, col : col + P].bitcast(FP4X4),
-                            lhsT_scale=w_s[:, col : col + P],
+                            lhsT=w4_p[g][s][:, col : col + P].bitcast(FP4X4),
+                            lhsT_scale=w4_s[g][s][:, col : col + P],
                             rhs=v_w[s, k][:, w0 : w0 + BLOCK].bitcast(FP8X4),
                             rhs_scale=v_s[s][:, first + m0 : first + m0 + BLOCK],
-                            start=(s == 0),
-                            stop=(s == PASSES - 1),
+                            start=(s == 0 and t == 0),
+                            stop=(s == PASSES - 1 and t == PACK - 1),
                         )
                 if not product_first:
                     nc.scalar.activation(a_sb[g][d][:, :, m0 : m0 + BLOCK], acc, ACT.Copy)
@@ -238,68 +249,105 @@ def tile_list_mixed_layer_step_kernel(
 
         out_rows = out.rearrange("(g p t) j -> g p t j", g=GROUPS, t=PACK)
 
-        def finish(d):
+        def finish(d, g):
             first, count = SPANS[d]
             per_bank = BANK // count
-            for g in range(GROUPS):
-                for t0 in range(0, PACK, per_bank):
-                    result = ring.tile([P, per_bank, count], F32, name="result", bufs=6)
-                    y = psum.tile([P, per_bank, count], F32, name="y", bufs=2)
-                    for i in range(per_bank):
-                        col = K_PASS * g + P * (t0 + i)
-                        for s in range(PASSES):
-                            nc.tensor.matmul_mx(
-                                out=y[:, i, :],
-                                lhsT=w8_p[s][:, col : col + P].bitcast(FP8X4),
-                                lhsT_scale=w_s[4 + 4 * s : P, col : col + P],
-                                rhs=h_q[s][d][:].bitcast(FP8X4),
-                                rhs_scale=h_s[s][d][:],
-                                start=(s == 0),
-                                stop=(s == PASSES - 1),
-                            )
-                    for i in range(per_bank):
-                        t = t0 + i
-                        nc.vector.scalar_tensor_tensor(
-                            result[:, i, :], a_sb[g][d][:, t, :], step_sb[:, g, t : t + 1], y[:, i, :],
-                            ALU.mult, ALU.add,
+            for t0 in range(0, PACK, per_bank):
+                result = ring.tile([P, per_bank, count], F32, name="result", bufs=6)
+                y = take_bank()[:].rearrange("p (i n) -> p i n", i=per_bank)
+                for i in range(per_bank):
+                    col = P * (t0 + i)
+                    for s in range(PASSES):
+                        nc.tensor.matmul_mx(
+                            out=y[:, i, :],
+                            lhsT=w8_p[s][g][:, col : col + P].bitcast(FP8X4),
+                            lhsT_scale=w8_s[g][4 * s : P, col : col + P],
+                            rhs=h_q[s][d][:].bitcast(FP8X4),
+                            rhs_scale=h_s[s][d][:],
+                            start=(s == 0),
+                            stop=(s == PASSES - 1),
                         )
-                    nc.sync.dma_start(out=out_rows[g][:, t0 : t0 + per_bank, first : first + count], in_=result[:])
+                for i in range(per_bank):
+                    t = t0 + i
+                    nc.vector.scalar_tensor_tensor(
+                        result[:, i, :], a_sb[g][d][:, t, :], step_sb[:, g, t : t + 1], y[:, i, :],
+                        ALU.mult, ALU.add,
+                    )
+                nc.sync.dma_start(out=out_rows[g][:, t0 : t0 + per_bank, first : first + count], in_=result[:])
 
-        for c in range(2):
-            gather(v2_w[c], tab2_w, list2, c * HALF, HALF)
-        for c in range(2):
-            gather(v2_s[c], tab2_s, list2, c * HALF, HALF)
+        v2_s[0] = kept([P, HALF], U8, "v2_s0")
+        v2_w[0] = kept([P, HALF], U16, "v2_w0")
+        v2_s[1] = kept([P, HALF], U8, "v2_s1")
+        gather(v2_s[0], tab2_s, list2, 0, HALF)
+        gather(v2_s[1], tab2_s, list2, HALF, HALF)
         round_w2_on_scalar(0, 0)
-        round_w2_on_scalar(0, 1)
+        round_w2_on_vector(0, 1)
         quantize_w2(0)
+        gather(v2_w[0], tab2_w, list2, 0, HALF)
         round_w2_on_scalar(1, 0)
-        round_w2_on_vector(1, 1)
         make_decay(0, 0, HALF)
+        v_s0 = placed([P, S], U8, "v_s0", 0)
+        v_s = [v_s0, v_s1]
+        gather(v_s0, tab_s, list1, 0, S)
+        round_w2_on_vector(1, 1)
         quantize_w2(1)
-
-        gather(v_s[0], tab_s, list1, 0, S)
-        for z in range(QUADS):
-            nc.scalar.dma_start(
-                out=v_s[1][32 * z : 32 * z + 4, :].bitcast(I32), in_=v_s[0][32 * z + 4 : 32 * z + 8, :].bitcast(I32)
-            )
-        deal_narrow(w_s[:], ws_raw[:])
-        deal_narrow(w4_p[:], w4_raw[:])
-        for k in range(S // CHUNK):
-            gather_tab_words(k)
         make_decay(1, 0, HALF)
-        for s in range(PASSES):
-            deal_words(w8_p[s][:].bitcast(I32), w8_raw[s][:].bitcast(I32))
 
-        last = len(SPANS) - 1
-        make_h(1, 0, False)
-        make_h(0, 0, False)
-        for d in range(len(SPANS)):
-            quantize_h(0, d)
-            quantize_h(1, d)
-            if d < last:
-                first = SPANS[d + 1][0]
-                for g in (1, 0):
-                    if first >= HALF and first % CHUNK == 0:
-                        make_decay(g, first, CHUNK)
-                    make_h(g, d + 1, d + 1 == last)
-            finish(d)
+        for z in range(QUADS):
+            nc.sync.dma_start(
+                out=v_s1[z:P:32, :].bitcast(I32), in_=v_s0[4 + z : P : 32, :].bitcast(I32)
+            )
+        load_words(tab_w[1], tab_words[1].rearrange("p c i -> p (c i)"))
+        load_w4(1)
+        for s in range(PASSES):
+            load_words(w8_raw[s], w8_words[s].rearrange("p c i -> p (c i)"))
+        nc.sync.dma_start(out=step_sb[:], in_=step.rearrange("(g p t) -> p g t", g=GROUPS, t=PACK))
+        for g in range(GROUPS):
+            for s in range(PASSES):
+                deal(w4_s[g][s][:], w4s_raw[:, H * s + K_PASS * g : H * s + K_PASS * (g + 1)])
+        for g in range(GROUPS):
+            for s in range(PASSES):
+                deal(w4_p[g][s][:], w4_raw[g][:, K_PASS * s : K_PASS * (s + 1)])
+        for g in range(GROUPS):
+            deal(w8_s[g][:], w8s_raw[:, K_PASS * g : K_PASS * (g + 1)])
+        v2_w[1] = placed([P, HALF], U16, "v2_w1", 3 * W2_BYTES)
+        gather(v2_w[1], tab2_w, list2, HALF, HALF)
+        for s in range(PASSES):
+            for k in range(S // CHUNK):
+                gather_tab_words(s, k)
+
+        make_h(0, 0, True)
+        make_h(0, 1, True)
+        quantize_h(0, 0)
+        make_h(1, 0, True)
+        deal_w8(0)
+        quantize_h(0, 1)
+        make_h(1, 1, True)
+        quantize_h(1, 0)
+        make_decay(0, 512, CHUNK)
+        deal_w8(1)
+        quantize_h(1, 1)
+        finish(0, 0)
+        make_decay(1, 512, CHUNK)
+        finish(0, 1)
+        make_h(0, 2, True)
+        finish(1, 0)
+        make_decay(0, 768, CHUNK)
+        quantize_h(0, 2)
+        make_h(1, 2, True)
+        finish(1, 1)
+        make_decay(1, 768, CHUNK)
+        quantize_h(1, 2)
+        make_h(0, 3, True)
+        finish(2, 0)
+        make_h(0, 4, True)
+        quantize_h(0, 3)
+        make_h(1, 3, True)
+        quantize_h(0, 4)
+        make_h(1, 4, True)
+        quantize_h(1, 3)
+        finish(2, 1)
+        quantize_h(1, 4)
+        for d in (3, 4):
+            for g in range(GROUPS):
+                finish(d, g)

@@ -24,12 +24,13 @@ GROUPS = H // K_PASS
 QUADS = 4
 BANK = 512
 BANKS = 8
+H_BUFS = 2
 HALF = S // 2
 CHUNK = 256
 BLOCK = BANK // PACK
 W2_COLS = 256
 W2_BYTES = 2 * PACK * K_PASS
-SPANS = ((0, 256), (256, 256), (512, 256), (768, 128), (896, 128))
+SPANS = ((0, 512), (512, 256), (768, 128), (896, 128))
 
 
 def tile_list_mixed_layer_step_kernel(
@@ -105,7 +106,6 @@ def tile_list_mixed_layer_step_kernel(
                 out=w4s_raw[r:P:32, :].bitcast(I32).rearrange("z (s c) -> z s c", s=PASSES),
                 in_=w4_scales[:, r:16:4, :].bitcast(I32).rearrange("s z c -> z s c"),
             )
-        load_two_planes(nc.gpsimd, w8s_raw, w8_scales)
         load_w2(1, 0)
         load_w2(1, 1)
         load_words(tab_w[0], tab_words[0].rearrange("p c i -> p (c i)"))
@@ -120,23 +120,22 @@ def tile_list_mixed_layer_step_kernel(
         w2_q = [kept([P, K_PASS], U32, "w2_q%d" % g) for g in range(GROUPS)]
         w2_s = [kept([P, K_PASS], U8, "w2_s%d" % g) for g in range(GROUPS)]
         w4_s = [
-            [placed([P, K_PASS], U8, "w4_s%d%d" % (g, s), S + K_PASS * (PASSES * g + s)) for s in range(PASSES)]
+            [placed([P, K_PASS], U8, "w4_s%d%d" % (g, s), W2_BYTES + 4 * K_PASS + K_PASS * (PASSES * g + s)) for s in range(PASSES)]
             for g in range(GROUPS)
         ]
         w4_p = [
             [placed([P, K_PASS], U16, "w4_p0%d" % s, W2_BYTES + 2 * K_PASS * s) for s in range(PASSES)],
             [kept([P, K_PASS], U16, "w4_p1%d" % s) for s in range(PASSES)],
         ]
-        w8_s = [placed([P, K_PASS], U8, "w8_s%d" % g, 2 * W2_BYTES + 2 * K_PASS + K_PASS * g) for g in range(GROUPS)]
-        w8_p = [[kept([P, K_PASS], U32, "w8_p%d%d" % (s, g)) for g in range(GROUPS)] for s in range(PASSES)]
+        w8_s = [kept([P, K_PASS], U8, "w8_s%d" % g) for g in range(GROUPS)]
+        w8_p = [kept([P, H], U32, "w8_p%d" % s) for s in range(PASSES)]
         decay = [[kept([P, 2, HALF, 2], F32, "decay%d%d" % (g, c)) for c in range(2)] for g in range(GROUPS)]
         a_sb = [[kept([P, PACK, n], F32, "a_sb%d%d" % (g, d)) for d, (f, n) in enumerate(SPANS)] for g in range(GROUPS)]
-        h_q = [[kept([P, n], U32, "h_q%d%d" % (g, d)) for d, (f, n) in enumerate(SPANS)] for g in range(GROUPS)]
-        h_s = [[kept([P, n], U8, "h_s%d%d" % (g, d)) for d, (f, n) in enumerate(SPANS)] for g in range(GROUPS)]
+        h_q = [kept([P, GROUPS * n], U32, "h_q%d" % d) for d, (f, n) in enumerate(SPANS)]
+        h_s = [kept([P, GROUPS * n], U8, "h_s%d" % d) for d, (f, n) in enumerate(SPANS)]
         h_bf = {}
         v_w = {}
         v2_w = {}
-        v2_s = {}
         banks = [psum.tile([P, BANK], F32, name="bank%d" % i) for i in range(BANKS)]
         taken = []
 
@@ -147,9 +146,11 @@ def tile_list_mixed_layer_step_kernel(
         def gather(dst, window, offsets, first, count):
             nc.vector.tensor_copy(dst[:], window[:].indirect(offsets[:, first // 16 : (first + count) // 16]))
 
-        def gather_tab_words(s, k):
-            v_w[s, k] = kept([P, CHUNK], U32, "v_w%d%d" % (s, k))
-            gather(v_w[s, k], tab_w[s], list1, k * CHUNK, CHUNK)
+        def gather_tab_words(s, first, count):
+            words = placed([P, count], U32, "v_w%d_%d" % (s, first), 4 * W2_BYTES + 4 * (first if s == 0 else S + first % HALF))
+            gather(words, tab_w[s], list1, first, count)
+            for m0 in range(0, count, BLOCK):
+                v_w[s, first + m0] = words[:, m0 : m0 + BLOCK]
 
         m_cols = W2_COLS // PACK
 
@@ -167,6 +168,12 @@ def tile_list_mixed_layer_step_kernel(
                 in_=w2_raw[g][q][:].rearrange("p i (m u e) -> p u m i e", u=2, e=2),
             )
 
+        def round_w2_on_gpsimd(g, q):
+            nc.gpsimd.tensor_copy(
+                out=w2_bf[g][:, :, m_cols * q : m_cols * (q + 1), :],
+                in_=w2_raw[g][q][:].rearrange("p i (m t) -> p t m i", t=PACK),
+            )
+
         def quantize_w2(g):
             nc.vector.quantize_mx(
                 out=w2_q[g][:].bitcast(FP8X4), scales=w2_s[g][:], in_=w2_bf[g][:].rearrange("p t m i -> p (t m i)")
@@ -177,12 +184,11 @@ def tile_list_mixed_layer_step_kernel(
                 out=dst.rearrange("p (t m) -> p t m", t=PACK), in_=src.rearrange("p (m t) -> p t m", t=PACK)
             )
 
-        def deal_w8(g):
-            for s in range(PASSES):
-                nc.vector.tensor_copy(
-                    out=w8_p[s][g][:].bitcast(I32).rearrange("p (u e m) -> p u m e", u=2, e=2),
-                    in_=w8_raw[s][:, K_PASS * g : K_PASS * (g + 1)].bitcast(I32).rearrange("p (m u e) -> p u m e", u=2, e=2),
-                )
+        def deal_w8(s):
+            nc.vector.tensor_copy(
+                out=w8_p[s][:].bitcast(I32).rearrange("p (g u e m) -> p g u m e", u=2, e=2, m=P),
+                in_=w8_raw[s][:].bitcast(I32).rearrange("p (g m u e) -> p g u m e", u=2, e=2, m=P),
+            )
 
         def make_decay(g, first, count):
             c, n0 = divmod(first, HALF)
@@ -199,7 +205,7 @@ def tile_list_mixed_layer_step_kernel(
                         lhsT=w2_q[g][:, P * (2 * u + e) : P * (2 * u + e + 1)].bitcast(FP8X4),
                         lhsT_scale=w2_s[g][:, P * (2 * u + e) : P * (2 * u + e + 1)],
                         rhs=v2_w[c][:, n0 : n0 + count].bitcast(FP4X4),
-                        rhs_scale=v2_s[c][:, n0 : n0 + count],
+                        rhs_scale=v2_s[:, first : first + count],
                         start=True,
                         stop=True,
                     )
@@ -212,39 +218,41 @@ def tile_list_mixed_layer_step_kernel(
                     decay[g][c][:, u, n0 : n0 + count, :], square[:].rearrange("p e n -> p n e"), ACT.Exp, scale=-1.0
                 )
 
-        def make_h(g, d, product_first):
+        def make_h(g, d, m0, engine):
             first, count = SPANS[d]
-            c, n0 = divmod(first, HALF)
-            h_bf[g, d] = ring.tile([P, count, PACK], BF16, name="h_bf%d" % g, bufs=2, align_bytes=64)
-            for m0 in range(0, count, BLOCK):
-                k, w0 = divmod(first + m0, CHUNK)
-                acc = take_bank()[:].rearrange("p (t n) -> p t n", t=PACK)
-                for s in range(PASSES):
-                    for t in range(PACK):
-                        col = P * t
-                        nc.tensor.matmul_mx(
-                            out=acc[:, t, :],
-                            lhsT=w4_p[g][s][:, col : col + P].bitcast(FP4X4),
-                            lhsT_scale=w4_s[g][s][:, col : col + P],
-                            rhs=v_w[s, k][:, w0 : w0 + BLOCK].bitcast(FP8X4),
-                            rhs_scale=v_s[s][:, first + m0 : first + m0 + BLOCK],
-                            start=(s == 0 and t == 0),
-                            stop=(s == PASSES - 1 and t == PACK - 1),
-                        )
-                if not product_first:
-                    nc.scalar.activation(a_sb[g][d][:, :, m0 : m0 + BLOCK], acc, ACT.Copy)
-                nc.vector.tensor_tensor(
-                    h_bf[g, d][:, m0 : m0 + BLOCK, :].rearrange("p n (u e) -> p n u e", u=2),
-                    acc.rearrange("p (u e) n -> p n u e", u=2),
-                    decay[g][c][:, :, n0 + m0 : n0 + m0 + BLOCK, :].rearrange("p u n e -> p n u e"),
-                    ALU.mult,
-                )
-                if product_first:
-                    nc.scalar.activation(a_sb[g][d][:, :, m0 : m0 + BLOCK], acc, ACT.Copy)
+            c, n0 = divmod(first + m0, HALF)
+            if d not in h_bf:
+                h_bf[d] = ring.tile([P, GROUPS, count, PACK], BF16, name="h_bf", bufs=H_BUFS, align_bytes=64)
+            acc = take_bank()[:].rearrange("p (t n) -> p t n", t=PACK)
+            for s in range(PASSES):
+                for t in range(PACK):
+                    nc.tensor.matmul_mx(
+                        out=acc[:, t, :],
+                        lhsT=w4_p[g][s][:, P * t : P * (t + 1)].bitcast(FP4X4),
+                        lhsT_scale=w4_s[g][s][:, P * t : P * (t + 1)],
+                        rhs=v_w[s, first + m0].bitcast(FP8X4),
+                        rhs_scale=v_s[s][:, first + m0 : first + m0 + BLOCK],
+                        start=(s == 0 and t == 0),
+                        stop=(s == PASSES - 1 and t == PACK - 1),
+                    )
+            kept_a = a_sb[g][d][:, :, m0 : m0 + BLOCK]
+            h = h_bf[d][:, g, m0 : m0 + BLOCK, :].rearrange("p n (u e) -> p n u e", u=2)
+            factor = decay[g][c][:, :, n0 : n0 + BLOCK, :].rearrange("p u n e -> p n u e")
+            if engine in "VW":
+                nc.vector.tensor_tensor(h, acc.rearrange("p (u e) n -> p n u e", u=2), factor, ALU.mult)
+            if engine in "VP":
+                nc.scalar.activation(kept_a, acc, ACT.Copy)
+            else:
+                nc.vector.tensor_copy(out=kept_a, in_=acc)
+            if engine in "PQ":
+                nc.gpsimd.tensor_tensor(h, kept_a.rearrange("p (u e) n -> p n u e", u=2), factor, ALU.mult)
 
-        def quantize_h(g, d):
+        def quantize_h(d, g0=0, g1=GROUPS):
+            count = SPANS[d][1]
             nc.vector.quantize_mx(
-                out=h_q[g][d][:].bitcast(FP8X4), scales=h_s[g][d][:], in_=h_bf[g, d][:].rearrange("p n t -> p (n t)")
+                out=h_q[d][:, count * g0 : count * g1].bitcast(FP8X4),
+                scales=h_s[d][:, count * g0 : count * g1],
+                in_=h_bf[d][:, g0:g1].rearrange("p g n t -> p (g n t)"),
             )
 
         out_rows = out.rearrange("(g p t) j -> g p t j", g=GROUPS, t=PACK)
@@ -260,10 +268,10 @@ def tile_list_mixed_layer_step_kernel(
                     for s in range(PASSES):
                         nc.tensor.matmul_mx(
                             out=y[:, i, :],
-                            lhsT=w8_p[s][g][:, col : col + P].bitcast(FP8X4),
+                            lhsT=w8_p[s][:, K_PASS * g + col : K_PASS * g + col + P].bitcast(FP8X4),
                             lhsT_scale=w8_s[g][4 * s : P, col : col + P],
-                            rhs=h_q[s][d][:].bitcast(FP8X4),
-                            rhs_scale=h_s[s][d][:],
+                            rhs=h_q[d][:, count * s : count * (s + 1)].bitcast(FP8X4),
+                            rhs_scale=h_s[d][:, count * s : count * (s + 1)],
                             start=(s == 0),
                             stop=(s == PASSES - 1),
                         )
@@ -275,79 +283,75 @@ def tile_list_mixed_layer_step_kernel(
                     )
                 nc.sync.dma_start(out=out_rows[g][:, t0 : t0 + per_bank, first : first + count], in_=result[:])
 
-        v2_s[0] = kept([P, HALF], U8, "v2_s0")
+        v2_s = kept([P, S], U8, "v2_s")
         v2_w[0] = kept([P, HALF], U16, "v2_w0")
-        v2_s[1] = kept([P, HALF], U8, "v2_s1")
-        gather(v2_s[0], tab2_s, list2, 0, HALF)
-        gather(v2_s[1], tab2_s, list2, HALF, HALF)
+        gather(v2_s, tab2_s, list2, 0, S)
         round_w2_on_scalar(0, 0)
         round_w2_on_vector(0, 1)
         quantize_w2(0)
         gather(v2_w[0], tab2_w, list2, 0, HALF)
-        round_w2_on_scalar(1, 0)
         make_decay(0, 0, HALF)
         v_s0 = placed([P, S], U8, "v_s0", 0)
         v_s = [v_s0, v_s1]
         gather(v_s0, tab_s, list1, 0, S)
+        round_w2_on_gpsimd(1, 0)
         round_w2_on_vector(1, 1)
         quantize_w2(1)
         make_decay(1, 0, HALF)
-
         for z in range(QUADS):
-            nc.sync.dma_start(
-                out=v_s1[z:P:32, :].bitcast(I32), in_=v_s0[4 + z : P : 32, :].bitcast(I32)
-            )
+            nc.sync.dma_start(out=v_s1[z:P:32, :].bitcast(I32), in_=v_s0[4 + z : P : 32, :].bitcast(I32))
         load_words(tab_w[1], tab_words[1].rearrange("p c i -> p (c i)"))
         load_w4(1)
+        load_two_planes(nc.sync, w8s_raw, w8_scales)
         for s in range(PASSES):
             load_words(w8_raw[s], w8_words[s].rearrange("p c i -> p (c i)"))
         nc.sync.dma_start(out=step_sb[:], in_=step.rearrange("(g p t) -> p g t", g=GROUPS, t=PACK))
+
         for g in range(GROUPS):
             for s in range(PASSES):
                 deal(w4_s[g][s][:], w4s_raw[:, H * s + K_PASS * g : H * s + K_PASS * (g + 1)])
-        for g in range(GROUPS):
             for s in range(PASSES):
                 deal(w4_p[g][s][:], w4_raw[g][:, K_PASS * s : K_PASS * (s + 1)])
         for g in range(GROUPS):
             deal(w8_s[g][:], w8s_raw[:, K_PASS * g : K_PASS * (g + 1)])
+        gather_tab_words(0, 0, HALF)
         v2_w[1] = placed([P, HALF], U16, "v2_w1", 3 * W2_BYTES)
         gather(v2_w[1], tab2_w, list2, HALF, HALF)
-        for s in range(PASSES):
-            for k in range(S // CHUNK):
-                gather_tab_words(s, k)
-
-        make_h(0, 0, True)
-        make_h(0, 1, True)
-        quantize_h(0, 0)
-        make_h(1, 0, True)
+        gather_tab_words(0, HALF, HALF)
+        gather_tab_words(1, 0, HALF)
         deal_w8(0)
-        quantize_h(0, 1)
-        make_h(1, 1, True)
-        quantize_h(1, 0)
-        make_decay(0, 512, CHUNK)
         deal_w8(1)
-        quantize_h(1, 1)
+        make_h(0, 0, 0, "V")
+        make_h(0, 0, 128, "V")
+        make_h(0, 0, 256, "V")
+        make_h(0, 0, 384, "V")
+        make_h(1, 0, 0, "V")
+        quantize_h(0, 0, 1)
+        make_h(1, 0, 128, "V")
+        make_h(1, 0, 256, "V")
+        make_h(1, 0, 384, "V")
+        make_decay(0, 512, 256)
+        quantize_h(0, 1, 2)
+        make_decay(1, 512, 256)
         finish(0, 0)
-        make_decay(1, 512, CHUNK)
+        gather_tab_words(1, 512, 512)
+        make_decay(0, 768, 256)
+        make_h(0, 1, 0, "V")
+        make_h(0, 1, 128, "V")
+        make_h(1, 1, 0, "V")
+        make_h(1, 1, 128, "V")
+        quantize_h(1)
         finish(0, 1)
-        make_h(0, 2, True)
+        make_decay(1, 768, 256)
         finish(1, 0)
-        make_decay(0, 768, CHUNK)
-        quantize_h(0, 2)
-        make_h(1, 2, True)
+        make_h(0, 2, 0, "V")
+        make_h(1, 2, 0, "V")
+        quantize_h(2)
+        make_h(0, 3, 0, "V")
+        make_h(1, 3, 0, "V")
+        quantize_h(3)
         finish(1, 1)
-        make_decay(1, 768, CHUNK)
-        quantize_h(1, 2)
-        make_h(0, 3, True)
         finish(2, 0)
-        make_h(0, 4, True)
-        quantize_h(0, 3)
-        make_h(1, 3, True)
-        quantize_h(0, 4)
-        make_h(1, 4, True)
-        quantize_h(1, 3)
         finish(2, 1)
-        quantize_h(1, 4)
-        for d in (3, 4):
-            for g in range(GROUPS):
-                finish(d, g)
+        finish(3, 0)
+        finish(3, 1)

@@ -30,7 +30,7 @@ CHUNK = 256
 BLOCK = BANK // PACK
 W2_COLS = 256
 W2_BYTES = 2 * PACK * K_PASS
-SPANS = ((0, 512), (512, 256), (768, 128), (896, 128))
+SPANS = ((0, 512), (512, 256), (768, 256))
 
 
 def tile_list_mixed_layer_step_kernel(
@@ -56,7 +56,7 @@ def tile_list_mixed_layer_step_kernel(
         tab2_s = kept([P, T], U8, "tab2_s")
         tab_w = [kept([P, T], U32, "tab_w%d" % s) for s in range(PASSES)]
         tab_s = placed([P, T], U8, "tab_s", 3 * W2_BYTES)
-        w2_raw = [[kept([P, PACK, W2_COLS], F32, "w2_raw%d%d" % (g, q)) for q in range(2)] for g in range(GROUPS)]
+        w2_raw = [[placed([P, PACK, W2_COLS], F32, "w2_raw%d%d" % (g, q), 8 * W2_BYTES + W2_BYTES * (2 * g + q)) for q in range(2)] for g in range(GROUPS)]
         w4_raw = [
             placed([P, PASSES * K_PASS], U16, "w4_raw0", 2 * W2_BYTES), kept([P, PASSES * K_PASS], U16, "w4_raw1")
         ]
@@ -67,7 +67,7 @@ def tile_list_mixed_layer_step_kernel(
         step_sb = kept([P, GROUPS, PACK], F32, "step_sb")
         v_s1 = kept([P, S], U8, "v_s1")
 
-        for plane in (tab2_s, tab_s, w4s_raw, w8s_raw, v_s1):
+        for plane in (tab2_s, w4s_raw, tab_s, w8s_raw, v_s1):
             nc.vector.memset(plane[:].bitcast(I32), 0)
 
         def load_words(tile, src):
@@ -100,16 +100,17 @@ def tile_list_mixed_layer_step_kernel(
         load_w2(0, 1)
         load_words(tab2_w, tab2_words[0])
         nc.sync.dma_start(list1[:], offs)
-        load_two_planes(nc.gpsimd, tab_s, tab_scales)
         for r in range(4):
             nc.gpsimd.dma_start(
                 out=w4s_raw[r:P:32, :].bitcast(I32).rearrange("z (s c) -> z s c", s=PASSES),
                 in_=w4_scales[:, r:16:4, :].bitcast(I32).rearrange("s z c -> z s c"),
             )
+        load_two_planes(nc.gpsimd, tab_s, tab_scales)
         load_w2(1, 0)
         load_w2(1, 1)
         load_words(tab_w[0], tab_words[0].rearrange("p c i -> p (c i)"))
         load_w4(0)
+        load_words(tab_w[1], tab_words[1].rearrange("p c i -> p (c i)"))
 
         log_rate = kept([P, GROUPS * PACK], F32, "log_rate")
         root = kept([P, GROUPS * PACK], F32, "root")
@@ -120,8 +121,8 @@ def tile_list_mixed_layer_step_kernel(
         w2_q = [kept([P, K_PASS], U32, "w2_q%d" % g) for g in range(GROUPS)]
         w2_s = [kept([P, K_PASS], U8, "w2_s%d" % g) for g in range(GROUPS)]
         w4_s = [
-            [placed([P, K_PASS], U8, "w4_s%d%d" % (g, s), W2_BYTES + 4 * K_PASS + K_PASS * (PASSES * g + s)) for s in range(PASSES)]
-            for g in range(GROUPS)
+            [placed([P, K_PASS], U8, "w4_s0%d" % s, S + K_PASS * s) for s in range(PASSES)],
+            [placed([P, K_PASS], U8, "w4_s1%d" % s, W2_BYTES + 4 * K_PASS + K_PASS * s) for s in range(PASSES)],
         ]
         w4_p = [
             [placed([P, K_PASS], U16, "w4_p0%d" % s, W2_BYTES + 2 * K_PASS * s) for s in range(PASSES)],
@@ -147,7 +148,7 @@ def tile_list_mixed_layer_step_kernel(
             nc.vector.tensor_copy(dst[:], window[:].indirect(offsets[:, first // 16 : (first + count) // 16]))
 
         def gather_tab_words(s, first, count):
-            words = placed([P, count], U32, "v_w%d_%d" % (s, first), 4 * W2_BYTES + 4 * (first if s == 0 else S + first % HALF))
+            words = kept([P, count], U32, "v_w%d_%d" % (s, first))
             gather(words, tab_w[s], list1, first, count)
             for m0 in range(0, count, BLOCK):
                 v_w[s, first + m0] = words[:, m0 : m0 + BLOCK]
@@ -281,7 +282,10 @@ def tile_list_mixed_layer_step_kernel(
                         result[:, i, :], a_sb[g][d][:, t, :], step_sb[:, g, t : t + 1], y[:, i, :],
                         ALU.mult, ALU.add,
                     )
-                nc.sync.dma_start(out=out_rows[g][:, t0 : t0 + per_bank, first : first + count], in_=result[:])
+                    if d == len(SPANS) - 1:
+                        nc.sync.dma_start(out=out_rows[g][:, t, first : first + count], in_=result[:, i, :])
+                if d < len(SPANS) - 1:
+                    nc.sync.dma_start(out=out_rows[g][:, t0 : t0 + per_bank, first : first + count], in_=result[:])
 
         v2_s = kept([P, S], U8, "v2_s")
         v2_w[0] = kept([P, HALF], U16, "v2_w0")
@@ -291,16 +295,17 @@ def tile_list_mixed_layer_step_kernel(
         quantize_w2(0)
         gather(v2_w[0], tab2_w, list2, 0, HALF)
         make_decay(0, 0, HALF)
-        v_s0 = placed([P, S], U8, "v_s0", 0)
-        v_s = [v_s0, v_s1]
-        gather(v_s0, tab_s, list1, 0, S)
-        round_w2_on_gpsimd(1, 0)
+        v2_w[1] = placed([P, HALF], U16, "v2_w1", 0)
+        gather(v2_w[1], tab2_w, list2, HALF, HALF)
+        round_w2_on_vector(1, 0)
         round_w2_on_vector(1, 1)
         quantize_w2(1)
+        v_s0 = placed([P, S], U8, "v_s0", W2_BYTES + 6 * K_PASS)
+        v_s = [v_s0, v_s1]
+        gather(v_s0, tab_s, list1, 0, S)
         make_decay(1, 0, HALF)
         for z in range(QUADS):
             nc.sync.dma_start(out=v_s1[z:P:32, :].bitcast(I32), in_=v_s0[4 + z : P : 32, :].bitcast(I32))
-        load_words(tab_w[1], tab_words[1].rearrange("p c i -> p (c i)"))
         load_w4(1)
         load_two_planes(nc.sync, w8s_raw, w8_scales)
         for s in range(PASSES):
@@ -315,10 +320,9 @@ def tile_list_mixed_layer_step_kernel(
         for g in range(GROUPS):
             deal(w8_s[g][:], w8s_raw[:, K_PASS * g : K_PASS * (g + 1)])
         gather_tab_words(0, 0, HALF)
-        v2_w[1] = placed([P, HALF], U16, "v2_w1", 3 * W2_BYTES)
-        gather(v2_w[1], tab2_w, list2, HALF, HALF)
         gather_tab_words(0, HALF, HALF)
         gather_tab_words(1, 0, HALF)
+        gather_tab_words(1, 512, 512)
         deal_w8(0)
         deal_w8(1)
         make_h(0, 0, 0, "V")
@@ -326,32 +330,28 @@ def tile_list_mixed_layer_step_kernel(
         make_h(0, 0, 256, "V")
         make_h(0, 0, 384, "V")
         make_h(1, 0, 0, "V")
-        quantize_h(0, 0, 1)
         make_h(1, 0, 128, "V")
         make_h(1, 0, 256, "V")
-        make_h(1, 0, 384, "V")
         make_decay(0, 512, 256)
-        quantize_h(0, 1, 2)
-        make_decay(1, 512, 256)
-        finish(0, 0)
-        gather_tab_words(1, 512, 512)
-        make_decay(0, 768, 256)
+        quantize_h(0, 0, 1)
+        make_h(1, 0, 384, "V")
         make_h(0, 1, 0, "V")
+        make_decay(1, 512, 256)
+        quantize_h(0, 1, 2)
         make_h(0, 1, 128, "V")
         make_h(1, 1, 0, "V")
+        finish(0, 0)
+        make_decay(0, 768, 256)
         make_h(1, 1, 128, "V")
         quantize_h(1)
         finish(0, 1)
         make_decay(1, 768, 256)
         finish(1, 0)
         make_h(0, 2, 0, "V")
+        make_h(0, 2, 128, "V")
         make_h(1, 2, 0, "V")
+        make_h(1, 2, 128, "V")
         quantize_h(2)
-        make_h(0, 3, 0, "V")
-        make_h(1, 3, 0, "V")
-        quantize_h(3)
         finish(1, 1)
         finish(2, 0)
         finish(2, 1)
-        finish(3, 0)
-        finish(3, 1)

@@ -54,11 +54,11 @@ def tile_list_mixed_layer_step_kernel(
         list2 = kept([P, S // 16], U16, "list2")
         tab2_w = kept([P, T], U16, "tab2_w")
         tab2_s = kept([P, T], U8, "tab2_s")
-        tab_w = [kept([P, T], U32, "tab_w%d" % s) for s in range(PASSES)]
-        tab_s = placed([P, T], U8, "tab_s", 3 * W2_BYTES)
-        w2_raw = [[placed([P, PACK, W2_COLS], F32, "w2_raw%d%d" % (g, q), 8 * W2_BYTES + W2_BYTES * (2 * g + q)) for q in range(2)] for g in range(GROUPS)]
+        tab_w = [placed([P, T], U32, "tab_w0", 5 * W2_BYTES), kept([P, T], U32, "tab_w1")]
+        tab_s = kept([P, T], U8, "tab_s")
+        w2_raw = [kept([P, PACK, K_PASS], F32, "w2_raw%d" % g) for g in range(GROUPS)]
         w4_raw = [
-            placed([P, PASSES * K_PASS], U16, "w4_raw0", 2 * W2_BYTES), kept([P, PASSES * K_PASS], U16, "w4_raw1")
+            placed([P, PASSES * K_PASS], U16, "w4_raw0", 2 * W2_BYTES), placed([P, PASSES * K_PASS], U16, "w4_raw1", 4 * W2_BYTES)
         ]
         w4s_raw = kept([P, PASSES * H], U8, "w4s_raw")
         w8s_raw = kept([P, H], U8, "w8s_raw")
@@ -67,16 +67,15 @@ def tile_list_mixed_layer_step_kernel(
         step_sb = kept([P, GROUPS, PACK], F32, "step_sb")
         v_s1 = kept([P, S], U8, "v_s1")
 
-        for plane in (tab2_s, w4s_raw, tab_s, w8s_raw, v_s1):
+        for plane in (tab2_s, tab_s, w4s_raw, w8s_raw, v_s1):
             nc.vector.memset(plane[:].bitcast(I32), 0)
 
         def load_words(tile, src):
             nc.sync.dma_start(out=tile[:].bitcast(I32), in_=src.bitcast(I32))
 
-        def load_w2(g, q):
-            c0 = K_PASS * g + W2_COLS * q
+        def load_w2(g):
             nc.sync.dma_start(
-                out=w2_raw[g][q][:], in_=w2.rearrange("(p i) c -> p i c", i=PACK)[:, :, c0 : c0 + W2_COLS]
+                out=w2_raw[g][:], in_=w2.rearrange("(p i) c -> p i c", i=PACK)[:, :, K_PASS * g : K_PASS * (g + 1)]
             )
 
         def load_w4(g):
@@ -96,21 +95,18 @@ def tile_list_mixed_layer_step_kernel(
         nc.sync.dma_start(list2[:], offs2)
         for r in range(4):
             nc.sync.dma_start(out=tab2_s[r:P:32, :].bitcast(I32), in_=tab2_scales[0, r:16:4, :].bitcast(I32))
-        load_w2(0, 0)
-        load_w2(0, 1)
+        load_w2(0)
         load_words(tab2_w, tab2_words[0])
         nc.sync.dma_start(list1[:], offs)
+        load_two_planes(nc.sync, tab_s, tab_scales)
+        load_w2(1)
         for r in range(4):
-            nc.gpsimd.dma_start(
+            nc.sync.dma_start(
                 out=w4s_raw[r:P:32, :].bitcast(I32).rearrange("z (s c) -> z s c", s=PASSES),
                 in_=w4_scales[:, r:16:4, :].bitcast(I32).rearrange("s z c -> z s c"),
             )
-        load_two_planes(nc.gpsimd, tab_s, tab_scales)
-        load_w2(1, 0)
-        load_w2(1, 1)
         load_words(tab_w[0], tab_words[0].rearrange("p c i -> p (c i)"))
         load_w4(0)
-        load_words(tab_w[1], tab_words[1].rearrange("p c i -> p (c i)"))
 
         log_rate = kept([P, GROUPS * PACK], F32, "log_rate")
         root = kept([P, GROUPS * PACK], F32, "root")
@@ -121,14 +117,11 @@ def tile_list_mixed_layer_step_kernel(
         w2_q = [kept([P, K_PASS], U32, "w2_q%d" % g) for g in range(GROUPS)]
         w2_s = [kept([P, K_PASS], U8, "w2_s%d" % g) for g in range(GROUPS)]
         w4_s = [
-            [placed([P, K_PASS], U8, "w4_s0%d" % s, S + K_PASS * s) for s in range(PASSES)],
-            [placed([P, K_PASS], U8, "w4_s1%d" % s, W2_BYTES + 4 * K_PASS + K_PASS * s) for s in range(PASSES)],
+            [placed([P, K_PASS], U8, "w4_s0%d" % s, W2_BYTES + K_PASS * s) for s in range(PASSES)],
+            [placed([P, K_PASS], U8, "w4_s1%d" % s, 2 * W2_BYTES + 2 * K_PASS + K_PASS * s) for s in range(PASSES)],
         ]
-        w4_p = [
-            [placed([P, K_PASS], U16, "w4_p0%d" % s, W2_BYTES + 2 * K_PASS * s) for s in range(PASSES)],
-            [kept([P, K_PASS], U16, "w4_p1%d" % s) for s in range(PASSES)],
-        ]
-        w8_s = [kept([P, K_PASS], U8, "w8_s%d" % g) for g in range(GROUPS)]
+        w4_p = [[kept([P, K_PASS], U16, "w4_p%d%d" % (g, s)) for s in range(PASSES)] for g in range(GROUPS)]
+        w8_s = [placed([P, K_PASS], U8, "w8_s%d" % g, 4 * W2_BYTES + 2 * K_PASS + K_PASS * g) for g in range(GROUPS)]
         w8_p = [kept([P, H], U32, "w8_p%d" % s) for s in range(PASSES)]
         decay = [[kept([P, 2, HALF, 2], F32, "decay%d%d" % (g, c)) for c in range(2)] for g in range(GROUPS)]
         a_sb = [[kept([P, PACK, n], F32, "a_sb%d%d" % (g, d)) for d, (f, n) in enumerate(SPANS)] for g in range(GROUPS)]
@@ -159,20 +152,26 @@ def tile_list_mixed_layer_step_kernel(
             for u in range(2):
                 nc.scalar.activation(
                     w2_bf[g][:, 2 * u : 2 * u + 2, m_cols * q : m_cols * (q + 1), :].rearrange("p e m i -> p m i e"),
-                    w2_raw[g][q][:].rearrange("p i (m t) -> p m i t", t=PACK)[:, :, :, 2 * u : 2 * u + 2],
+                    w2_raw[g][:, :, W2_COLS * q : W2_COLS * (q + 1)].rearrange("p i (m t) -> p m i t", t=PACK)[:, :, :, 2 * u : 2 * u + 2],
                     ACT.Copy,
                 )
 
         def round_w2_on_vector(g, q):
             nc.vector.tensor_copy(
                 out=w2_bf[g][:, :, m_cols * q : m_cols * (q + 1), :].rearrange("p (u e) m i -> p u m i e", u=2),
-                in_=w2_raw[g][q][:].rearrange("p i (m u e) -> p u m i e", u=2, e=2),
+                in_=w2_raw[g][:, :, W2_COLS * q : W2_COLS * (q + 1)].rearrange("p i (m u e) -> p u m i e", u=2, e=2),
             )
 
         def round_w2_on_gpsimd(g, q):
             nc.gpsimd.tensor_copy(
                 out=w2_bf[g][:, :, m_cols * q : m_cols * (q + 1), :],
-                in_=w2_raw[g][q][:].rearrange("p i (m t) -> p t m i", t=PACK),
+                in_=w2_raw[g][:, :, W2_COLS * q : W2_COLS * (q + 1)].rearrange("p i (m t) -> p t m i", t=PACK),
+            )
+
+        def round_group_on_vector(g):
+            nc.vector.tensor_copy(
+                out=w2_bf[g][:].rearrange("p (u e) m i -> p u m i e", u=2),
+                in_=w2_raw[g][:].rearrange("p i (m u e) -> p u m i e", u=2, e=2),
             )
 
         def quantize_w2(g):
@@ -295,17 +294,15 @@ def tile_list_mixed_layer_step_kernel(
         quantize_w2(0)
         gather(v2_w[0], tab2_w, list2, 0, HALF)
         make_decay(0, 0, HALF)
-        v2_w[1] = placed([P, HALF], U16, "v2_w1", 0)
-        gather(v2_w[1], tab2_w, list2, HALF, HALF)
-        round_w2_on_vector(1, 0)
-        round_w2_on_vector(1, 1)
-        quantize_w2(1)
-        v_s0 = placed([P, S], U8, "v_s0", W2_BYTES + 6 * K_PASS)
+        v_s0 = placed([P, S], U8, "v_s0", 0)
         v_s = [v_s0, v_s1]
         gather(v_s0, tab_s, list1, 0, S)
+        round_group_on_vector(1)
+        quantize_w2(1)
         make_decay(1, 0, HALF)
         for z in range(QUADS):
             nc.sync.dma_start(out=v_s1[z:P:32, :].bitcast(I32), in_=v_s0[4 + z : P : 32, :].bitcast(I32))
+        load_words(tab_w[1], tab_words[1].rearrange("p c i -> p (c i)"))
         load_w4(1)
         load_two_planes(nc.sync, w8s_raw, w8_scales)
         for s in range(PASSES):
@@ -321,27 +318,29 @@ def tile_list_mixed_layer_step_kernel(
             deal(w8_s[g][:], w8s_raw[:, K_PASS * g : K_PASS * (g + 1)])
         gather_tab_words(0, 0, HALF)
         gather_tab_words(0, HALF, HALF)
+        v2_w[1] = placed([P, HALF], U16, "v2_w1", 5 * W2_BYTES)
+        gather(v2_w[1], tab2_w, list2, HALF, HALF)
         gather_tab_words(1, 0, HALF)
-        gather_tab_words(1, 512, 512)
+        gather_tab_words(1, HALF, HALF)
         deal_w8(0)
         deal_w8(1)
         make_h(0, 0, 0, "V")
         make_h(0, 0, 128, "V")
         make_h(0, 0, 256, "V")
         make_h(0, 0, 384, "V")
+        quantize_h(0, 0, 1)
         make_h(1, 0, 0, "V")
         make_h(1, 0, 128, "V")
-        make_h(1, 0, 256, "V")
         make_decay(0, 512, 256)
-        quantize_h(0, 0, 1)
+        make_h(1, 0, 256, "V")
         make_h(1, 0, 384, "V")
-        make_h(0, 1, 0, "V")
-        make_decay(1, 512, 256)
         quantize_h(0, 1, 2)
+        make_h(0, 1, 0, "V")
         make_h(0, 1, 128, "V")
-        make_h(1, 1, 0, "V")
+        make_decay(1, 512, 256)
         finish(0, 0)
         make_decay(0, 768, 256)
+        make_h(1, 1, 0, "V")
         make_h(1, 1, 128, "V")
         quantize_h(1)
         finish(0, 1)

@@ -151,15 +151,15 @@ def tile_list_mixed_layer_step_kernel(
         def round_w2_on_scalar(g, q):
             for u in range(2):
                 nc.scalar.activation(
-                    w2_bf[g][:, 2 * u : 2 * u + 2, m_cols * q : m_cols * (q + 1), :].rearrange("p e m i -> p m i e"),
-                    w2_raw[g][:, :, W2_COLS * q : W2_COLS * (q + 1)].rearrange("p i (m t) -> p m i t", t=PACK)[:, :, :, 2 * u : 2 * u + 2],
+                    w2_bf[g][:, 2 * u : 2 * u + 2, m_cols * q : m_cols * (q + 1), :].rearrange("p e m i -> p m e i"),
+                    w2_raw[g][:, :, W2_COLS * q : W2_COLS * (q + 1)].rearrange("p i (m t) -> p m t i", t=PACK)[:, :, 2 * u : 2 * u + 2, :],
                     ACT.Copy,
                 )
 
         def round_w2_on_vector(g, q):
             nc.vector.tensor_copy(
-                out=w2_bf[g][:, :, m_cols * q : m_cols * (q + 1), :].rearrange("p (u e) m i -> p u m i e", u=2),
-                in_=w2_raw[g][:, :, W2_COLS * q : W2_COLS * (q + 1)].rearrange("p i (m u e) -> p u m i e", u=2, e=2),
+                out=w2_bf[g][:, :, m_cols * q : m_cols * (q + 1), :].rearrange("p (u e) m i -> p u m e i", u=2),
+                in_=w2_raw[g][:, :, W2_COLS * q : W2_COLS * (q + 1)].rearrange("p i (m u e) -> p u m e i", u=2, e=2),
             )
 
         def round_w2_on_gpsimd(g, q):
@@ -170,8 +170,8 @@ def tile_list_mixed_layer_step_kernel(
 
         def round_group_on_vector(g):
             nc.vector.tensor_copy(
-                out=w2_bf[g][:].rearrange("p (u e) m i -> p u m i e", u=2),
-                in_=w2_raw[g][:].rearrange("p i (m u e) -> p u m i e", u=2, e=2),
+                out=w2_bf[g][:].rearrange("p (u e) m i -> p u m e i", u=2),
+                in_=w2_raw[g][:].rearrange("p i (m u e) -> p u m e i", u=2, e=2),
             )
 
         def quantize_w2(g):

@@ -54,9 +54,9 @@ def tile_list_mixed_layer_step_kernel(
         list2 = kept([P, S // 16], U16, "list2")
         tab2_w = kept([P, T], U16, "tab2_w")
         tab2_s = kept([P, T], U8, "tab2_s")
-        tab_w = [placed([P, T], U32, "tab_w0", 5 * W2_BYTES), kept([P, T], U32, "tab_w1")]
+        tab_w = [kept([P, T], U32, "tab_w%d" % s) for s in range(PASSES)]
         tab_s = kept([P, T], U8, "tab_s")
-        w2_raw = [kept([P, PACK, K_PASS], F32, "w2_raw%d" % g) for g in range(GROUPS)]
+        w2_raw = [kept([P, PACK, K_PASS], F32, "w2_raw0"), placed([P, PACK, K_PASS], F32, "w2_raw1", 5 * W2_BYTES)]
         w4_raw = [
             placed([P, PASSES * K_PASS], U16, "w4_raw0", 2 * W2_BYTES), placed([P, PASSES * K_PASS], U16, "w4_raw1", 4 * W2_BYTES)
         ]
@@ -186,8 +186,8 @@ def tile_list_mixed_layer_step_kernel(
 
         def deal_w8(s):
             nc.vector.tensor_copy(
-                out=w8_p[s][:].bitcast(I32).rearrange("p (g u e m) -> p g u m e", u=2, e=2, m=P),
-                in_=w8_raw[s][:].bitcast(I32).rearrange("p (g m u e) -> p g u m e", u=2, e=2, m=P),
+                out=w8_p[s][:].bitcast(I32).rearrange("p (g t m c) -> p g m t c", g=GROUPS, t=PACK, c=4),
+                in_=w8_raw[s][:].bitcast(I32).rearrange("p (g m c t) -> p g m t c", g=GROUPS, t=PACK, c=4),
             )
 
         def make_decay(g, first, count):
@@ -261,7 +261,6 @@ def tile_list_mixed_layer_step_kernel(
             first, count = SPANS[d]
             per_bank = BANK // count
             for t0 in range(0, PACK, per_bank):
-                result = ring.tile([P, per_bank, count], F32, name="result", bufs=6)
                 y = take_bank()[:].rearrange("p (i n) -> p i n", i=per_bank)
                 for i in range(per_bank):
                     col = P * (t0 + i)
@@ -278,13 +277,12 @@ def tile_list_mixed_layer_step_kernel(
                 for i in range(per_bank):
                     t = t0 + i
                     nc.vector.scalar_tensor_tensor(
-                        result[:, i, :], a_sb[g][d][:, t, :], step_sb[:, g, t : t + 1], y[:, i, :],
+                        a_sb[g][d][:, t, :], a_sb[g][d][:, t, :], step_sb[:, g, t : t + 1], y[:, i, :],
                         ALU.mult, ALU.add,
                     )
-                    if d == len(SPANS) - 1:
-                        nc.sync.dma_start(out=out_rows[g][:, t, first : first + count], in_=result[:, i, :])
-                if d < len(SPANS) - 1:
-                    nc.sync.dma_start(out=out_rows[g][:, t0 : t0 + per_bank, first : first + count], in_=result[:])
+                nc.sync.dma_start(
+                    out=out_rows[g][:, t0 : t0 + per_bank, first : first + count], in_=a_sb[g][d][:, t0 : t0 + per_bank, :]
+                )
 
         v2_s = kept([P, S], U8, "v2_s")
         v2_w[0] = kept([P, HALF], U16, "v2_w0")
@@ -294,7 +292,7 @@ def tile_list_mixed_layer_step_kernel(
         quantize_w2(0)
         gather(v2_w[0], tab2_w, list2, 0, HALF)
         make_decay(0, 0, HALF)
-        v_s0 = placed([P, S], U8, "v_s0", 0)
+        v_s0 = kept([P, S], U8, "v_s0")
         v_s = [v_s0, v_s1]
         gather(v_s0, tab_s, list1, 0, S)
         round_group_on_vector(1)
@@ -330,16 +328,16 @@ def tile_list_mixed_layer_step_kernel(
         make_h(0, 0, 384, "V")
         quantize_h(0, 0, 1)
         make_h(1, 0, 0, "V")
-        make_h(1, 0, 128, "V")
         make_decay(0, 512, 256)
+        make_h(1, 0, 128, "V")
         make_h(1, 0, 256, "V")
         make_h(1, 0, 384, "V")
         quantize_h(0, 1, 2)
         make_h(0, 1, 0, "V")
-        make_h(0, 1, 128, "V")
         make_decay(1, 512, 256)
         finish(0, 0)
         make_decay(0, 768, 256)
+        make_h(0, 1, 128, "V")
         make_h(1, 1, 0, "V")
         make_h(1, 1, 128, "V")
         quantize_h(1)

@@ -56,7 +56,7 @@ def tile_list_mixed_layer_step_kernel(
         tab2_s = kept([P, T], U8, "tab2_s")
         tab_w = [kept([P, T], U32, "tab_w%d" % s) for s in range(PASSES)]
         tab_s = kept([P, T], U8, "tab_s")
-        w2_raw = [kept([P, PACK, K_PASS], F32, "w2_raw0"), placed([P, PACK, K_PASS], F32, "w2_raw1", 5 * W2_BYTES)]
+        w2_raw = [kept([P, PACK, K_PASS], F32, "w2_raw%d" % g) for g in range(GROUPS)]
         w4_raw = [
             placed([P, PASSES * K_PASS], U16, "w4_raw0", 2 * W2_BYTES), placed([P, PASSES * K_PASS], U16, "w4_raw1", 4 * W2_BYTES)
         ]
@@ -67,15 +67,17 @@ def tile_list_mixed_layer_step_kernel(
         step_sb = kept([P, GROUPS, PACK], F32, "step_sb")
         v_s1 = kept([P, S], U8, "v_s1")
 
-        for plane in (tab2_s, tab_s, w4s_raw, w8s_raw, v_s1):
+        nc.gpsimd.memset(tab2_s[:].bitcast(I32), 0)
+        for plane in (tab_s, w4s_raw, w8s_raw, v_s1):
             nc.vector.memset(plane[:].bitcast(I32), 0)
 
         def load_words(tile, src):
             nc.sync.dma_start(out=tile[:].bitcast(I32), in_=src.bitcast(I32))
 
-        def load_w2(g):
+        def load_w2(g, c0, c1):
             nc.sync.dma_start(
-                out=w2_raw[g][:], in_=w2.rearrange("(p i) c -> p i c", i=PACK)[:, :, K_PASS * g : K_PASS * (g + 1)]
+                out=w2_raw[g][:, :, c0:c1],
+                in_=w2.rearrange("(p i) c -> p i c", i=PACK)[:, :, K_PASS * g + c0 : K_PASS * g + c1],
             )
 
         def load_w4(g):
@@ -93,13 +95,14 @@ def tile_list_mixed_layer_step_kernel(
 
         nc.sync.dma_start(out=rate_sb[:], in_=rate.rearrange("(g p t) -> p g t", g=GROUPS, t=PACK))
         nc.sync.dma_start(list2[:], offs2)
+        nc.sync.dma_start(list1[:], offs)
         for r in range(4):
             nc.sync.dma_start(out=tab2_s[r:P:32, :].bitcast(I32), in_=tab2_scales[0, r:16:4, :].bitcast(I32))
-        load_w2(0)
+        load_w2(0, 0, K_PASS)
         load_words(tab2_w, tab2_words[0])
-        nc.sync.dma_start(list1[:], offs)
+        load_w2(1, 0, W2_COLS)
+        load_w2(1, W2_COLS, K_PASS)
         load_two_planes(nc.sync, tab_s, tab_scales)
-        load_w2(1)
         for r in range(4):
             nc.sync.dma_start(
                 out=w4s_raw[r:P:32, :].bitcast(I32).rearrange("z (s c) -> z s c", s=PASSES),
@@ -107,6 +110,7 @@ def tile_list_mixed_layer_step_kernel(
             )
         load_words(tab_w[0], tab_words[0].rearrange("p c i -> p (c i)"))
         load_w4(0)
+        load_words(tab_w[1], tab_words[1].rearrange("p c i -> p (c i)"))
 
         log_rate = kept([P, GROUPS * PACK], F32, "log_rate")
         root = kept([P, GROUPS * PACK], F32, "root")
@@ -291,16 +295,18 @@ def tile_list_mixed_layer_step_kernel(
         round_w2_on_vector(0, 1)
         quantize_w2(0)
         gather(v2_w[0], tab2_w, list2, 0, HALF)
+        round_w2_on_scalar(1, 0)
         make_decay(0, 0, HALF)
+        v2_w[1] = kept([P, HALF], U16, "v2_w1")
+        gather(v2_w[1], tab2_w, list2, HALF, HALF)
         v_s0 = kept([P, S], U8, "v_s0")
         v_s = [v_s0, v_s1]
-        gather(v_s0, tab_s, list1, 0, S)
-        round_group_on_vector(1)
+        round_w2_on_vector(1, 1)
         quantize_w2(1)
+        gather(v_s0, tab_s, list1, 0, S)
         make_decay(1, 0, HALF)
         for z in range(QUADS):
             nc.sync.dma_start(out=v_s1[z:P:32, :].bitcast(I32), in_=v_s0[4 + z : P : 32, :].bitcast(I32))
-        load_words(tab_w[1], tab_words[1].rearrange("p c i -> p (c i)"))
         load_w4(1)
         load_two_planes(nc.sync, w8s_raw, w8_scales)
         for s in range(PASSES):
@@ -316,8 +322,6 @@ def tile_list_mixed_layer_step_kernel(
             deal(w8_s[g][:], w8s_raw[:, K_PASS * g : K_PASS * (g + 1)])
         gather_tab_words(0, 0, HALF)
         gather_tab_words(0, HALF, HALF)
-        v2_w[1] = placed([P, HALF], U16, "v2_w1", 5 * W2_BYTES)
-        gather(v2_w[1], tab2_w, list2, HALF, HALF)
         gather_tab_words(1, 0, HALF)
         gather_tab_words(1, HALF, HALF)
         deal_w8(0)

@@ -24,13 +24,12 @@ GROUPS = H // K_PASS
 QUADS = 4
 BANK = 512
 BANKS = 8
-H_BUFS = 2
 HALF = S // 2
 CHUNK = 256
 BLOCK = BANK // PACK
 W2_COLS = 256
 W2_BYTES = 2 * PACK * K_PASS
-SPANS = ((0, 512), (512, 256), (768, 256))
+SPANS = ((0, HALF), (HALF, CHUNK), (HALF + CHUNK, CHUNK))
 
 
 def tile_list_mixed_layer_step_kernel(
@@ -40,7 +39,7 @@ def tile_list_mixed_layer_step_kernel(
     nc = tc.nc
     with ExitStack() as ctx:
         keep = ctx.enter_context(tc.tile_pool(name="keep", bufs=1))
-        reuse = ctx.enter_context(tc.tile_pool(name="reuse", bufs=1))
+        twice = ctx.enter_context(tc.tile_pool(name="twice", bufs=1))
         ring = ctx.enter_context(tc.tile_pool(name="ring", bufs=3))
         psum = ctx.enter_context(tc.psum_pool(name="psum", bufs=1))
 
@@ -48,7 +47,7 @@ def tile_list_mixed_layer_step_kernel(
             return keep.tile(shape, dtype, name=name, align_bytes=64)
 
         def placed(shape, dtype, name, offset):
-            return reuse.tile(shape, dtype, name=name, align_bytes=64, offset=offset)
+            return twice.tile(shape, dtype, name=name, align_bytes=64, offset=offset)
 
         list1 = kept([P, S // 16], U16, "list1")
         list2 = kept([P, S // 16], U16, "list2")
@@ -57,9 +56,7 @@ def tile_list_mixed_layer_step_kernel(
         tab_w = [kept([P, T], U32, "tab_w%d" % s) for s in range(PASSES)]
         tab_s = kept([P, T], U8, "tab_s")
         w2_raw = [kept([P, PACK, K_PASS], F32, "w2_raw%d" % g) for g in range(GROUPS)]
-        w4_raw = [
-            placed([P, PASSES * K_PASS], U16, "w4_raw0", 2 * W2_BYTES), placed([P, PASSES * K_PASS], U16, "w4_raw1", 4 * W2_BYTES)
-        ]
+        w4_raw = [kept([P, PASSES * K_PASS], U16, "w4_raw0"), placed([P, PASSES * K_PASS], U16, "w4_raw1", W2_BYTES)]
         w4s_raw = kept([P, PASSES * H], U8, "w4s_raw")
         w8s_raw = kept([P, H], U8, "w8s_raw")
         w8_raw = [kept([P, H], U32, "w8_raw%d" % s) for s in range(PASSES)]
@@ -87,23 +84,23 @@ def tile_list_mixed_layer_step_kernel(
                 in_=w4_words.bitcast(I32).rearrange("s p c -> p s c")[:, :, half * g : half * (g + 1)],
             )
 
-        def load_two_planes(queue, tile, src):
+        def load_two_planes(tile, src):
             for z in range(QUADS):
-                queue.dma_start(
+                nc.sync.dma_start(
                     out=tile[32 * z : 32 * z + 8, :].bitcast(I32), in_=src[:, 4 * z : 4 * z + 4, :].bitcast(I32)
                 )
 
         nc.sync.dma_start(out=rate_sb[:], in_=rate.rearrange("(g p t) -> p g t", g=GROUPS, t=PACK))
         nc.sync.dma_start(list2[:], offs2)
         nc.sync.dma_start(list1[:], offs)
-        for r in range(4):
+        for r in range(QUADS):
             nc.sync.dma_start(out=tab2_s[r:P:32, :].bitcast(I32), in_=tab2_scales[0, r:16:4, :].bitcast(I32))
         load_w2(0, 0, K_PASS)
         load_words(tab2_w, tab2_words[0])
         load_w2(1, 0, W2_COLS)
         load_w2(1, W2_COLS, K_PASS)
-        load_two_planes(nc.sync, tab_s, tab_scales)
-        for r in range(4):
+        load_two_planes(tab_s, tab_scales)
+        for r in range(QUADS):
             nc.sync.dma_start(
                 out=w4s_raw[r:P:32, :].bitcast(I32).rearrange("z (s c) -> z s c", s=PASSES),
                 in_=w4_scales[:, r:16:4, :].bitcast(I32).rearrange("s z c -> z s c"),
@@ -117,15 +114,15 @@ def tile_list_mixed_layer_step_kernel(
         nc.scalar.activation(log_rate[:], rate_sb[:].rearrange("p g t -> p (g t)"), ACT.Ln, scale=-1.0)
         nc.scalar.activation(root[:], log_rate[:], ACT.Exp, scale=0.5)
 
-        w2_bf = [placed([P, PACK, P, PACK], BF16, "w2_bf%d" % g, W2_BYTES * g) for g in range(GROUPS)]
+        w2_bf = [kept([P, PACK, P, PACK], BF16, "w2_bf0"), placed([P, PACK, P, PACK], BF16, "w2_bf1", 0)]
         w2_q = [kept([P, K_PASS], U32, "w2_q%d" % g) for g in range(GROUPS)]
         w2_s = [kept([P, K_PASS], U8, "w2_s%d" % g) for g in range(GROUPS)]
         w4_s = [
-            [placed([P, K_PASS], U8, "w4_s0%d" % s, W2_BYTES + K_PASS * s) for s in range(PASSES)],
-            [placed([P, K_PASS], U8, "w4_s1%d" % s, 2 * W2_BYTES + 2 * K_PASS + K_PASS * s) for s in range(PASSES)],
+            [placed([P, K_PASS], U8, "w4_s%d%d" % (g, s), K_PASS * (PASSES * g + s)) for s in range(PASSES)]
+            for g in range(GROUPS)
         ]
         w4_p = [[kept([P, K_PASS], U16, "w4_p%d%d" % (g, s)) for s in range(PASSES)] for g in range(GROUPS)]
-        w8_s = [placed([P, K_PASS], U8, "w8_s%d" % g, 4 * W2_BYTES + 2 * K_PASS + K_PASS * g) for g in range(GROUPS)]
+        w8_s = [placed([P, K_PASS], U8, "w8_s%d" % g, W2_BYTES + K_PASS * (PASSES + g)) for g in range(GROUPS)]
         w8_p = [kept([P, H], U32, "w8_p%d" % s) for s in range(PASSES)]
         decay = [[kept([P, 2, HALF, 2], F32, "decay%d%d" % (g, c)) for c in range(2)] for g in range(GROUPS)]
         a_sb = [[kept([P, PACK, n], F32, "a_sb%d%d" % (g, d)) for d, (f, n) in enumerate(SPANS)] for g in range(GROUPS)]
@@ -152,30 +149,23 @@ def tile_list_mixed_layer_step_kernel(
 
         m_cols = W2_COLS // PACK
 
+        def w2_piece(g, q):
+            return w2_bf[g][:, :, m_cols * q : m_cols * (q + 1), :], w2_raw[g][:, :, W2_COLS * q : W2_COLS * (q + 1)]
+
         def round_w2_on_scalar(g, q):
+            dst, src = w2_piece(g, q)
             for u in range(2):
                 nc.scalar.activation(
-                    w2_bf[g][:, 2 * u : 2 * u + 2, m_cols * q : m_cols * (q + 1), :].rearrange("p e m i -> p m e i"),
-                    w2_raw[g][:, :, W2_COLS * q : W2_COLS * (q + 1)].rearrange("p i (m t) -> p m t i", t=PACK)[:, :, 2 * u : 2 * u + 2, :],
+                    dst[:, 2 * u : 2 * u + 2].rearrange("p e m i -> p m e i"),
+                    src.rearrange("p i (m t) -> p m t i", t=PACK)[:, :, 2 * u : 2 * u + 2, :],
                     ACT.Copy,
                 )
 
         def round_w2_on_vector(g, q):
+            dst, src = w2_piece(g, q)
             nc.vector.tensor_copy(
-                out=w2_bf[g][:, :, m_cols * q : m_cols * (q + 1), :].rearrange("p (u e) m i -> p u m e i", u=2),
-                in_=w2_raw[g][:, :, W2_COLS * q : W2_COLS * (q + 1)].rearrange("p i (m u e) -> p u m e i", u=2, e=2),
-            )
-
-        def round_w2_on_gpsimd(g, q):
-            nc.gpsimd.tensor_copy(
-                out=w2_bf[g][:, :, m_cols * q : m_cols * (q + 1), :],
-                in_=w2_raw[g][:, :, W2_COLS * q : W2_COLS * (q + 1)].rearrange("p i (m t) -> p t m i", t=PACK),
-            )
-
-        def round_group_on_vector(g):
-            nc.vector.tensor_copy(
-                out=w2_bf[g][:].rearrange("p (u e) m i -> p u m e i", u=2),
-                in_=w2_raw[g][:].rearrange("p i (m u e) -> p u m e i", u=2, e=2),
+                out=dst.rearrange("p (u e) m i -> p u m e i", u=2),
+                in_=src.rearrange("p i (m u e) -> p u m e i", u=2, e=2),
             )
 
         def quantize_w2(g):
@@ -222,11 +212,12 @@ def tile_list_mixed_layer_step_kernel(
                     decay[g][c][:, u, n0 : n0 + count, :], square[:].rearrange("p e n -> p n e"), ACT.Exp, scale=-1.0
                 )
 
-        def make_h(g, d, m0, engine):
+        def make_h(g, d, k):
             first, count = SPANS[d]
+            m0 = BLOCK * k
             c, n0 = divmod(first + m0, HALF)
             if d not in h_bf:
-                h_bf[d] = ring.tile([P, GROUPS, count, PACK], BF16, name="h_bf", bufs=H_BUFS, align_bytes=64)
+                h_bf[d] = ring.tile([P, GROUPS, count, PACK], BF16, name="h_bf", bufs=2, align_bytes=64)
             acc = take_bank()[:].rearrange("p (t n) -> p t n", t=PACK)
             for s in range(PASSES):
                 for t in range(PACK):
@@ -239,17 +230,13 @@ def tile_list_mixed_layer_step_kernel(
                         start=(s == 0 and t == 0),
                         stop=(s == PASSES - 1 and t == PACK - 1),
                     )
-            kept_a = a_sb[g][d][:, :, m0 : m0 + BLOCK]
-            h = h_bf[d][:, g, m0 : m0 + BLOCK, :].rearrange("p n (u e) -> p n u e", u=2)
-            factor = decay[g][c][:, :, n0 : n0 + BLOCK, :].rearrange("p u n e -> p n u e")
-            if engine in "VW":
-                nc.vector.tensor_tensor(h, acc.rearrange("p (u e) n -> p n u e", u=2), factor, ALU.mult)
-            if engine in "VP":
-                nc.scalar.activation(kept_a, acc, ACT.Copy)
-            else:
-                nc.vector.tensor_copy(out=kept_a, in_=acc)
-            if engine in "PQ":
-                nc.gpsimd.tensor_tensor(h, kept_a.rearrange("p (u e) n -> p n u e", u=2), factor, ALU.mult)
+            nc.vector.tensor_tensor(
+                h_bf[d][:, g, m0 : m0 + BLOCK, :].rearrange("p n (u e) -> p n u e", u=2),
+                acc.rearrange("p (u e) n -> p n u e", u=2),
+                decay[g][c][:, :, n0 : n0 + BLOCK, :].rearrange("p u n e -> p n u e"),
+                ALU.mult,
+            )
+            nc.scalar.activation(a_sb[g][d][:, :, m0 : m0 + BLOCK], acc, ACT.Copy)
 
         def quantize_h(d, g0=0, g1=GROUPS):
             count = SPANS[d][1]
@@ -285,7 +272,8 @@ def tile_list_mixed_layer_step_kernel(
                         ALU.mult, ALU.add,
                     )
                 nc.sync.dma_start(
-                    out=out_rows[g][:, t0 : t0 + per_bank, first : first + count], in_=a_sb[g][d][:, t0 : t0 + per_bank, :]
+                    out=out_rows[g][:, t0 : t0 + per_bank, first : first + count],
+                    in_=a_sb[g][d][:, t0 : t0 + per_bank, :],
                 )
 
         v2_s = kept([P, S], U8, "v2_s")
@@ -305,10 +293,11 @@ def tile_list_mixed_layer_step_kernel(
         quantize_w2(1)
         gather(v_s0, tab_s, list1, 0, S)
         make_decay(1, 0, HALF)
-        for z in range(QUADS):
-            nc.sync.dma_start(out=v_s1[z:P:32, :].bitcast(I32), in_=v_s0[4 + z : P : 32, :].bitcast(I32))
+
+        for r in range(QUADS):
+            nc.sync.dma_start(out=v_s1[r:P:32, :].bitcast(I32), in_=v_s0[4 + r : P : 32, :].bitcast(I32))
         load_w4(1)
-        load_two_planes(nc.sync, w8s_raw, w8_scales)
+        load_two_planes(w8s_raw, w8_scales)
         for s in range(PASSES):
             load_words(w8_raw[s], w8_words[s].rearrange("p c i -> p (c i)"))
         nc.sync.dma_start(out=step_sb[:], in_=step.rearrange("(g p t) -> p g t", g=GROUPS, t=PACK))
@@ -316,43 +305,41 @@ def tile_list_mixed_layer_step_kernel(
         for g in range(GROUPS):
             for s in range(PASSES):
                 deal(w4_s[g][s][:], w4s_raw[:, H * s + K_PASS * g : H * s + K_PASS * (g + 1)])
-            for s in range(PASSES):
+            for s in range(PASSES) if g == 0 else reversed(range(PASSES)):
                 deal(w4_p[g][s][:], w4_raw[g][:, K_PASS * s : K_PASS * (s + 1)])
         for g in range(GROUPS):
             deal(w8_s[g][:], w8s_raw[:, K_PASS * g : K_PASS * (g + 1)])
-        gather_tab_words(0, 0, HALF)
-        gather_tab_words(0, HALF, HALF)
-        gather_tab_words(1, 0, HALF)
-        gather_tab_words(1, HALF, HALF)
-        deal_w8(0)
-        deal_w8(1)
-        make_h(0, 0, 0, "V")
-        make_h(0, 0, 128, "V")
-        make_h(0, 0, 256, "V")
-        make_h(0, 0, 384, "V")
+        for s in range(PASSES):
+            for first in range(0, S, HALF):
+                gather_tab_words(s, first, HALF)
+        for s in range(PASSES):
+            deal_w8(s)
+
+        for k in range(HALF // BLOCK):
+            make_h(0, 0, k)
         quantize_h(0, 0, 1)
-        make_h(1, 0, 0, "V")
-        make_decay(0, 512, 256)
-        make_h(1, 0, 128, "V")
-        make_h(1, 0, 256, "V")
-        make_h(1, 0, 384, "V")
+        make_h(1, 0, 0)
+        make_decay(0, *SPANS[1])
+        for k in range(1, HALF // BLOCK):
+            make_h(1, 0, k)
         quantize_h(0, 1, 2)
-        make_h(0, 1, 0, "V")
-        make_decay(1, 512, 256)
+
+        make_h(0, 1, 0)
+        make_decay(1, *SPANS[1])
         finish(0, 0)
-        make_decay(0, 768, 256)
-        make_h(0, 1, 128, "V")
-        make_h(1, 1, 0, "V")
-        make_h(1, 1, 128, "V")
+        make_decay(0, *SPANS[2])
+        make_h(0, 1, 1)
+        for k in range(CHUNK // BLOCK):
+            make_h(1, 1, k)
         quantize_h(1)
         finish(0, 1)
-        make_decay(1, 768, 256)
+
+        make_decay(1, *SPANS[2])
         finish(1, 0)
-        make_h(0, 2, 0, "V")
-        make_h(0, 2, 128, "V")
-        make_h(1, 2, 0, "V")
-        make_h(1, 2, 128, "V")
+        for g in range(GROUPS):
+            for k in range(CHUNK // BLOCK):
+                make_h(g, 2, k)
         quantize_h(2)
         finish(1, 1)
-        finish(2, 0)
-        finish(2, 1)
+        for g in range(GROUPS):
+            finish(2, g)

@@ -56,7 +56,10 @@ def tile_list_mixed_layer_step_kernel(
         tab_w = [kept([P, T], U32, "tab_w%d" % s) for s in range(PASSES)]
         tab_s = kept([P, T], U8, "tab_s")
         w2_raw = [kept([P, PACK, K_PASS], F32, "w2_raw%d" % g) for g in range(GROUPS)]
-        w4_raw = [kept([P, PASSES * K_PASS], U16, "w4_raw0"), placed([P, PASSES * K_PASS], U16, "w4_raw1", W2_BYTES)]
+        w4_raw = [
+            kept([P, PASSES * K_PASS], U16, "w4_raw0"),
+            placed([P, PASSES * K_PASS], U16, "w4_raw1", W2_BYTES),
+        ]
         w4s_raw = kept([P, PASSES * H], U8, "w4s_raw")
         w8s_raw = kept([P, H], U8, "w8s_raw")
         w8_raw = [kept([P, H], U32, "w8_raw%d" % s) for s in range(PASSES)]
@@ -315,31 +318,21 @@ def tile_list_mixed_layer_step_kernel(
         for s in range(PASSES):
             deal_w8(s)
 
-        for k in range(HALF // BLOCK):
-            make_h(0, 0, k)
-        quantize_h(0, 0, 1)
-        make_h(1, 0, 0)
-        make_decay(0, *SPANS[1])
-        for k in range(1, HALF // BLOCK):
-            make_h(1, 0, k)
-        quantize_h(0, 1, 2)
-
-        make_h(0, 1, 0)
-        make_decay(1, *SPANS[1])
-        finish(0, 0)
-        make_decay(0, *SPANS[2])
-        make_h(0, 1, 1)
-        for k in range(CHUNK // BLOCK):
-            make_h(1, 1, k)
-        quantize_h(1)
-        finish(0, 1)
-
-        make_decay(1, *SPANS[2])
-        finish(1, 0)
         for g in range(GROUPS):
-            for k in range(CHUNK // BLOCK):
-                make_h(g, 2, k)
-        quantize_h(2)
-        finish(1, 1)
+            for k in range(HALF // BLOCK):
+                make_h(g, 0, k)
+            quantize_h(0, g, g + 1)
+            if g == 0:
+                make_decay(0, *SPANS[1])
+        for d in range(1, len(SPANS)):
+            make_decay(1, *SPANS[d])
+            finish(d - 1, 0)
+            if d + 1 < len(SPANS):
+                make_decay(0, *SPANS[d + 1])
+            for g in range(GROUPS):
+                for k in range(CHUNK // BLOCK):
+                    make_h(g, d, k)
+            quantize_h(d)
+            finish(d - 1, 1)
         for g in range(GROUPS):
-            finish(2, g)
+            finish(len(SPANS) - 1, g)

@@ -66,9 +66,10 @@ def tile_list_mixed_layer_step_kernel(
         rate_sb = kept([P, GROUPS, PACK], F32, "rate_sb")
         step_sb = kept([P, GROUPS, PACK], F32, "step_sb")
         v_s1 = kept([P, S], U8, "v_s1")
+        v2_s = kept([P, S], U8, "v2_s")
 
         nc.gpsimd.memset(tab2_s[:].bitcast(I32), 0)
-        for plane in (tab_s, w4s_raw, w8s_raw, v_s1):
+        for plane in (v2_s, tab_s, w4s_raw, w8s_raw, v_s1):
             nc.vector.memset(plane[:].bitcast(I32), 0)
 
         def load_words(tile, src):
@@ -96,11 +97,18 @@ def tile_list_mixed_layer_step_kernel(
         nc.sync.dma_start(out=rate_sb[:], in_=rate.rearrange("(g p t) -> p g t", g=GROUPS, t=PACK))
         nc.sync.dma_start(list2[:], offs2)
         nc.sync.dma_start(list1[:], offs)
-        for r in range(QUADS):
-            nc.sync.dma_start(out=tab2_s[r:P:32, :].bitcast(I32), in_=tab2_scales[0, r:16:4, :].bitcast(I32))
+        nc.sync.dma_start(out=tab2_s[0:P:8, :].bitcast(I32), in_=tab2_scales[0].bitcast(I32))
         load_w2(0, 0, K_PASS)
         load_words(tab2_w, tab2_words[0])
         load_w2(1, 0, W2_COLS)
+
+        def gather(dst, window, offsets, first, count):
+            nc.vector.tensor_copy(dst[:], window[:].indirect(offsets[:, first // 16 : (first + count) // 16]))
+
+        v2_rows = kept([P, S], U8, "v2_rows")
+        gather(v2_rows, tab2_s, list2, 0, S)
+        for r in range(QUADS):
+            nc.sync.dma_start(out=v2_s[r:P:32, :].bitcast(I32), in_=v2_rows[8 * r : P : 32, :].bitcast(I32))
         load_w2(1, W2_COLS, K_PASS)
         load_two_planes(tab_s, tab_scales)
         for r in range(QUADS):
@@ -140,9 +148,6 @@ def tile_list_mixed_layer_step_kernel(
         def take_bank():
             taken.append(banks[len(taken) % BANKS])
             return taken[-1]
-
-        def gather(dst, window, offsets, first, count):
-            nc.vector.tensor_copy(dst[:], window[:].indirect(offsets[:, first // 16 : (first + count) // 16]))
 
         def gather_tab_words(s, first, count):
             words = kept([P, count], U32, "v_w%d_%d" % (s, first))
@@ -279,13 +284,11 @@ def tile_list_mixed_layer_step_kernel(
                     in_=a_sb[g][d][:, t0 : t0 + per_bank, :],
                 )
 
-        v2_s = kept([P, S], U8, "v2_s")
         v2_w[0] = kept([P, HALF], U16, "v2_w0")
-        gather(v2_s, tab2_s, list2, 0, S)
         round_w2_on_scalar(0, 0)
         round_w2_on_vector(0, 1)
-        quantize_w2(0)
         gather(v2_w[0], tab2_w, list2, 0, HALF)
+        quantize_w2(0)
         round_w2_on_scalar(1, 0)
         make_decay(0, 0, HALF)
         v2_w[1] = kept([P, HALF], U16, "v2_w1")

@@ -57,12 +57,12 @@ def tile_list_mixed_layer_step_kernel(
         tab_s = kept([P, T], U8, "tab_s")
         w2_raw = [kept([P, PACK, K_PASS], F32, "w2_raw%d" % g) for g in range(GROUPS)]
         w4_raw = [
-            kept([P, PASSES * K_PASS], U16, "w4_raw0"),
-            placed([P, PASSES * K_PASS], U16, "w4_raw1", W2_BYTES),
+            placed([P, PASSES * K_PASS], U16, "w4_raw0", 5 * W2_BYTES),
+            kept([P, PASSES * K_PASS], U16, "w4_raw1"),
         ]
         w4s_raw = kept([P, PASSES * H], U8, "w4s_raw")
         w8s_raw = kept([P, H], U8, "w8s_raw")
-        w8_raw = [kept([P, H], U32, "w8_raw%d" % s) for s in range(PASSES)]
+        w8_raw = [kept([P, PASSES, K_PASS], U32, "w8_raw%d" % g) for g in range(GROUPS)]
         rate_sb = kept([P, GROUPS, PACK], F32, "rate_sb")
         step_sb = kept([P, GROUPS, PACK], F32, "step_sb")
         v_s1 = kept([P, S], U8, "v_s1")
@@ -129,17 +129,26 @@ def tile_list_mixed_layer_step_kernel(
         w2_q = [kept([P, K_PASS], U32, "w2_q%d" % g) for g in range(GROUPS)]
         w2_s = [kept([P, K_PASS], U8, "w2_s%d" % g) for g in range(GROUPS)]
         w4_s = [
-            [placed([P, K_PASS], U8, "w4_s%d%d" % (g, s), K_PASS * (PASSES * g + s)) for s in range(PASSES)]
+            [placed([P, K_PASS], U8, "w4_s%d%d" % (g, s), 5 * W2_BYTES * g + K_PASS * s) for s in range(PASSES)]
             for g in range(GROUPS)
         ]
         w4_p = [[kept([P, K_PASS], U16, "w4_p%d%d" % (g, s)) for s in range(PASSES)] for g in range(GROUPS)]
-        w8_s = [placed([P, K_PASS], U8, "w8_s%d" % g, W2_BYTES + K_PASS * (PASSES + g)) for g in range(GROUPS)]
-        w8_p = [kept([P, H], U32, "w8_p%d" % s) for s in range(PASSES)]
+        w8_s = [
+            placed([P, K_PASS], U8, "w8_s0", 2 * W2_BYTES + 4 * K_PASS),
+            placed([P, K_PASS], U8, "w8_s1", 3 * W2_BYTES + 4 * CHUNK),
+        ]
+        h_first = [placed([P, HALF, PACK], BF16, "h_first%d" % g, (2 + g) * W2_BYTES) for g in range(GROUPS)]
+        w8_late = placed([P, PASSES, K_PASS], U32, "w8_p1", 3 * W2_BYTES + 4 * CHUNK + K_PASS)
+        w8_p = [
+            [kept([P, K_PASS], U32, "w8_p00")[:], placed([P, K_PASS], U32, "w8_p01", 2 * W2_BYTES)[:]],
+            [w8_late[:, s, :] for s in range(PASSES)],
+        ]
         decay = [[kept([P, 2, HALF, 2], F32, "decay%d%d" % (g, c)) for c in range(2)] for g in range(GROUPS)]
         a_sb = [[kept([P, PACK, n], F32, "a_sb%d%d" % (g, d)) for d, (f, n) in enumerate(SPANS)] for g in range(GROUPS)]
         h_q = [kept([P, GROUPS * n], U32, "h_q%d" % d) for d, (f, n) in enumerate(SPANS)]
         h_s = [kept([P, GROUPS * n], U8, "h_s%d" % d) for d, (f, n) in enumerate(SPANS)]
-        h_bf = {}
+        h_later = [kept([P, GROUPS, n, PACK], BF16, "h_bf%d" % d) for d, (f, n) in enumerate(SPANS[1:])]
+        h_bf = [[h[:] for h in h_first]] + [[h[:, g] for g in range(GROUPS)] for h in h_later]
         v_w = {}
         v2_w = {}
         banks = [psum.tile([P, BANK], F32, name="bank%d" % i) for i in range(BANKS)]
@@ -149,8 +158,9 @@ def tile_list_mixed_layer_step_kernel(
             taken.append(banks[len(taken) % BANKS])
             return taken[-1]
 
-        def gather_tab_words(s, first, count):
-            words = kept([P, count], U32, "v_w%d_%d" % (s, first))
+        def gather_tab_words(s, first, count, words=None):
+            if words is None:
+                words = kept([P, count], U32, "v_w%d_%d" % (s, first))
             gather(words, tab_w[s], list1, first, count)
             for m0 in range(0, count, BLOCK):
                 v_w[s, first + m0] = words[:, m0 : m0 + BLOCK]
@@ -186,10 +196,10 @@ def tile_list_mixed_layer_step_kernel(
                 out=dst.rearrange("p (t m) -> p t m", t=PACK), in_=src.rearrange("p (m t) -> p t m", t=PACK)
             )
 
-        def deal_w8(s):
-            nc.vector.tensor_copy(
-                out=w8_p[s][:].bitcast(I32).rearrange("p (g t m c) -> p g m t c", g=GROUPS, t=PACK, c=4),
-                in_=w8_raw[s][:].bitcast(I32).rearrange("p (g m c t) -> p g m t c", g=GROUPS, t=PACK, c=4),
+        def deal_w8(g, s):
+            nc.gpsimd.tensor_copy(
+                out=w8_p[g][s].rearrange("p (t m c) -> p m t c", t=PACK, c=4),
+                in_=w8_raw[g][:, s, :].rearrange("p (m c t) -> p m t c", t=PACK, c=4),
             )
 
         def make_decay(g, first, count):
@@ -224,8 +234,6 @@ def tile_list_mixed_layer_step_kernel(
             first, count = SPANS[d]
             m0 = BLOCK * k
             c, n0 = divmod(first + m0, HALF)
-            if d not in h_bf:
-                h_bf[d] = ring.tile([P, GROUPS, count, PACK], BF16, name="h_bf", bufs=2, align_bytes=64)
             acc = take_bank()[:].rearrange("p (t n) -> p t n", t=PACK)
             for s in range(PASSES):
                 for t in range(PACK):
@@ -239,19 +247,19 @@ def tile_list_mixed_layer_step_kernel(
                         stop=(s == PASSES - 1 and t == PACK - 1),
                     )
             nc.vector.tensor_tensor(
-                h_bf[d][:, g, m0 : m0 + BLOCK, :].rearrange("p n (u e) -> p n u e", u=2),
+                h_bf[d][g][:, m0 : m0 + BLOCK, :].rearrange("p n (u e) -> p n u e", u=2),
                 acc.rearrange("p (u e) n -> p n u e", u=2),
                 decay[g][c][:, :, n0 : n0 + BLOCK, :].rearrange("p u n e -> p n u e"),
                 ALU.mult,
             )
             nc.scalar.activation(a_sb[g][d][:, :, m0 : m0 + BLOCK], acc, ACT.Copy)
 
-        def quantize_h(d, g0=0, g1=GROUPS):
+        def quantize_h(d, g0, g1, values):
             count = SPANS[d][1]
             nc.vector.quantize_mx(
                 out=h_q[d][:, count * g0 : count * g1].bitcast(FP8X4),
                 scales=h_s[d][:, count * g0 : count * g1],
-                in_=h_bf[d][:, g0:g1].rearrange("p g n t -> p (g n t)"),
+                in_=values,
             )
 
         out_rows = out.rearrange("(g p t) j -> g p t j", g=GROUPS, t=PACK)
@@ -266,7 +274,7 @@ def tile_list_mixed_layer_step_kernel(
                     for s in range(PASSES):
                         nc.tensor.matmul_mx(
                             out=y[:, i, :],
-                            lhsT=w8_p[s][:, K_PASS * g + col : K_PASS * g + col + P].bitcast(FP8X4),
+                            lhsT=w8_p[g][s][:, col : col + P].bitcast(FP8X4),
                             lhsT_scale=w8_s[g][4 * s : P, col : col + P],
                             rhs=h_q[d][:, count * s : count * (s + 1)].bitcast(FP8X4),
                             rhs_scale=h_s[d][:, count * s : count * (s + 1)],
@@ -279,10 +287,12 @@ def tile_list_mixed_layer_step_kernel(
                         a_sb[g][d][:, t, :], a_sb[g][d][:, t, :], step_sb[:, g, t : t + 1], y[:, i, :],
                         ALU.mult, ALU.add,
                     )
-                nc.sync.dma_start(
-                    out=out_rows[g][:, t0 : t0 + per_bank, first : first + count],
-                    in_=a_sb[g][d][:, t0 : t0 + per_bank, :],
-                )
+                last = first + count == S and g == GROUPS - 1 and t0 + per_bank == PACK
+                rows = 1 if last else per_bank
+                for t in range(t0, t0 + per_bank, rows):
+                    nc.sync.dma_start(
+                        out=out_rows[g][:, t : t + rows, first : first + count], in_=a_sb[g][d][:, t : t + rows, :]
+                    )
 
         v2_w[0] = kept([P, HALF], U16, "v2_w0")
         round_w2_on_scalar(0, 0)
@@ -304,8 +314,11 @@ def tile_list_mixed_layer_step_kernel(
             nc.sync.dma_start(out=v_s1[r:P:32, :].bitcast(I32), in_=v_s0[4 + r : P : 32, :].bitcast(I32))
         load_w4(1)
         load_two_planes(w8s_raw, w8_scales)
-        for s in range(PASSES):
-            load_words(w8_raw[s], w8_words[s].rearrange("p c i -> p (c i)"))
+        for g in range(GROUPS):
+            nc.sync.dma_start(
+                out=w8_raw[g][:].bitcast(I32),
+                in_=w8_words.rearrange("s p c i -> p s (c i)").bitcast(I32)[:, :, K_PASS * g : K_PASS * (g + 1)],
+            )
         nc.sync.dma_start(out=step_sb[:], in_=step.rearrange("(g p t) -> p g t", g=GROUPS, t=PACK))
 
         for g in range(GROUPS):
@@ -313,20 +326,21 @@ def tile_list_mixed_layer_step_kernel(
                 deal(w4_s[g][s][:], w4s_raw[:, H * s + K_PASS * g : H * s + K_PASS * (g + 1)])
             for s in range(PASSES) if g == 0 else reversed(range(PASSES)):
                 deal(w4_p[g][s][:], w4_raw[g][:, K_PASS * s : K_PASS * (s + 1)])
-        for g in range(GROUPS):
-            deal(w8_s[g][:], w8s_raw[:, K_PASS * g : K_PASS * (g + 1)])
-        for s in range(PASSES):
-            for first in range(0, S, HALF):
-                gather_tab_words(s, first, HALF)
-        for s in range(PASSES):
-            deal_w8(s)
+        gather_tab_words(0, 0, HALF)
+        gather_tab_words(0, HALF, HALF)
+        gather_tab_words(1, 0, HALF)
+        gather_tab_words(1, *SPANS[1])
+        deal_w8(0, 0)
 
+        make_decay(0, *SPANS[1])
         for g in range(GROUPS):
             for k in range(HALF // BLOCK):
                 make_h(g, 0, k)
-            quantize_h(0, g, g + 1)
-            if g == 0:
-                make_decay(0, *SPANS[1])
+            quantize_h(0, g, g + 1, h_bf[0][g].rearrange("p n t -> p (n t)"))
+            deal(w8_s[g][:], w8s_raw[:, K_PASS * g : K_PASS * (g + 1)])
+            for s in range(1 - g, PASSES):
+                deal_w8(g, s)
+        gather_tab_words(1, *SPANS[2], placed([P, CHUNK], U32, "v_w_last", 3 * W2_BYTES))
         for d in range(1, len(SPANS)):
             make_decay(1, *SPANS[d])
             finish(d - 1, 0)
@@ -335,7 +349,7 @@ def tile_list_mixed_layer_step_kernel(
             for g in range(GROUPS):
                 for k in range(CHUNK // BLOCK):
                     make_h(g, d, k)
-            quantize_h(d)
+            quantize_h(d, 0, GROUPS, h_later[d - 1][:].rearrange("p g n t -> p (g n t)"))
             finish(d - 1, 1)
         for g in range(GROUPS):
             finish(len(SPANS) - 1, g)

@@ -128,9 +128,10 @@ def tile_list_mixed_layer_step_kernel(
         w2_bf = [kept([P, PACK, P, PACK], BF16, "w2_bf0"), placed([P, PACK, P, PACK], BF16, "w2_bf1", 0)]
         w2_q = [kept([P, K_PASS], U32, "w2_q%d" % g) for g in range(GROUPS)]
         w2_s = [kept([P, K_PASS], U8, "w2_s%d" % g) for g in range(GROUPS)]
+        w4_s_late = placed([P, PASSES, K_PASS], U8, "w4_s1", 5 * W2_BYTES)
         w4_s = [
-            [placed([P, K_PASS], U8, "w4_s%d%d" % (g, s), 5 * W2_BYTES * g + K_PASS * s) for s in range(PASSES)]
-            for g in range(GROUPS)
+            [placed([P, K_PASS], U8, "w4_s0%d" % s, K_PASS * s)[:] for s in range(PASSES)],
+            [w4_s_late[:, s, :] for s in range(PASSES)],
         ]
         w4_p = [[kept([P, K_PASS], U16, "w4_p%d%d" % (g, s)) for s in range(PASSES)] for g in range(GROUPS)]
         w8_s = [
@@ -321,13 +322,17 @@ def tile_list_mixed_layer_step_kernel(
             )
         nc.sync.dma_start(out=step_sb[:], in_=step.rearrange("(g p t) -> p g t", g=GROUPS, t=PACK))
 
+        for s in range(PASSES):
+            deal(w4_s[0][s], w4s_raw[:, H * s : H * s + K_PASS])
         for g in range(GROUPS):
-            for s in range(PASSES):
-                deal(w4_s[g][s][:], w4s_raw[:, H * s + K_PASS * g : H * s + K_PASS * (g + 1)])
             for s in range(PASSES) if g == 0 else reversed(range(PASSES)):
                 deal(w4_p[g][s][:], w4_raw[g][:, K_PASS * s : K_PASS * (s + 1)])
         gather_tab_words(0, 0, HALF)
         gather_tab_words(0, HALF, HALF)
+        nc.vector.tensor_copy(
+            out=w4_s_late[:].rearrange("p s (t m) -> p s t m", t=PACK),
+            in_=w4s_raw[:].rearrange("p (s g m t) -> p s g t m", s=PASSES, g=GROUPS, t=PACK)[:, :, 1],
+        )
         gather_tab_words(1, 0, HALF)
         gather_tab_words(1, *SPANS[1])
         deal_w8(0, 0)

@@ -57,7 +57,7 @@ def tile_list_mixed_layer_step_kernel(
         tab_s = kept([P, T], U8, "tab_s")
         w2_raw = [kept([P, PACK, K_PASS], F32, "w2_raw%d" % g) for g in range(GROUPS)]
         w4_raw = [
-            placed([P, PASSES * K_PASS], U16, "w4_raw0", 5 * W2_BYTES),
+            placed([P, PASSES * K_PASS], U16, "w4_raw0", 6 * W2_BYTES),
             kept([P, PASSES * K_PASS], U16, "w4_raw1"),
         ]
         w4s_raw = kept([P, PASSES * H], U8, "w4s_raw")
@@ -128,18 +128,16 @@ def tile_list_mixed_layer_step_kernel(
         w2_bf = [kept([P, PACK, P, PACK], BF16, "w2_bf0"), placed([P, PACK, P, PACK], BF16, "w2_bf1", 0)]
         w2_q = [kept([P, K_PASS], U32, "w2_q%d" % g) for g in range(GROUPS)]
         w2_s = [kept([P, K_PASS], U8, "w2_s%d" % g) for g in range(GROUPS)]
-        w4_s_late = placed([P, PASSES, K_PASS], U8, "w4_s1", 5 * W2_BYTES)
+        w4_s_late = placed([P, PASSES, K_PASS], U8, "w4_s1", 6 * W2_BYTES)
         w4_s = [
             [placed([P, K_PASS], U8, "w4_s0%d" % s, K_PASS * s)[:] for s in range(PASSES)],
             [w4_s_late[:, s, :] for s in range(PASSES)],
         ]
         w4_p = [[kept([P, K_PASS], U16, "w4_p%d%d" % (g, s)) for s in range(PASSES)] for g in range(GROUPS)]
-        w8_s = [
-            placed([P, K_PASS], U8, "w8_s0", 2 * W2_BYTES + 4 * K_PASS),
-            placed([P, K_PASS], U8, "w8_s1", 3 * W2_BYTES + 4 * CHUNK),
-        ]
-        h_first = [placed([P, HALF, PACK], BF16, "h_first%d" % g, (2 + g) * W2_BYTES) for g in range(GROUPS)]
-        w8_late = placed([P, PASSES, K_PASS], U32, "w8_p1", 3 * W2_BYTES + 4 * CHUNK + K_PASS)
+        w8_s_both = kept([P, GROUPS, K_PASS], U8, "w8_s")
+        w8_s = [w8_s_both[:, g, :] for g in range(GROUPS)]
+        h_first = [placed([P, HALF, PACK], BF16, "h_first%d" % g, (2 + 2 * g) * W2_BYTES) for g in range(GROUPS)]
+        w8_late = placed([P, PASSES, K_PASS], U32, "w8_p1", 4 * W2_BYTES + 64 + 4 * CHUNK)
         w8_p = [
             [kept([P, K_PASS], U32, "w8_p00")[:], placed([P, K_PASS], U32, "w8_p01", 2 * W2_BYTES)[:]],
             [w8_late[:, s, :] for s in range(PASSES)],
@@ -148,16 +146,18 @@ def tile_list_mixed_layer_step_kernel(
         a_sb = [[kept([P, PACK, n], F32, "a_sb%d%d" % (g, d)) for d, (f, n) in enumerate(SPANS)] for g in range(GROUPS)]
         h_q = [kept([P, GROUPS * n], U32, "h_q%d" % d) for d, (f, n) in enumerate(SPANS)]
         h_s = [kept([P, GROUPS * n], U8, "h_s%d" % d) for d, (f, n) in enumerate(SPANS)]
-        h_later = [kept([P, GROUPS, n, PACK], BF16, "h_bf%d" % d) for d, (f, n) in enumerate(SPANS[1:])]
+        h_later = [
+            placed([P, GROUPS, CHUNK, PACK], BF16, "h_bf1", 7 * W2_BYTES),
+            placed([P, GROUPS, CHUNK, PACK], BF16, "h_bf2", 15 * W2_BYTES // 2),
+        ]
+        held = [placed([P, 1, HALF], F32, "held0", 7 * W2_BYTES), placed([P, 2, CHUNK], F32, "held1", 8 * W2_BYTES)]
+        a_pairs = kept([P, 2, CHUNK, 2], F32, "a_pairs")
         h_bf = [[h[:] for h in h_first]] + [[h[:, g] for g in range(GROUPS)] for h in h_later]
         v_w = {}
+        v_wide = {}
         v2_w = {}
         banks = [psum.tile([P, BANK], F32, name="bank%d" % i) for i in range(BANKS)]
-        taken = []
-
-        def take_bank():
-            taken.append(banks[len(taken) % BANKS])
-            return taken[-1]
+        pairs = [banks[2 * i : 2 * i + 2] for i in range(BANKS // 2)]
 
         def gather_tab_words(s, first, count, words=None):
             if words is None:
@@ -165,6 +165,8 @@ def tile_list_mixed_layer_step_kernel(
             gather(words, tab_w[s], list1, first, count)
             for m0 in range(0, count, BLOCK):
                 v_w[s, first + m0] = words[:, m0 : m0 + BLOCK]
+            for m0 in range(0, count, CHUNK):
+                v_wide[s, first + m0] = words[:, m0 : m0 + CHUNK]
 
         m_cols = W2_COLS // PACK
 
@@ -203,7 +205,7 @@ def tile_list_mixed_layer_step_kernel(
                 in_=w8_raw[g][:, s, :].rearrange("p (m c t) -> p m t c", t=PACK, c=4),
             )
 
-        def make_decay(g, first, count):
+        def make_decay(g, first, count, given):
             c, n0 = divmod(first, HALF)
             per_bank = BANK // count
             for u in range(2):
@@ -211,7 +213,7 @@ def tile_list_mixed_layer_step_kernel(
                 b = []
                 for e in range(2):
                     if e % per_bank == 0:
-                        bank = take_bank()
+                        bank = given[(2 * u + e) // per_bank]
                     b.append(bank[:, count * (e % per_bank) : count * (e % per_bank + 1)])
                     nc.tensor.matmul_mx(
                         out=b[e],
@@ -231,11 +233,11 @@ def tile_list_mixed_layer_step_kernel(
                     decay[g][c][:, u, n0 : n0 + count, :], square[:].rearrange("p e n -> p n e"), ACT.Exp, scale=-1.0
                 )
 
-        def make_h(g, d, k):
+        def make_h(g, d, k, bank):
             first, count = SPANS[d]
             m0 = BLOCK * k
             c, n0 = divmod(first + m0, HALF)
-            acc = take_bank()[:].rearrange("p (t n) -> p t n", t=PACK)
+            acc = bank[:].rearrange("p (t n) -> p t n", t=PACK)
             for s in range(PASSES):
                 for t in range(PACK):
                     nc.tensor.matmul_mx(
@@ -253,7 +255,33 @@ def tile_list_mixed_layer_step_kernel(
                 decay[g][c][:, :, n0 : n0 + BLOCK, :].rearrange("p u n e -> p n u e"),
                 ALU.mult,
             )
-            nc.scalar.activation(a_sb[g][d][:, :, m0 : m0 + BLOCK], acc, ACT.Copy)
+
+            def copy_a(copy):
+                copy(out=a_sb[g][d][:, :, m0 : m0 + BLOCK], in_=acc)
+
+            return copy_a
+
+        def make_h_on_gpsimd(d, given):
+            first, count = SPANS[d]
+            c, n0 = divmod(first, HALF)
+            for u, bank in enumerate(given):
+                acc = bank[:].rearrange("p (e n) -> p e n", e=2)
+                for s in range(PASSES):
+                    for e in range(2):
+                        t = 2 * u + e
+                        nc.tensor.matmul_mx(
+                            out=acc[:, e, :],
+                            lhsT=w4_p[0][s][:, P * t : P * (t + 1)].bitcast(FP4X4),
+                            lhsT_scale=w4_s[0][s][:, P * t : P * (t + 1)],
+                            rhs=v_wide[s, first].bitcast(FP8X4),
+                            rhs_scale=v_s[s][:, first : first + count],
+                            start=(s == 0 and e == 0),
+                            stop=(s == PASSES - 1 and e == 1),
+                        )
+                nc.scalar.copy(out=a_pairs[:, u], in_=acc.rearrange("p e n -> p n e"))
+                nc.gpsimd.tensor_tensor(
+                    h_bf[d][0][:, :, 2 * u : 2 * u + 2], a_pairs[:, u], decay[0][c][:, u, n0 : n0 + count, :], ALU.mult
+                )
 
         def quantize_h(d, g0, g1, values):
             count = SPANS[d][1]
@@ -265,11 +293,12 @@ def tile_list_mixed_layer_step_kernel(
 
         out_rows = out.rearrange("(g p t) j -> g p t j", g=GROUPS, t=PACK)
 
-        def finish(d, g):
+        def finish(d, g, t_first, given, res=None):
             first, count = SPANS[d]
             per_bank = BANK // count
-            for t0 in range(0, PACK, per_bank):
-                y = take_bank()[:].rearrange("p (i n) -> p i n", i=per_bank)
+            for t0, bank in zip(range(t_first, PACK, per_bank), given):
+                y = bank[:].rearrange("p (i n) -> p i n", i=per_bank)
+                result = a_sb[g][d][:, t0 : t0 + per_bank, :] if res is None else res[:]
                 for i in range(per_bank):
                     col = P * (t0 + i)
                     for s in range(PASSES):
@@ -284,15 +313,16 @@ def tile_list_mixed_layer_step_kernel(
                         )
                 for i in range(per_bank):
                     t = t0 + i
+                    a = a_pairs[:, t // 2, :, t % 2] if (g, d) == (0, 2) else a_sb[g][d][:, t, :]
                     nc.vector.scalar_tensor_tensor(
-                        a_sb[g][d][:, t, :], a_sb[g][d][:, t, :], step_sb[:, g, t : t + 1], y[:, i, :],
+                        result[:, i, :], a, step_sb[:, g, t : t + 1], y[:, i, :],
                         ALU.mult, ALU.add,
                     )
                 last = first + count == S and g == GROUPS - 1 and t0 + per_bank == PACK
                 rows = 1 if last else per_bank
-                for t in range(t0, t0 + per_bank, rows):
+                for i in range(0, per_bank, rows):
                     nc.sync.dma_start(
-                        out=out_rows[g][:, t : t + rows, first : first + count], in_=a_sb[g][d][:, t : t + rows, :]
+                        out=out_rows[g][:, t0 + i : t0 + i + rows, first : first + count], in_=result[:, i : i + rows, :]
                     )
 
         v2_w[0] = kept([P, HALF], U16, "v2_w0")
@@ -301,7 +331,7 @@ def tile_list_mixed_layer_step_kernel(
         gather(v2_w[0], tab2_w, list2, 0, HALF)
         quantize_w2(0)
         round_w2_on_scalar(1, 0)
-        make_decay(0, 0, HALF)
+        make_decay(0, 0, HALF, pairs[0] + pairs[1])
         v2_w[1] = kept([P, HALF], U16, "v2_w1")
         gather(v2_w[1], tab2_w, list2, HALF, HALF)
         v_s0 = kept([P, S], U8, "v_s0")
@@ -309,7 +339,7 @@ def tile_list_mixed_layer_step_kernel(
         round_w2_on_vector(1, 1)
         quantize_w2(1)
         gather(v_s0, tab_s, list1, 0, S)
-        make_decay(1, 0, HALF)
+        make_decay(1, 0, HALF, pairs[2] + pairs[3])
 
         for r in range(QUADS):
             nc.sync.dma_start(out=v_s1[r:P:32, :].bitcast(I32), in_=v_s0[4 + r : P : 32, :].bitcast(I32))
@@ -335,26 +365,45 @@ def tile_list_mixed_layer_step_kernel(
         )
         gather_tab_words(1, 0, HALF)
         gather_tab_words(1, *SPANS[1])
+        nc.gpsimd.tensor_copy(
+            out=w8_s_both[:].rearrange("p g (t m) -> p g t m", t=PACK),
+            in_=w8s_raw[:].rearrange("p (g m t) -> p g t m", g=GROUPS, t=PACK),
+        )
         deal_w8(0, 0)
 
-        make_decay(0, *SPANS[1])
+        make_decay(0, *SPANS[1], pairs[0])
         for g in range(GROUPS):
-            for k in range(HALF // BLOCK):
-                make_h(g, 0, k)
+            for k, bank in enumerate(pairs[1] + pairs[2] if g == 0 else pairs[3] + pairs[0]):
+                make_h(g, 0, k, bank)(nc.scalar.copy)
             quantize_h(0, g, g + 1, h_bf[0][g].rearrange("p n t -> p (n t)"))
-            deal(w8_s[g][:], w8s_raw[:, K_PASS * g : K_PASS * (g + 1)])
             for s in range(1 - g, PASSES):
                 deal_w8(g, s)
-        gather_tab_words(1, *SPANS[2], placed([P, CHUNK], U32, "v_w_last", 3 * W2_BYTES))
-        for d in range(1, len(SPANS)):
-            make_decay(1, *SPANS[d])
-            finish(d - 1, 0)
-            if d + 1 < len(SPANS):
-                make_decay(0, *SPANS[d + 1])
-            for g in range(GROUPS):
-                for k in range(CHUNK // BLOCK):
-                    make_h(g, d, k)
+        gather_tab_words(1, *SPANS[2], placed([P, CHUNK], U32, "v_w_last", 4 * W2_BYTES + 64))
+
+        def make_span_h(g, d, given):
+            return [make_h(g, d, k, bank) for k, bank in enumerate(given)]
+
+        def quantize_span(d):
             quantize_h(d, 0, GROUPS, h_later[d - 1][:].rearrange("p g n t -> p (g n t)"))
-            finish(d - 1, 1)
-        for g in range(GROUPS):
-            finish(len(SPANS) - 1, g)
+
+        make_decay(1, *SPANS[1], pairs[1])
+        first_copies = make_span_h(0, 1, pairs[2])
+        first_copies[0](nc.scalar.copy)
+        finish(0, 0, 0, pairs[3] + pairs[0])
+        make_decay(0, *SPANS[2], pairs[1])
+        late_copies = make_span_h(1, 1, pairs[3])
+        first_copies[1](nc.vector.tensor_copy)
+        quantize_span(1)
+        finish(0, 1, 0, pairs[0] + pairs[2][:1])
+        make_h_on_gpsimd(2, pairs[1])
+        finish(0, 1, 3, pairs[2][1:], res=held[0])
+        make_decay(1, *SPANS[2], pairs[0])
+        finish(1, 0, 0, pairs[2])
+        late_copies += make_span_h(1, 2, pairs[1])
+        for copy_a in late_copies:
+            copy_a(nc.scalar.copy)
+        finish(1, 1, 0, pairs[0][:1])
+        quantize_span(2)
+        finish(1, 1, 2, pairs[0][1:], res=held[1])
+        finish(2, 0, 0, pairs[2])
+        finish(2, 1, 0, pairs[3])

@@ -62,7 +62,7 @@ def tile_list_mixed_layer_step_kernel(
         ]
         w4s_raw = kept([P, PASSES * H], U8, "w4s_raw")
         w8s_raw = kept([P, H], U8, "w8s_raw")
-        w8_raw = [kept([P, PASSES, K_PASS], U32, "w8_raw%d" % g) for g in range(GROUPS)]
+        w8_raw = [kept([P, PASSES, K_PASS], U32, "w8_raw0"), placed([P, PASSES, K_PASS], U32, "w8_raw1", 9 * W2_BYTES)]
         rate_sb = kept([P, GROUPS, PACK], F32, "rate_sb")
         step_sb = kept([P, GROUPS, PACK], F32, "step_sb")
         v_s1 = kept([P, S], U8, "v_s1")
@@ -144,6 +144,9 @@ def tile_list_mixed_layer_step_kernel(
         ]
         decay = [[kept([P, 2, HALF, 2], F32, "decay%d%d" % (g, c)) for c in range(2)] for g in range(GROUPS)]
         a_sb = [[kept([P, PACK, n], F32, "a_sb%d%d" % (g, d)) for d, (f, n) in enumerate(SPANS)] for g in range(GROUPS)]
+        a_sb[0][1] = placed([P, PACK, CHUNK], F32, "a_held", 9 * W2_BYTES)
+        last_squares = [placed([P, 2, CHUNK], F32, "last_square%d" % u, 10 * W2_BYTES + 8 * CHUNK * u) for u in range(2)]
+        a_sb[1][1] = placed([P, PACK, CHUNK], F32, "a_late", 10 * W2_BYTES)
         h_q = [kept([P, GROUPS * n], U32, "h_q%d" % d) for d, (f, n) in enumerate(SPANS)]
         h_s = [kept([P, GROUPS * n], U8, "h_s%d" % d) for d, (f, n) in enumerate(SPANS)]
         h_later = [
@@ -205,11 +208,11 @@ def tile_list_mixed_layer_step_kernel(
                 in_=w8_raw[g][:, s, :].rearrange("p (m c t) -> p m t c", t=PACK, c=4),
             )
 
-        def make_decay(g, first, count, given):
+        def make_decay(g, first, count, given, squares=None):
             c, n0 = divmod(first, HALF)
             per_bank = BANK // count
             for u in range(2):
-                square = ring.tile([P, 2, count], F32, name="square")
+                square = squares[u] if squares else ring.tile([P, 2, count], F32, name="square")
                 b = []
                 for e in range(2):
                     if e % per_bank == 0:
@@ -293,7 +296,7 @@ def tile_list_mixed_layer_step_kernel(
 
         out_rows = out.rearrange("(g p t) j -> g p t j", g=GROUPS, t=PACK)
 
-        def finish(d, g, t_first, given, res=None):
+        def finish(d, g, t_first, given, res=None, order=(0, 1)):
             first, count = SPANS[d]
             per_bank = BANK // count
             for t0, bank in zip(range(t_first, PACK, per_bank), given):
@@ -301,15 +304,15 @@ def tile_list_mixed_layer_step_kernel(
                 result = a_sb[g][d][:, t0 : t0 + per_bank, :] if res is None else res[:]
                 for i in range(per_bank):
                     col = P * (t0 + i)
-                    for s in range(PASSES):
+                    for s in order:
                         nc.tensor.matmul_mx(
                             out=y[:, i, :],
                             lhsT=w8_p[g][s][:, col : col + P].bitcast(FP8X4),
                             lhsT_scale=w8_s[g][4 * s : P, col : col + P],
                             rhs=h_q[d][:, count * s : count * (s + 1)].bitcast(FP8X4),
                             rhs_scale=h_s[d][:, count * s : count * (s + 1)],
-                            start=(s == 0),
-                            stop=(s == PASSES - 1),
+                            start=(s == order[0]),
+                            stop=(s == order[-1]),
                         )
                 for i in range(per_bank):
                     t = t0 + i
@@ -389,21 +392,23 @@ def tile_list_mixed_layer_step_kernel(
         make_decay(1, *SPANS[1], pairs[1])
         first_copies = make_span_h(0, 1, pairs[2])
         first_copies[0](nc.scalar.copy)
-        finish(0, 0, 0, pairs[3] + pairs[0])
+        finish(0, 0, 0, pairs[3])
+        finish(0, 0, 2, pairs[0], order=(1, 0))
         make_decay(0, *SPANS[2], pairs[1])
         late_copies = make_span_h(1, 1, pairs[3])
         first_copies[1](nc.vector.tensor_copy)
         quantize_span(1)
-        finish(0, 1, 0, pairs[0] + pairs[2][:1])
+        finish(0, 1, 0, pairs[0])
         make_h_on_gpsimd(2, pairs[1])
+        finish(0, 1, 2, pairs[2][:1])
+        make_decay(1, *SPANS[2], [pairs[0][0], pairs[1][0]], last_squares)
         finish(0, 1, 3, pairs[2][1:], res=held[0])
-        make_decay(1, *SPANS[2], pairs[0])
-        finish(1, 0, 0, pairs[2])
-        late_copies += make_span_h(1, 2, pairs[1])
+        finish(1, 0, 0, [pairs[0][1], pairs[2][0]])
+        late_copies += make_span_h(1, 2, [pairs[1][1], pairs[2][1]])
         for copy_a in late_copies:
             copy_a(nc.scalar.copy)
         finish(1, 1, 0, pairs[0][:1])
         quantize_span(2)
-        finish(1, 1, 2, pairs[0][1:], res=held[1])
-        finish(2, 0, 0, pairs[2])
+        finish(1, 1, 2, pairs[1][:1], res=held[1])
+        finish(2, 0, 0, [pairs[0][1], pairs[2][0]])
         finish(2, 1, 0, pairs[3])

@@ -110,13 +110,15 @@ def tile_list_mixed_layer_step_kernel(
         for r in range(QUADS):
             nc.sync.dma_start(out=v2_s[r:P:32, :].bitcast(I32), in_=v2_rows[8 * r : P : 32, :].bitcast(I32))
         load_w2(1, W2_COLS, K_PASS)
-        load_two_planes(tab_s, tab_scales)
+        for r in range(QUADS):
+            nc.sync.dma_start(out=tab_s[r:P:32, :].bitcast(I32), in_=tab_scales[0, r:16:4, :].bitcast(I32))
+        nc.sync.dma_start(out=tab_s[4:P:8, :].bitcast(I32), in_=tab_scales[1].bitcast(I32))
+        load_words(tab_w[0], tab_words[0].rearrange("p c i -> p (c i)"))
         for r in range(QUADS):
             nc.sync.dma_start(
                 out=w4s_raw[r:P:32, :].bitcast(I32).rearrange("z (s c) -> z s c", s=PASSES),
                 in_=w4_scales[:, r:16:4, :].bitcast(I32).rearrange("s z c -> z s c"),
             )
-        load_words(tab_w[0], tab_words[0].rearrange("p c i -> p (c i)"))
         load_w4(0)
         load_words(tab_w[1], tab_words[1].rearrange("p c i -> p (c i)"))
 
@@ -345,7 +347,7 @@ def tile_list_mixed_layer_step_kernel(
         make_decay(1, 0, HALF, pairs[2] + pairs[3])
 
         for r in range(QUADS):
-            nc.sync.dma_start(out=v_s1[r:P:32, :].bitcast(I32), in_=v_s0[4 + r : P : 32, :].bitcast(I32))
+            nc.sync.dma_start(out=v_s1[r:P:32, :].bitcast(I32), in_=v_s0[8 * r + 4 : P : 32, :].bitcast(I32))
         load_w4(1)
         load_two_planes(w8s_raw, w8_scales)
         for g in range(GROUPS):
@@ -358,14 +360,15 @@ def tile_list_mixed_layer_step_kernel(
         for s in range(PASSES):
             deal(w4_s[0][s], w4s_raw[:, H * s : H * s + K_PASS])
         for g in range(GROUPS):
+            if g == 1:
+                nc.gpsimd.tensor_copy(
+                    out=w4_s_late[:].rearrange("p s (t m) -> p s t m", t=PACK),
+                    in_=w4s_raw[:].rearrange("p (s g m t) -> p s g t m", s=PASSES, g=GROUPS, t=PACK)[:, :, 1],
+                )
             for s in range(PASSES) if g == 0 else reversed(range(PASSES)):
                 deal(w4_p[g][s][:], w4_raw[g][:, K_PASS * s : K_PASS * (s + 1)])
         gather_tab_words(0, 0, HALF)
         gather_tab_words(0, HALF, HALF)
-        nc.vector.tensor_copy(
-            out=w4_s_late[:].rearrange("p s (t m) -> p s t m", t=PACK),
-            in_=w4s_raw[:].rearrange("p (s g m t) -> p s g t m", s=PASSES, g=GROUPS, t=PACK)[:, :, 1],
-        )
         gather_tab_words(1, 0, HALF)
         gather_tab_words(1, *SPANS[1])
         nc.gpsimd.tensor_copy(

@@ -130,16 +130,12 @@ def tile_list_mixed_layer_step_kernel(
         w2_bf = [kept([P, PACK, P, PACK], BF16, "w2_bf0"), placed([P, PACK, P, PACK], BF16, "w2_bf1", 0)]
         w2_q = [kept([P, K_PASS], U32, "w2_q%d" % g) for g in range(GROUPS)]
         w2_s = [kept([P, K_PASS], U8, "w2_s%d" % g) for g in range(GROUPS)]
-        w4_s_late = placed([P, PASSES, K_PASS], U8, "w4_s1", 6 * W2_BYTES)
-        w4_s = [
-            [placed([P, K_PASS], U8, "w4_s0%d" % s, K_PASS * s)[:] for s in range(PASSES)],
-            [w4_s_late[:, s, :] for s in range(PASSES)],
-        ]
+        w4_s_both = [placed([P, PASSES, K_PASS], U8, "w4_s%d" % g, 6 * g * W2_BYTES) for g in range(GROUPS)]
+        w4_s = [[w4_s_both[g][:, s, :] for s in range(PASSES)] for g in range(GROUPS)]
         w4_p = [[kept([P, K_PASS], U16, "w4_p%d%d" % (g, s)) for s in range(PASSES)] for g in range(GROUPS)]
-        w8_s_both = kept([P, GROUPS, K_PASS], U8, "w8_s")
-        w8_s = [w8_s_both[:, g, :] for g in range(GROUPS)]
+        w8_s = [kept([P, K_PASS], U8, "w8_s0"), placed([P, K_PASS], U8, "w8_s1", 4 * W2_BYTES + 64 + 4 * CHUNK)]
         h_first = [placed([P, HALF, PACK], BF16, "h_first%d" % g, (2 + 2 * g) * W2_BYTES) for g in range(GROUPS)]
-        w8_late = placed([P, PASSES, K_PASS], U32, "w8_p1", 4 * W2_BYTES + 64 + 4 * CHUNK)
+        w8_late = placed([P, PASSES, K_PASS], U32, "w8_p1", 4 * W2_BYTES + 64 + 4 * CHUNK + K_PASS)
         w8_p = [
             [kept([P, K_PASS], U32, "w8_p00")[:], placed([P, K_PASS], U32, "w8_p01", 2 * W2_BYTES)[:]],
             [w8_late[:, s, :] for s in range(PASSES)],
@@ -155,7 +151,7 @@ def tile_list_mixed_layer_step_kernel(
             placed([P, GROUPS, CHUNK, PACK], BF16, "h_bf1", 7 * W2_BYTES),
             placed([P, GROUPS, CHUNK, PACK], BF16, "h_bf2", 15 * W2_BYTES // 2),
         ]
-        held = [placed([P, 1, HALF], F32, "held0", 7 * W2_BYTES), placed([P, 2, CHUNK], F32, "held1", 8 * W2_BYTES)]
+        held = placed([P, 1, HALF], F32, "held", 7 * W2_BYTES)
         a_pairs = kept([P, 2, CHUNK, 2], F32, "a_pairs")
         h_bf = [[h[:] for h in h_first]] + [[h[:, g] for g in range(GROUPS)] for h in h_later]
         v_w = {}
@@ -357,24 +353,18 @@ def tile_list_mixed_layer_step_kernel(
             )
         nc.sync.dma_start(out=step_sb[:], in_=step.rearrange("(g p t) -> p g t", g=GROUPS, t=PACK))
 
-        for s in range(PASSES):
-            deal(w4_s[0][s], w4s_raw[:, H * s : H * s + K_PASS])
         for g in range(GROUPS):
-            if g == 1:
-                nc.gpsimd.tensor_copy(
-                    out=w4_s_late[:].rearrange("p s (t m) -> p s t m", t=PACK),
-                    in_=w4s_raw[:].rearrange("p (s g m t) -> p s g t m", s=PASSES, g=GROUPS, t=PACK)[:, :, 1],
-                )
+            nc.gpsimd.tensor_copy(
+                out=w4_s_both[g][:].rearrange("p s (t m) -> p s t m", t=PACK),
+                in_=w4s_raw[:].rearrange("p (s g m t) -> p s g t m", s=PASSES, g=GROUPS, t=PACK)[:, :, g],
+            )
             for s in range(PASSES) if g == 0 else reversed(range(PASSES)):
                 deal(w4_p[g][s][:], w4_raw[g][:, K_PASS * s : K_PASS * (s + 1)])
         gather_tab_words(0, 0, HALF)
         gather_tab_words(0, HALF, HALF)
         gather_tab_words(1, 0, HALF)
         gather_tab_words(1, *SPANS[1])
-        nc.gpsimd.tensor_copy(
-            out=w8_s_both[:].rearrange("p g (t m) -> p g t m", t=PACK),
-            in_=w8s_raw[:].rearrange("p (g m t) -> p g t m", g=GROUPS, t=PACK),
-        )
+        deal(w8_s[0][:], w8s_raw[:, 0:K_PASS])
         deal_w8(0, 0)
 
         make_decay(0, *SPANS[1], pairs[0])
@@ -382,6 +372,8 @@ def tile_list_mixed_layer_step_kernel(
             for k, bank in enumerate(pairs[1] + pairs[2] if g == 0 else pairs[3] + pairs[0]):
                 make_h(g, 0, k, bank)(nc.scalar.copy)
             quantize_h(0, g, g + 1, h_bf[0][g].rearrange("p n t -> p (n t)"))
+            if g == 1:
+                deal(w8_s[1][:], w8s_raw[:, K_PASS:H])
             for s in range(1 - g, PASSES):
                 deal_w8(g, s)
         gather_tab_words(1, *SPANS[2], placed([P, CHUNK], U32, "v_w_last", 4 * W2_BYTES + 64))
@@ -405,13 +397,13 @@ def tile_list_mixed_layer_step_kernel(
         make_h_on_gpsimd(2, pairs[1])
         finish(0, 1, 2, pairs[2][:1])
         make_decay(1, *SPANS[2], [pairs[0][0], pairs[1][0]], last_squares)
-        finish(0, 1, 3, pairs[2][1:], res=held[0])
+        finish(0, 1, 3, pairs[2][1:], res=held)
         finish(1, 0, 0, [pairs[0][1], pairs[2][0]])
         late_copies += make_span_h(1, 2, [pairs[1][1], pairs[2][1]])
         for copy_a in late_copies:
             copy_a(nc.scalar.copy)
-        finish(1, 1, 0, pairs[0][:1])
-        quantize_span(2)
-        finish(1, 1, 2, pairs[1][:1], res=held[1])
+        for g in range(GROUPS):
+            quantize_h(2, g, g + 1, h_bf[2][g].rearrange("p n t -> p (n t)"))
+        finish(1, 1, 0, [pairs[0][0], pairs[1][0]])
         finish(2, 0, 0, [pairs[0][1], pairs[2][0]])
         finish(2, 1, 0, pairs[3])

@@ -133,9 +133,10 @@ def tile_list_mixed_layer_step_kernel(
         w4_s_both = [placed([P, PASSES, K_PASS], U8, "w4_s%d" % g, 6 * g * W2_BYTES) for g in range(GROUPS)]
         w4_s = [[w4_s_both[g][:, s, :] for s in range(PASSES)] for g in range(GROUPS)]
         w4_p = [[kept([P, K_PASS], U16, "w4_p%d%d" % (g, s)) for s in range(PASSES)] for g in range(GROUPS)]
-        w8_s = [kept([P, K_PASS], U8, "w8_s0"), placed([P, K_PASS], U8, "w8_s1", 4 * W2_BYTES + 64 + 4 * CHUNK)]
+        w8_s_both = kept([P, GROUPS, K_PASS], U8, "w8_s")
+        w8_s = [w8_s_both[:, g, :] for g in range(GROUPS)]
         h_first = [placed([P, HALF, PACK], BF16, "h_first%d" % g, (2 + 2 * g) * W2_BYTES) for g in range(GROUPS)]
-        w8_late = placed([P, PASSES, K_PASS], U32, "w8_p1", 4 * W2_BYTES + 64 + 4 * CHUNK + K_PASS)
+        w8_late = placed([P, PASSES, K_PASS], U32, "w8_p1", 4 * W2_BYTES + 64 + 4 * CHUNK)
         w8_p = [
             [kept([P, K_PASS], U32, "w8_p00")[:], placed([P, K_PASS], U32, "w8_p01", 2 * W2_BYTES)[:]],
             [w8_late[:, s, :] for s in range(PASSES)],
@@ -364,7 +365,10 @@ def tile_list_mixed_layer_step_kernel(
         gather_tab_words(0, HALF, HALF)
         gather_tab_words(1, 0, HALF)
         gather_tab_words(1, *SPANS[1])
-        deal(w8_s[0][:], w8s_raw[:, 0:K_PASS])
+        nc.gpsimd.tensor_copy(
+            out=w8_s_both[:].rearrange("p g (t m) -> p g t m", t=PACK),
+            in_=w8s_raw[:].rearrange("p (g m t) -> p g t m", g=GROUPS, t=PACK),
+        )
         deal_w8(0, 0)
 
         make_decay(0, *SPANS[1], pairs[0])
@@ -372,8 +376,6 @@ def tile_list_mixed_layer_step_kernel(
             for k, bank in enumerate(pairs[1] + pairs[2] if g == 0 else pairs[3] + pairs[0]):
                 make_h(g, 0, k, bank)(nc.scalar.copy)
             quantize_h(0, g, g + 1, h_bf[0][g].rearrange("p n t -> p (n t)"))
-            if g == 1:
-                deal(w8_s[1][:], w8s_raw[:, K_PASS:H])
             for s in range(1 - g, PASSES):
                 deal_w8(g, s)
         gather_tab_words(1, *SPANS[2], placed([P, CHUNK], U32, "v_w_last", 4 * W2_BYTES + 64))

@@ -323,7 +323,8 @@ def tile_list_mixed_layer_step_kernel(
                 last = first + count == S and g == GROUPS - 1 and t0 + per_bank == PACK
                 rows = 1 if last else per_bank
                 for i in range(0, per_bank, rows):
-                    nc.sync.dma_start(
+                    second = first + count == S and (t0 // per_bank + i) % 2 == 1
+                    (nc.scalar if second else nc.sync).dma_start(
                         out=out_rows[g][:, t0 + i : t0 + i + rows, first : first + count], in_=result[:, i : i + rows, :]
                     )
 

@@ -28,6 +28,7 @@ HALF = S // 2
 CHUNK = 256
 BLOCK = BANK // PACK
 W2_COLS = 256
+ALIGN = 256
 W2_BYTES = 2 * PACK * K_PASS
 SPANS = ((0, HALF), (HALF, CHUNK), (HALF + CHUNK, CHUNK))
 
@@ -44,10 +45,10 @@ def tile_list_mixed_layer_step_kernel(
         psum = ctx.enter_context(tc.psum_pool(name="psum", bufs=1))
 
         def kept(shape, dtype, name):
-            return keep.tile(shape, dtype, name=name, align_bytes=64)
+            return keep.tile(shape, dtype, name=name, align_bytes=ALIGN)
 
         def placed(shape, dtype, name, offset):
-            return twice.tile(shape, dtype, name=name, align_bytes=64, offset=offset)
+            return twice.tile(shape, dtype, name=name, align_bytes=ALIGN, offset=offset)
 
         list1 = kept([P, S // 16], U16, "list1")
         list2 = kept([P, S // 16], U16, "list2")
@@ -136,7 +137,7 @@ def tile_list_mixed_layer_step_kernel(
         w8_s_both = kept([P, GROUPS, K_PASS], U8, "w8_s")
         w8_s = [w8_s_both[:, g, :] for g in range(GROUPS)]
         h_first = [placed([P, HALF, PACK], BF16, "h_first%d" % g, (2 + 2 * g) * W2_BYTES) for g in range(GROUPS)]
-        w8_late = placed([P, PASSES, K_PASS], U32, "w8_p1", 4 * W2_BYTES + 64 + 4 * CHUNK)
+        w8_late = placed([P, PASSES, K_PASS], U32, "w8_p1", 4 * W2_BYTES + 4 * CHUNK)
         w8_p = [
             [kept([P, K_PASS], U32, "w8_p00")[:], placed([P, K_PASS], U32, "w8_p01", 2 * W2_BYTES)[:]],
             [w8_late[:, s, :] for s in range(PASSES)],
@@ -379,7 +380,7 @@ def tile_list_mixed_layer_step_kernel(
             quantize_h(0, g, g + 1, h_bf[0][g].rearrange("p n t -> p (n t)"))
             for s in range(1 - g, PASSES):
                 deal_w8(g, s)
-        gather_tab_words(1, *SPANS[2], placed([P, CHUNK], U32, "v_w_last", 4 * W2_BYTES + 64))
+        gather_tab_words(1, *SPANS[2], placed([P, CHUNK], U32, "v_w_last", 4 * W2_BYTES))
 
         def make_span_h(g, d, given):
             return [make_h(g, d, k, bank) for k, bank in enumerate(given)]

from contextlib import ExitStack

import concourse.mybir as mybir

K, K2, T, S, H = 1024, 512, 2048, 1024, 1024
FLOPS = 2 * S * H * (K + K2 + H)

F32 = mybir.dt.float32
BF16 = mybir.dt.bfloat16
I32 = mybir.dt.int32
U32 = mybir.dt.uint32
U16 = mybir.dt.uint16
U8 = mybir.dt.uint8
FP8X4 = mybir.dt.float8_e4m3fn_x4
FP4X4 = mybir.dt.float4_e2m1fn_x4
ALU = mybir.AluOpType
ACT = mybir.ActivationFunctionType

P = 128
PACK = 4
K_PASS = P * PACK
PASSES = K // K_PASS
GROUPS = H // K_PASS
QUADS = 4
BANK = 512
BANKS = 8
HALF = S // 2
CHUNK = 256
BLOCK = BANK // PACK
W2_COLS = 256
ALIGN = 256
W2_BYTES = 2 * PACK * K_PASS
SPANS = ((0, HALF), (HALF, CHUNK), (HALF + CHUNK, CHUNK))


def tile_list_mixed_layer_step_kernel(
    tc, tab_words, tab_scales, offs, tab2_words, tab2_scales, offs2,
    w4_words, w4_scales, w2, rate, w8_words, w8_scales, step, out,
):
    nc = tc.nc
    with ExitStack() as ctx:
        keep = ctx.enter_context(tc.tile_pool(name="keep", bufs=1))
        twice = ctx.enter_context(tc.tile_pool(name="twice", bufs=1))
        ring = ctx.enter_context(tc.tile_pool(name="ring", bufs=3))
        psum = ctx.enter_context(tc.psum_pool(name="psum", bufs=1))

        def kept(shape, dtype, name):
            return keep.tile(shape, dtype, name=name, align_bytes=ALIGN)

        def placed(shape, dtype, name, offset):
            return twice.tile(shape, dtype, name=name, align_bytes=ALIGN, offset=offset)

        list1 = kept([P, S // 16], U16, "list1")
        list2 = kept([P, S // 16], U16, "list2")
        tab2_w = kept([P, T], U16, "tab2_w")
        tab2_s = kept([P, T], U8, "tab2_s")
        tab_w = [kept([P, T], U32, "tab_w%d" % s) for s in range(PASSES)]
        tab_s = kept([P, T], U8, "tab_s")
        w2_raw = [kept([P, PACK, K_PASS], F32, "w2_raw%d" % g) for g in range(GROUPS)]
        w4_raw = [
            placed([P, PASSES * K_PASS], U16, "w4_raw0", 6 * W2_BYTES),
            kept([P, PASSES * K_PASS], U16, "w4_raw1"),
        ]
        w4s_raw = kept([P, PASSES * H], U8, "w4s_raw")
        w8s_raw = kept([P, H], U8, "w8s_raw")
        w8_raw = [kept([P, PASSES, K_PASS], U32, "w8_raw0"), placed([P, PASSES, K_PASS], U32, "w8_raw1", 9 * W2_BYTES)]
        rate_sb = kept([P, GROUPS, PACK], F32, "rate_sb")
        step_sb = kept([P, GROUPS, PACK], F32, "step_sb")
        v_s1 = kept([P, S], U8, "v_s1")
        v2_s = kept([P, S], U8, "v2_s")

        nc.gpsimd.memset(tab2_s[:].bitcast(I32), 0)
        for plane in (v2_s, tab_s, w4s_raw, w8s_raw, v_s1):
            nc.vector.memset(plane[:].bitcast(I32), 0)

        def load_words(tile, src):
            nc.sync.dma_start(out=tile[:].bitcast(I32), in_=src.bitcast(I32))

        def load_w2(g, c0, c1):
            nc.sync.dma_start(
                out=w2_raw[g][:, :, c0:c1],
                in_=w2.rearrange("(p i) c -> p i c", i=PACK)[:, :, K_PASS * g + c0 : K_PASS * g + c1],
            )

        def load_w4(g):
            half = K_PASS // 2
            nc.sync.dma_start(
                out=w4_raw[g][:].bitcast(I32).rearrange("p (s c) -> p s c", s=PASSES),
                in_=w4_words.bitcast(I32).rearrange("s p c -> p s c")[:, :, half * g : half * (g + 1)],
            )

        def load_two_planes(tile, src):
            for z in range(QUADS):
                nc.sync.dma_start(
                    out=tile[32 * z : 32 * z + 8, :].bitcast(I32), in_=src[:, 4 * z : 4 * z + 4, :].bitcast(I32)
                )

        nc.sync.dma_start(out=rate_sb[:], in_=rate.rearrange("(g p t) -> p g t", g=GROUPS, t=PACK))
        nc.sync.dma_start(list2[:], offs2)
        nc.sync.dma_start(list1[:], offs)
        nc.sync.dma_start(out=tab2_s[0:P:8, :].bitcast(I32), in_=tab2_scales[0].bitcast(I32))
        load_w2(0, 0, K_PASS)
        load_words(tab2_w, tab2_words[0])
        load_w2(1, 0, W2_COLS)

        def gather(dst, window, offsets, first, count):
            nc.vector.tensor_copy(dst[:], window[:].indirect(offsets[:, first // 16 : (first + count) // 16]))

        v2_rows = kept([P, S], U8, "v2_rows")
        gather(v2_rows, tab2_s, list2, 0, S)
        for r in range(QUADS):
            nc.sync.dma_start(out=v2_s[r:P:32, :].bitcast(I32), in_=v2_rows[8 * r : P : 32, :].bitcast(I32))
        load_w2(1, W2_COLS, K_PASS)
        for r in range(QUADS):
            nc.sync.dma_start(out=tab_s[r:P:32, :].bitcast(I32), in_=tab_scales[0, r:16:4, :].bitcast(I32))
        nc.sync.dma_start(out=tab_s[4:P:8, :].bitcast(I32), in_=tab_scales[1].bitcast(I32))
        load_words(tab_w[0], tab_words[0].rearrange("p c i -> p (c i)"))
        for r in range(QUADS):
            nc.sync.dma_start(
                out=w4s_raw[r:P:32, :].bitcast(I32).rearrange("z (s c) -> z s c", s=PASSES),
                in_=w4_scales[:, r:16:4, :].bitcast(I32).rearrange("s z c -> z s c"),
            )
        load_w4(0)
        load_words(tab_w[1], tab_words[1].rearrange("p c i -> p (c i)"))

        log_rate = kept([P, GROUPS * PACK], F32, "log_rate")
        root = kept([P, GROUPS * PACK], F32, "root")
        nc.scalar.activation(log_rate[:], rate_sb[:].rearrange("p g t -> p (g t)"), ACT.Ln, scale=-1.0)
        nc.scalar.activation(root[:], log_rate[:], ACT.Exp, scale=0.5)

        w2_bf = [kept([P, PACK, P, PACK], BF16, "w2_bf0"), placed([P, PACK, P, PACK], BF16, "w2_bf1", 0)]
        w2_q = [kept([P, K_PASS], U32, "w2_q%d" % g) for g in range(GROUPS)]
        w2_s = [kept([P, K_PASS], U8, "w2_s%d" % g) for g in range(GROUPS)]
        w4_s_both = [placed([P, PASSES, K_PASS], U8, "w4_s%d" % g, 6 * g * W2_BYTES) for g in range(GROUPS)]
        w4_s = [[w4_s_both[g][:, s, :] for s in range(PASSES)] for g in range(GROUPS)]
        w4_p = [[kept([P, K_PASS], U16, "w4_p%d%d" % (g, s)) for s in range(PASSES)] for g in range(GROUPS)]
        w8_s_both = kept([P, GROUPS, K_PASS], U8, "w8_s")
        w8_s = [w8_s_both[:, g, :] for g in range(GROUPS)]
        h_first = [placed([P, HALF, PACK], BF16, "h_first%d" % g, (2 + 2 * g) * W2_BYTES) for g in range(GROUPS)]
        w8_late = placed([P, PASSES, K_PASS], U32, "w8_p1", 4 * W2_BYTES + 4 * CHUNK)
        w8_p = [
            [kept([P, K_PASS], U32, "w8_p00")[:], placed([P, K_PASS], U32, "w8_p01", 2 * W2_BYTES)[:]],
            [w8_late[:, s, :] for s in range(PASSES)],
        ]
        decay = [[kept([P, 2, HALF, 2], F32, "decay%d%d" % (g, c)) for c in range(2)] for g in range(GROUPS)]
        a_sb = [[kept([P, PACK, n], F32, "a_sb%d%d" % (g, d)) for d, (f, n) in enumerate(SPANS)] for g in range(GROUPS)]
        a_sb[0][1] = placed([P, PACK, CHUNK], F32, "a_held", 9 * W2_BYTES)
        last_squares = [placed([P, 2, CHUNK], F32, "last_square%d" % u, 10 * W2_BYTES + 8 * CHUNK * u) for u in range(2)]
        a_sb[1][1] = placed([P, PACK, CHUNK], F32, "a_late", 10 * W2_BYTES)
        h_q = [kept([P, GROUPS * n], U32, "h_q%d" % d) for d, (f, n) in enumerate(SPANS)]
        h_s = [kept([P, GROUPS * n], U8, "h_s%d" % d) for d, (f, n) in enumerate(SPANS)]
        h_later = [
            placed([P, GROUPS, CHUNK, PACK], BF16, "h_bf1", 7 * W2_BYTES),
            placed([P, GROUPS, CHUNK, PACK], BF16, "h_bf2", 15 * W2_BYTES // 2),
        ]
        held = placed([P, 1, HALF], F32, "held", 7 * W2_BYTES)
        a_pairs = kept([P, 2, CHUNK, 2], F32, "a_pairs")
        h_bf = [[h[:] for h in h_first]] + [[h[:, g] for g in range(GROUPS)] for h in h_later]
        v_w = {}
        v_wide = {}
        v2_w = {}
        banks = [psum.tile([P, BANK], F32, name="bank%d" % i) for i in range(BANKS)]
        pairs = [banks[2 * i : 2 * i + 2] for i in range(BANKS // 2)]

        def gather_tab_words(s, first, count, words=None):
            if words is None:
                words = kept([P, count], U32, "v_w%d_%d" % (s, first))
            gather(words, tab_w[s], list1, first, count)
            for m0 in range(0, count, BLOCK):
                v_w[s, first + m0] = words[:, m0 : m0 + BLOCK]
            for m0 in range(0, count, CHUNK):
                v_wide[s, first + m0] = words[:, m0 : m0 + CHUNK]

        m_cols = W2_COLS // PACK

        def w2_piece(g, q):
            return w2_bf[g][:, :, m_cols * q : m_cols * (q + 1), :], w2_raw[g][:, :, W2_COLS * q : W2_COLS * (q + 1)]

        def round_w2_on_scalar(g, q):
            dst, src = w2_piece(g, q)
            for u in range(2):
                nc.scalar.activation(
                    dst[:, 2 * u : 2 * u + 2].rearrange("p e m i -> p m e i"),
                    src.rearrange("p i (m t) -> p m t i", t=PACK)[:, :, 2 * u : 2 * u + 2, :],
                    ACT.Copy,
                )

        def round_w2_on_vector(g, q):
            dst, src = w2_piece(g, q)
            nc.vector.tensor_copy(
                out=dst.rearrange("p (u e) m i -> p u m e i", u=2),
                in_=src.rearrange("p i (m u e) -> p u m e i", u=2, e=2),
            )

        def quantize_w2(g):
            nc.vector.quantize_mx(
                out=w2_q[g][:].bitcast(FP8X4), scales=w2_s[g][:], in_=w2_bf[g][:].rearrange("p t m i -> p (t m i)")
            )

        def deal(dst, src):
            nc.gpsimd.tensor_copy(
                out=dst.rearrange("p (t m) -> p t m", t=PACK), in_=src.rearrange("p (m t) -> p t m", t=PACK)
            )

        def deal_w8(g, s):
            nc.gpsimd.tensor_copy(
                out=w8_p[g][s].rearrange("p (t m c) -> p m t c", t=PACK, c=4),
                in_=w8_raw[g][:, s, :].rearrange("p (m c t) -> p m t c", t=PACK, c=4),
            )

        def make_decay(g, first, count, given, squares=None):
            c, n0 = divmod(first, HALF)
            per_bank = BANK // count
            for u in range(2):
                square = squares[u] if squares else ring.tile([P, 2, count], F32, name="square")
                b = []
                for e in range(2):
                    if e % per_bank == 0:
                        bank = given[(2 * u + e) // per_bank]
                    b.append(bank[:, count * (e % per_bank) : count * (e % per_bank + 1)])
                    nc.tensor.matmul_mx(
                        out=b[e],
                        lhsT=w2_q[g][:, P * (2 * u + e) : P * (2 * u + e + 1)].bitcast(FP8X4),
                        lhsT_scale=w2_s[g][:, P * (2 * u + e) : P * (2 * u + e + 1)],
                        rhs=v2_w[c][:, n0 : n0 + count].bitcast(FP4X4),
                        rhs_scale=v2_s[:, first : first + count],
                        start=True,
                        stop=True,
                    )
                for e in range(2):
                    t = 2 * u + e
                    nc.scalar.activation(
                        square[:, e, :], b[e], ACT.Square, scale=root[:, PACK * g + t : PACK * g + t + 1]
                    )
                nc.scalar.activation(
                    decay[g][c][:, u, n0 : n0 + count, :], square[:].rearrange("p e n -> p n e"), ACT.Exp, scale=-1.0
                )

        def make_h(g, d, k, bank):
            first, count = SPANS[d]
            m0 = BLOCK * k
            c, n0 = divmod(first + m0, HALF)
            acc = bank[:].rearrange("p (t n) -> p t n", t=PACK)
            for s in range(PASSES):
                for t in range(PACK):
                    nc.tensor.matmul_mx(
                        out=acc[:, t, :],
                        lhsT=w4_p[g][s][:, P * t : P * (t + 1)].bitcast(FP4X4),
                        lhsT_scale=w4_s[g][s][:, P * t : P * (t + 1)],
                        rhs=v_w[s, first + m0].bitcast(FP8X4),
                        rhs_scale=v_s[s][:, first + m0 : first + m0 + BLOCK],
                        start=(s == 0 and t == 0),
                        stop=(s == PASSES - 1 and t == PACK - 1),
                    )
            nc.vector.tensor_tensor(
                h_bf[d][g][:, m0 : m0 + BLOCK, :].rearrange("p n (u e) -> p n u e", u=2),
                acc.rearrange("p (u e) n -> p n u e", u=2),
                decay[g][c][:, :, n0 : n0 + BLOCK, :].rearrange("p u n e -> p n u e"),
                ALU.mult,
            )

            def copy_a(copy):
                copy(out=a_sb[g][d][:, :, m0 : m0 + BLOCK], in_=acc)

            return copy_a

        def make_h_on_gpsimd(d, given):
            first, count = SPANS[d]
            c, n0 = divmod(first, HALF)
            for u, bank in enumerate(given):
                acc = bank[:].rearrange("p (e n) -> p e n", e=2)
                for s in range(PASSES):
                    for e in range(2):
                        t = 2 * u + e
                        nc.tensor.matmul_mx(
                            out=acc[:, e, :],
                            lhsT=w4_p[0][s][:, P * t : P * (t + 1)].bitcast(FP4X4),
                            lhsT_scale=w4_s[0][s][:, P * t : P * (t + 1)],
                            rhs=v_wide[s, first].bitcast(FP8X4),
                            rhs_scale=v_s[s][:, first : first + count],
                            start=(s == 0 and e == 0),
                            stop=(s == PASSES - 1 and e == 1),
                        )
                nc.scalar.copy(out=a_pairs[:, u], in_=acc.rearrange("p e n -> p n e"))
                nc.gpsimd.tensor_tensor(
                    h_bf[d][0][:, :, 2 * u : 2 * u + 2], a_pairs[:, u], decay[0][c][:, u, n0 : n0 + count, :], ALU.mult
                )

        def quantize_h(d, g0, g1, values):
            count = SPANS[d][1]
            nc.vector.quantize_mx(
                out=h_q[d][:, count * g0 : count * g1].bitcast(FP8X4),
                scales=h_s[d][:, count * g0 : count * g1],
                in_=values,
            )

        out_rows = out.rearrange("(g p t) j -> g p t j", g=GROUPS, t=PACK)

        def finish(d, g, t_first, given, res=None, order=(0, 1)):
            first, count = SPANS[d]
            per_bank = BANK // count
            for t0, bank in zip(range(t_first, PACK, per_bank), given):
                y = bank[:].rearrange("p (i n) -> p i n", i=per_bank)
                result = a_sb[g][d][:, t0 : t0 + per_bank, :] if res is None else res[:]
                for i in range(per_bank):
                    col = P * (t0 + i)
                    for s in order:
                        nc.tensor.matmul_mx(
                            out=y[:, i, :],
                            lhsT=w8_p[g][s][:, col : col + P].bitcast(FP8X4),
                            lhsT_scale=w8_s[g][4 * s : P, col : col + P],
                            rhs=h_q[d][:, count * s : count * (s + 1)].bitcast(FP8X4),
                            rhs_scale=h_s[d][:, count * s : count * (s + 1)],
                            start=(s == order[0]),
                            stop=(s == order[-1]),
                        )
                for i in range(per_bank):
                    t = t0 + i
                    a = a_pairs[:, t // 2, :, t % 2] if (g, d) == (0, 2) else a_sb[g][d][:, t, :]
                    nc.vector.scalar_tensor_tensor(
                        result[:, i, :], a, step_sb[:, g, t : t + 1], y[:, i, :],
                        ALU.mult, ALU.add,
                    )
                last = first + count == S and g == GROUPS - 1 and t0 + per_bank == PACK
                rows = 1 if last else per_bank
                for i in range(0, per_bank, rows):
                    second = first + count == S and (t0 // per_bank + i) % 2 == 1
                    (nc.scalar if second else nc.sync).dma_start(
                        out=out_rows[g][:, t0 + i : t0 + i + rows, first : first + count], in_=result[:, i : i + rows, :]
                    )

        v2_w[0] = kept([P, HALF], U16, "v2_w0")
        round_w2_on_scalar(0, 0)
        round_w2_on_vector(0, 1)
        gather(v2_w[0], tab2_w, list2, 0, HALF)
        quantize_w2(0)
        round_w2_on_scalar(1, 0)
        make_decay(0, 0, HALF, pairs[0] + pairs[1])
        v2_w[1] = kept([P, HALF], U16, "v2_w1")
        gather(v2_w[1], tab2_w, list2, HALF, HALF)
        v_s0 = kept([P, S], U8, "v_s0")
        v_s = [v_s0, v_s1]
        round_w2_on_vector(1, 1)
        quantize_w2(1)
        gather(v_s0, tab_s, list1, 0, S)
        make_decay(1, 0, HALF, pairs[2] + pairs[3])

        for r in range(QUADS):
            nc.sync.dma_start(out=v_s1[r:P:32, :].bitcast(I32), in_=v_s0[8 * r + 4 : P : 32, :].bitcast(I32))
        load_w4(1)
        load_two_planes(w8s_raw, w8_scales)
        for g in range(GROUPS):
            nc.sync.dma_start(
                out=w8_raw[g][:].bitcast(I32),
                in_=w8_words.rearrange("s p c i -> p s (c i)").bitcast(I32)[:, :, K_PASS * g : K_PASS * (g + 1)],
            )
        nc.sync.dma_start(out=step_sb[:], in_=step.rearrange("(g p t) -> p g t", g=GROUPS, t=PACK))

        for g in range(GROUPS):
            nc.gpsimd.tensor_copy(
                out=w4_s_both[g][:].rearrange("p s (t m) -> p s t m", t=PACK),
                in_=w4s_raw[:].rearrange("p (s g m t) -> p s g t m", s=PASSES, g=GROUPS, t=PACK)[:, :, g],
            )
            for s in range(PASSES) if g == 0 else reversed(range(PASSES)):
                deal(w4_p[g][s][:], w4_raw[g][:, K_PASS * s : K_PASS * (s + 1)])
        gather_tab_words(0, 0, HALF)
        gather_tab_words(0, HALF, HALF)
        gather_tab_words(1, 0, HALF)
        gather_tab_words(1, *SPANS[1])
        nc.gpsimd.tensor_copy(
            out=w8_s_both[:].rearrange("p g (t m) -> p g t m", t=PACK),
            in_=w8s_raw[:].rearrange("p (g m t) -> p g t m", g=GROUPS, t=PACK),
        )
        deal_w8(0, 0)

        make_decay(0, *SPANS[1], pairs[0])
        for g in range(GROUPS):
            for k, bank in enumerate(pairs[1] + pairs[2] if g == 0 else pairs[3] + pairs[0]):
                make_h(g, 0, k, bank)(nc.scalar.copy)
            quantize_h(0, g, g + 1, h_bf[0][g].rearrange("p n t -> p (n t)"))
            for s in range(1 - g, PASSES):
                deal_w8(g, s)
        gather_tab_words(1, *SPANS[2], placed([P, CHUNK], U32, "v_w_last", 4 * W2_BYTES))

        def make_span_h(g, d, given):
            return [make_h(g, d, k, bank) for k, bank in enumerate(given)]

        def quantize_span(d):
            quantize_h(d, 0, GROUPS, h_later[d - 1][:].rearrange("p g n t -> p (g n t)"))

        make_decay(1, *SPANS[1], pairs[1])
        first_copies = make_span_h(0, 1, pairs[2])
        first_copies[0](nc.scalar.copy)
        finish(0, 0, 0, pairs[3])
        finish(0, 0, 2, pairs[0], order=(1, 0))
        make_decay(0, *SPANS[2], pairs[1])
        late_copies = make_span_h(1, 1, pairs[3])
        first_copies[1](nc.vector.tensor_copy)
        quantize_span(1)
        finish(0, 1, 0, pairs[0])
        make_h_on_gpsimd(2, pairs[1])
        finish(0, 1, 2, pairs[2][:1])
        make_decay(1, *SPANS[2], [pairs[0][0], pairs[1][0]], last_squares)
        finish(0, 1, 3, pairs[2][1:], res=held)
        finish(1, 0, 0, [pairs[0][1], pairs[2][0]])
        late_copies += make_span_h(1, 2, [pairs[1][1], pairs[2][1]])
        for copy_a in late_copies:
            copy_a(nc.scalar.copy)
        for g in range(GROUPS):
            quantize_h(2, g, g + 1, h_bf[2][g].rearrange("p n t -> p (n t)"))
        finish(1, 1, 0, [pairs[0][0], pairs[1][0]])
        finish(2, 0, 0, [pairs[0][1], pairs[2][0]])
        finish(2, 1, 0, pairs[3])
